import numpy as np
import ml_dtypes


def mxq(x, axis, fmt="e4m3"):
    dtype, down = {"e4m3": (ml_dtypes.float8_e4m3fn, 7), "e5m2": (ml_dtypes.float8_e5m2, 14)}[fmt]
    v = np.moveaxis(np.asarray(x, np.float32).astype(ml_dtypes.bfloat16).astype(np.float64), axis, -1)
    blocks = v.reshape(v.shape[:-1] + (-1, 32))
    amax = np.abs(blocks).max(-1, keepdims=True)
    byte = np.maximum(np.where(amax > 0, np.frexp(amax)[1] - 1 + 127, 0) - down, 1)
    scale = np.exp2(byte - 127.0)
    codes = (blocks / scale).astype(np.float32).astype(dtype).astype(np.float64)
    return np.moveaxis((codes * scale).reshape(v.shape), -1, axis)


WIDE = False


def mx_kscale(k):
    if not WIDE:
        return np.ones(k)
    levels = np.array([10, -10, 5, -5, 0])
    if k % 512:
        return np.exp2(np.random.permutation(np.resize(levels, k // 32))).repeat(32)
    a = np.empty((k // 512, 16))
    for p in range(k // 512):
        a[p, :8] = np.random.permutation(np.resize(levels, 8))
        for g in range(8):
            far = levels[np.abs(levels - a[p, g]) >= 10]
            a[p, g + 8] = far[np.random.randint(len(far))]
    return np.exp2(a.ravel()).repeat(32)


def f64(x):
    return np.asarray(x).astype(np.float64)


def striped(idx):
    return np.tile(idx.reshape(-1, 16).T, (8, 1)).astype(np.uint16)


def unstriped(offs):
    return offs[:16].T.reshape(-1).astype(np.int64)


E2M1 = np.array([0.0, 0.5, 1.0, 1.5, 2.0, 3.0, 4.0, 6.0, -0.0, -0.5, -1.0, -1.5, -2.0, -3.0, -4.0, -6.0])


def pack_weight(w, fmt):
    k, n = w.shape
    w = f64(np.asarray(w, np.float32).astype(ml_dtypes.bfloat16)).reshape(k // 32, 32, n)
    amax = np.abs(w).max(1)
    if fmt == "e4m3":
        byte = np.frexp(amax)[1] - 1 + 127 - 7
    else:
        mant, ex = np.frexp(amax / 6.0)
        byte = np.where(mant > 0.5, ex, ex - 1) + 127
    byte = np.clip(np.where(amax > 0, byte, 1), 1, 254)
    scaled = (w * np.exp2(127.0 - byte)[:, None, :]).reshape(k, n).astype(np.float32)
    by_word = np.ascontiguousarray(scaled.reshape(k // 512, 128, 4, n).transpose(0, 1, 3, 2))
    if fmt == "e4m3":
        words = by_word.astype(ml_dtypes.float8_e4m3fn).view(np.uint8)
    else:
        c = by_word.astype(ml_dtypes.float4_e2m1fn).view(np.uint8) & 0xF
        words = (c[..., 0::2] | (c[..., 1::2] << 4)).reshape(k // 512, 128, 2 * n)
    return np.ascontiguousarray(words), np.ascontiguousarray(byte.astype(np.uint8).reshape(k // 512, 16, n))


def unpack_weight(words, scales, fmt):
    g, _, n = scales.shape
    words = np.ascontiguousarray(words).reshape(g, 128, n, -1)
    if fmt == "e4m3":
        vals = words.view(ml_dtypes.float8_e4m3fn).astype(np.float64)
    else:
        nib = np.empty((g, 128, n, 4), np.uint8)
        nib[..., 0::2] = words & 0xF
        nib[..., 1::2] = words >> 4
        vals = E2M1[nib]
    vals = vals * np.repeat(np.exp2(scales.astype(np.float64) - 127.0), 8, axis=1)[..., None]
    return vals.transpose(0, 1, 3, 2).reshape(g * 512, n)


def gelu(v):
    return 0.5 * v * (1.0 + np.tanh(np.sqrt(2.0 / np.pi) * (v + 0.044715 * v**3)))


K, H, T, S, T2, P, S2, T3 = 1024, 512, 2048, 1024, 2048, 1024, 512, 1024

def setup_inputs():
    n = np.random.standard_normal
    s = mx_kscale(K)[:, None]
    u = mx_kscale(H)[:, None]
    tab_words, tab_scales = pack_weight(n((K, T)) * s, "e4m3")
    tab2_words, tab2_scales = pack_weight(0.35 * n((H, T3)) / np.sqrt(H) / u, "e4m3")
    w2_words, w2_scales = pack_weight(0.8 * n((K, H)) / np.sqrt(K) / s, "e2m1")
    w3_words, w3_scales = pack_weight(0.8 * n((K, H)) / np.sqrt(K) / s * u.T, "e4m3")
    return {
        "tab_words": tab_words, "tab_scales": tab_scales,
        "offs": striped(np.random.permutation(T)[:S]),
        "w1": (0.8 * n((K, H)) / np.sqrt(K) / s * u.T).astype(np.float32),
        "w2_words": w2_words, "w2_scales": w2_scales,
        "w3_words": w3_words, "w3_scales": w3_scales,
        "w4": (0.8 * n((K, H)) / np.sqrt(K) / s).astype(np.float32),
        "page0": (n((H, T2)) * u).astype(np.float32),
        "wgs": np.exp(0.3 * n((128, S))).astype(np.float32),
        "offs3": striped(np.random.permutation(T2)[:S]),
        "tab2_words": tab2_words, "tab2_scales": tab2_scales,
        "offs2": striped(np.random.permutation(T3)[:S2]),
        "offs4": striped(np.random.permutation(T2)[:P]),
        "mode": np.random.uniform(-1.0, 1.0, S2).astype(np.float32),
    }

def reference(tab_words, tab_scales, offs, w1, w2_words, w2_scales, w3_words, w3_scales, w4, page0, wgs, offs3, tab2_words, tab2_scales, offs2, offs4, mode):
    v = unpack_weight(tab_words, tab_scales, "e4m3")[:, unstriped(offs)]
    i0 = mxq(f64(w1), 0, "e4m3").T @ v
    q1 = unpack_weight(w2_words, w2_scales, "e2m1").T @ v
    q0 = unpack_weight(w3_words, w3_scales, "e4m3").T @ v
    i1 = mxq(f64(w4), 0, "e4m3").T @ v
    h = i0 * q1 - q0 * i1
    page = f64(page0).copy()
    page[:, unstriped(offs3)] = np.tile(f64(wgs), (H // 128, 1)) * h
    v2 = unpack_weight(tab2_words, tab2_scales, "e4m3")[:, unstriped(offs2)]
    e = v2.T @ mxq(page, 0, "e4m3")
    x = e[:, unstriped(offs4)]
    return np.cos(x + f64(mode)[:, None])

@@ -1,0 +1,317 @@
+import math
+from contextlib import ExitStack
+
+import concourse.mybir as mybir
+from concourse.masks import make_identity
+
+K, H, T, S, T2, PICK, S2, T3 = 1024, 512, 2048, 1024, 2048, 1024, 512, 1024
+FLOPS = 2 * (4 * K * H * S + H * S2 * T2)
+
+F32 = mybir.dt.float32
+BF16 = mybir.dt.bfloat16
+I32 = mybir.dt.int32
+U32 = mybir.dt.uint32
+U16 = mybir.dt.uint16
+U8 = mybir.dt.uint8
+FP8X4 = mybir.dt.float8_e4m3fn_x4
+FP4X4 = mybir.dt.float4_e2m1fn_x4
+ALU = mybir.AluOpType
+ACT = mybir.ActivationFunctionType
+
+P = 128
+PACK = 4
+N = 512
+PASSES = K // (P * PACK)
+HALVES = S // N
+TILES_PER_HALF = N // P
+CHUNKS = T2 // N
+PER_COL = 16
+BANKS = 8
+PRODUCT_BANKS = 6
+TWO_PI = 2.0 * math.pi
+
+
+def tile_list_track_phase_board_kernel(
+    tc, tab_words, tab_scales, offs, w1, w2_words, w2_scales, w3_words, w3_scales, w4,
+    page0, wgs, offs3, tab2_words, tab2_scales, offs2, offs4, mode, out,
+):
+    nc = tc.nc
+    with ExitStack() as ctx:
+        keep = ctx.enter_context(tc.tile_pool(name="keep", bufs=1))
+        ring = ctx.enter_context(tc.tile_pool(name="ring", bufs=1))
+        psum = ctx.enter_context(tc.psum_pool(name="psum", bufs=1))
+
+        def kept(shape, dtype, name):
+            return keep.tile(shape, dtype, name=name, align_bytes=64)
+
+        def slab(shape, name):
+            return ring.tile(shape, F32, name=name, tag="slab", bufs=4, align_bytes=64)
+
+        def woven(name):
+            return ring.tile([P, PACK * N], BF16, name=name, tag="woven", bufs=4, align_bytes=64)
+
+        def piece(shape, dtype, name):
+            return ring.tile(shape, dtype, name=name, tag="piece", bufs=20, align_bytes=64)
+
+        banks = [psum.tile([P, N], F32, name=f"bank{b}") for b in range(BANKS)]
+        product_banks, turn_banks = banks[:PRODUCT_BANKS], banks[PRODUCT_BANKS:]
+
+        def next_bank(rotation):
+            rotation.append(rotation.pop(0))
+            return rotation[-1]
+
+        def load_list(source, name):
+            tile = keep.tile(list(source.shape), U16, name=name)
+            nc.sync.dma_start(tile[:], source)
+            return tile
+
+        def zeroed_plane(shape, name):
+            tile = kept(shape, U8, name)
+            nc.vector.memset(tile[:].bitcast(I32), 0)
+            return tile
+
+        def load_weight_scales(tile, source):
+            for q in range(4):
+                nc.sync.dma_start(
+                    tile[32 * q : 32 * q + 4, :, :].bitcast(I32),
+                    source[:, 4 * q : 4 * q + 4, :].rearrange("a r c -> r a c").bitcast(I32),
+                )
+
+        def entries(tile, first, count):
+            return tile[:, first // PER_COL : (first + count) // PER_COL]
+
+        tab_plane = zeroed_plane([P, T], "tab_plane")
+        w3_plane = zeroed_plane([P, PASSES, H], "w3_plane")
+        w2_plane = zeroed_plane([P, PASSES, H], "w2_plane")
+        tab2_plane = zeroed_plane([P, T3], "tab2_plane")
+        v_plane1 = zeroed_plane([P, S], "v_plane1")
+        ident = kept([P, P], F32, "ident")
+        make_identity(nc, ident[:])
+        warm = kept([P, 1], F32, "warm")
+        nc.scalar.activation(warm[:], ident[:, 0:1], ACT.Sin)
+
+        def load_raw(w, a, name):
+            raw = slab([P, PACK, H], name)
+            nc.sync.dma_start(raw[:], w[N * a : N * (a + 1), :].rearrange("(p i) c -> p i c", i=PACK))
+            return raw
+
+        def load_words(source, columns, name):
+            tile = kept([P, columns], I32, name)
+            nc.sync.dma_start(tile[:], source.rearrange("p n i -> p (n i)").bitcast(I32))
+            return tile
+
+        page_rows = page0.rearrange("(p t) c -> t p c", t=PACK)
+        wgs_rows = wgs.rearrange("(m t) j -> t m j", t=PACK)
+        page = [kept([P, T2], F32, f"page{t}") for t in range(PACK)]
+        weight = [kept([P, S], F32, f"weight{t}") for t in range(PACK)]
+
+        def load_board(t):
+            nc.sync.dma_start(page[t][:], page_rows[t])
+            for q in (0, 2, 1, 3):
+                nc.sync.dma_start(weight[t][32 * q : 32 * q + 32, :], wgs_rows[t])
+
+        list2 = load_list(offs2, "list2")
+        tab2 = load_words(tab2_words[0], T3, "tab2")
+        list1 = load_list(offs, "list1")
+        tab = [load_words(tab_words[0], T, "tab0")]
+        for q in range(4):
+            nc.sync.dma_start(
+                tab_plane[32 * q : 32 * q + 4 * PASSES, :].bitcast(I32),
+                tab_scales[:, 4 * q : 4 * q + 4, :].bitcast(I32),
+            )
+        tab.append(load_words(tab_words[1], T, "tab1"))
+        w3_codes = kept([P, PASSES, H], U32, "w3_codes")
+        nc.sync.dma_start(w3_codes[:].bitcast(I32), w3_words.rearrange("a p n i -> p a (n i)").bitcast(I32))
+        load_weight_scales(w3_plane, w3_scales)
+        w4_raw = [load_raw(w4, 0, "w4_raw0")]
+        w2_codes = kept([P, PASSES, 2 * H], U8, "w2_codes")
+        nc.sync.dma_start(w2_codes[:].bitcast(I32), w2_words.rearrange("a p n -> p a n").bitcast(I32))
+        load_weight_scales(w2_plane, w2_scales)
+        w4_raw.append(load_raw(w4, 1, "w4_raw1"))
+        for q in range(4):
+            nc.sync.dma_start(
+                tab2_plane[32 * q : 32 * q + 4, :].bitcast(I32), tab2_scales[0, 4 * q : 4 * q + 4, :].bitcast(I32)
+            )
+        w1_raw = [load_raw(w1, 0, "w1_raw0")]
+        w1_raw.append(load_raw(w1, 1, "w1_raw1"))
+        list3 = load_list(offs3, "list3")
+        load_board(0)
+        load_board(1)
+        load_board(2)
+        load_board(3)
+        list4 = load_list(offs4, "list4")
+        phase = kept([P, S2 // P], F32, "phase")
+        with nc.allow_non_contiguous_dma(reason="one phase offset a partition"):
+            nc.sync.dma_start(phase[:], mode.rearrange("(n p) -> p n", p=P))
+
+        v2_codes = kept([P, S2], U32, "v2_codes")
+        v2_plane = kept([P, S2], U8, "v2_plane")
+        nc.vector.tensor_copy(v2_codes[:], tab2[:].bitcast(U32).indirect(list2[:]))
+        v_plane = kept([P, S], U8, "v_plane")
+        nc.vector.tensor_copy(v_plane[:], tab_plane[:].indirect(list1[:]))
+        nc.scalar.dma_start(v_plane1[0:112, :].bitcast(I32), v_plane[4:116, :].bitcast(I32))
+        nc.vector.tensor_copy(v2_plane[:], tab2_plane[:].indirect(list2[:]))
+        v_codes = [[None] * HALVES for a in range(PASSES)]
+        for h in range(HALVES):
+            for a in range(PASSES):
+                v_codes[a][h] = kept([P, N], U32, f"v_codes{a}_{h}")
+                nc.vector.tensor_copy(v_codes[a][h][:], tab[a][:].bitcast(U32).indirect(entries(list1, N * h, N)))
+
+        def product(h, jj, codes, planes, fp4, name):
+            bank = next_bank(product_banks)
+            cols = slice(P * jj, P * (jj + 1))
+            for a in range(PASSES):
+                if fp4 and a == 1:
+                    v_scale = v_plane1[:, N * h + P * jj : N * h + P * (jj + 1)]
+                else:
+                    v_scale = v_plane[4 * a : P, N * h + P * jj : N * h + P * (jj + 1)]
+                nc.tensor.matmul_mx(
+                    out=bank[:], lhsT=v_codes[a][h][:, cols].bitcast(FP8X4), lhsT_scale=v_scale,
+                    rhs=codes[a], rhs_scale=planes[a], start=(a == 0), stop=(a == PASSES - 1),
+                )
+            return bank
+
+        def quadrature(h, codes, planes, fp4, sign, name):
+            tiles = []
+            for jj in range(TILES_PER_HALF):
+                bank = product(h, jj, codes, planes, fp4, f"{name}_bank{h}_{jj}")
+                tile = piece([P, H], F32, f"{name}{h}_{jj}")
+                nc.scalar.activation(
+                    tile[:].rearrange("p (t m) -> p m t", t=PACK),
+                    bank[:].rearrange("p (m t) -> p m t", t=PACK), ACT.Copy, scale=sign,
+                )
+                tiles.append(tile)
+            return tiles
+
+        def times_in_phase(h, tiles, codes, planes, name):
+            for jj in range(TILES_PER_HALF):
+                bank = product(h, jj, codes, planes, False, f"{name}_bank{h}_{jj}")
+                nc.vector.tensor_tensor(tiles[jj][:], bank[:], tiles[jj][:], ALU.mult)
+
+        def weave_weight(raw, name, vector_share):
+            tile = woven(name)
+            dst = tile[:].rearrange("p (t m i) -> p m i t", t=PACK, i=PACK)
+            src = raw[:].rearrange("p i (m t) -> p m i t", t=PACK)
+            if vector_share > 0:
+                nc.vector.tensor_copy(dst[:, :vector_share], src[:, :vector_share])
+            if vector_share < P:
+                nc.scalar.copy(dst[:, vector_share:], src[:, vector_share:])
+            return tile
+
+        def quantize(tile, name):
+            codes = kept([P, N], U32, f"{name}_codes")
+            plane = kept([P, N], U8, f"{name}_plane")
+            nc.vector.quantize_mx(out=codes[:].bitcast(FP8X4), scales=plane[:], in_=tile[:])
+            return codes[:].bitcast(FP8X4), plane[:]
+
+        w2_c = [w2_codes[:, a, :].bitcast(FP4X4) for a in range(PASSES)]
+        w2_p = [w2_plane[:, a, :] for a in range(PASSES)]
+        w3_c = [w3_codes[:, a, :].bitcast(FP8X4) for a in range(PASSES)]
+        w3_p = [w3_plane[:, a, :] for a in range(PASSES)]
+
+        def quantize_weight(raws, shares, name):
+            both = [quantize(weave_weight(raws[a], f"{name}_woven{a}", shares[a]), f"{name}_{a}") for a in range(PASSES)]
+            return [x[0] for x in both], [x[1] for x in both]
+
+        cross = [kept([P, S], F32, f"cross{t}") for t in range(PACK)]
+
+        def turn(t, first, count):
+            bank = next_bank(turn_banks)
+            for k in reversed(range(count // P)):
+                h, jj = divmod(first // P + k, TILES_PER_HALF)
+                for n, term in enumerate((term_a, term_b)):
+                    nc.tensor.matmul(
+                        bank[:, P * k : P * (k + 1)], term[h][jj][:, P * t : P * (t + 1)], ident[:],
+                        start=(n == 0), stop=(n == 1), is_transpose=True,
+                    )
+            nc.scalar.copy(cross[t][:, first : first + count], bank[:, :count])
+
+        def scatter(t, first, count):
+            cols = slice(first, first + count)
+            nc.vector.tensor_tensor(
+                page[t][:].indirect(entries(list3, first, count)), cross[t][:, cols], weight[t][:, cols], ALU.mult
+            )
+
+        w4_c, w4_p = quantize_weight(w4_raw, (P, P), "w4")
+        term_b = [quadrature(0, w3_c, w3_p, False, -1.0, "term_b")]
+        term_a = [quadrature(0, w2_c, w2_p, True, 1.0, "term_a")]
+        times_in_phase(0, term_b[0], w4_c, w4_p, "i1")
+        term_b.append(quadrature(1, w3_c, w3_p, False, -1.0, "term_b"))
+        w1_c, w1_p = quantize_weight(w1_raw, (P, 64), "w1")
+        times_in_phase(0, term_a[0], w1_c, w1_p, "i0")
+        turn(0, 0, N // 2)
+        turn(0, N // 2, N // 2)
+        scatter(0, 0, N // 2)
+        scatter(0, N // 2, N // 2)
+        times_in_phase(1, term_b[1], w4_c, w4_p, "i1")
+        term_a.append(quadrature(1, w2_c, w2_p, True, 1.0, "term_a"))
+        times_in_phase(1, term_a[1], w1_c, w1_p, "i0")
+        turn(1, 0, N)
+        scatter(1, 0, N)
+        for t in range(2):
+            turn(t, N, N)
+            scatter(t, N, N)
+        for t in range(2, PACK):
+            turn(t, 0, N)
+            turn(t, N, N)
+
+        board = [woven(f"board{c}") for c in range(CHUNKS)]
+
+        def round_rows(engine_copy, pair, t, c):
+            engine_copy(pair[:, t % 2, :], page[t][:, N * c : N * (c + 1)])
+
+        def weave_pair(engine_copy, pair, u, c):
+            engine_copy(
+                board[c][:].rearrange("p (c i) -> p c i", i=PACK)[:, :, 2 * u : 2 * u + 2],
+                pair[:].rearrange("p i c -> p c i"),
+            )
+
+        low = [piece([P, 2, N], BF16, f"low{c}") for c in range(CHUNKS)]
+        high = [piece([P, 2, N], BF16, f"high{c}") for c in range(CHUNKS)]
+        for t in range(2):
+            for c in range(CHUNKS):
+                round_rows(nc.scalar.copy, low[c], t, c)
+        for c in range(CHUNKS):
+            weave_pair(nc.scalar.copy, low[c], 0, c)
+        scatter(2, 0, S)
+        for c in range(CHUNKS):
+            round_rows(nc.scalar.copy, high[c], 2, c)
+        scatter(3, 0, S)
+        copies = (nc.vector.tensor_copy, nc.vector.tensor_copy, nc.scalar.copy, nc.scalar.copy)
+        for c in (0, 1):
+            round_rows(copies[c], high[c], 3, c)
+        for c in (0, 1):
+            weave_pair(copies[c], high[c], 1, c)
+        for c in (2, 3):
+            round_rows(copies[c], high[c], 3, c)
+            weave_pair(copies[c], high[c], 1, c)
+        board_q = [quantize(board[c], f"board{c}") for c in range(CHUNKS)]
+
+        match = []
+        for n in range(S2 // P):
+            rows = slice(P * n, P * (n + 1))
+            match.append(slab([P, T2], f"match{n}"))
+            for c in range(CHUNKS):
+                bank = banks[CHUNKS * (n % 2) + (c if n < 2 else CHUNKS - 1 - c)]
+                nc.tensor.matmul_mx(
+                    out=bank[:], lhsT=v2_codes[:, rows].bitcast(FP8X4), lhsT_scale=v2_plane[:, rows],
+                    rhs=board_q[c][0], rhs_scale=board_q[c][1], start=True, stop=True,
+                )
+                nc.scalar.copy(match[n][:, N * c : N * (c + 1)], bank[:])
+
+        for n in range(S2 // P):
+            rows = slice(P * n, P * (n + 1))
+            offset = phase[:, n : n + 1]
+            widths = (N, N // 2, N // 2) if n == S2 // P - 1 else (N, N)
+            first = 0
+            for k, width in enumerate(widths):
+                picked = piece([P, width], F32, f"picked{n}_{k}")
+                turns = piece([P, width], I32, f"turns{n}_{k}")
+                angle = piece([P, width], F32, f"angle{n}_{k}")
+                nc.vector.tensor_copy(picked[:], match[n][:].indirect(entries(list4, first, width)))
+                nc.vector.tensor_scalar(turns[:], picked[:], offset, 1.0 / TWO_PI, ALU.add, ALU.mult)
+                nc.vector.scalar_tensor_tensor(angle[:], turns[:], -TWO_PI, picked[:], ALU.mult, ALU.add)
+                nc.scalar.activation(angle[:], angle[:], ACT.Abs, bias=offset)
+                nc.scalar.activation(angle[:], angle[:], ACT.Sin, bias=math.pi / 2, scale=-1.0)
+                nc.sync.dma_start(out[rows, first : first + width], angle[:])
+                first = first + width

@@ -50,11 +50,11 @@ def tile_list_track_phase_board_kernel(
         def woven(name):
             return ring.tile([P, PACK * N], BF16, name=name, tag="woven", bufs=4, align_bytes=64)
 
-        def piece(shape, dtype, name):
-            return ring.tile(shape, dtype, name=name, tag="piece", bufs=20, align_bytes=64)
+        def piece(shape, dtype, name, place):
+            return ring.tile(shape, dtype, name=name, tag=f"place{place}", align_bytes=64)
 
         banks = [psum.tile([P, N], F32, name=f"bank{b}") for b in range(BANKS)]
-        product_banks, turn_banks = banks[:PRODUCT_BANKS], banks[PRODUCT_BANKS:]
+        product_banks, turn_banks, match_banks = banks[:PRODUCT_BANKS], banks[PRODUCT_BANKS:], banks[:]
 
         def next_bank(rotation):
             rotation.append(rotation.pop(0))
@@ -171,11 +171,11 @@ def tile_list_track_phase_board_kernel(
                 )
             return bank
 
-        def quadrature(h, codes, planes, fp4, sign, name):
+        def quadrature(h, codes, planes, fp4, sign, name, place):
             tiles = []
             for jj in range(TILES_PER_HALF):
                 bank = product(h, jj, codes, planes, fp4, f"{name}_bank{h}_{jj}")
-                tile = piece([P, H], F32, f"{name}{h}_{jj}")
+                tile = piece([P, H], F32, f"{name}{h}_{jj}", place + jj)
                 nc.scalar.activation(
                     tile[:].rearrange("p (t m) -> p m t", t=PACK),
                     bank[:].rearrange("p (m t) -> p m t", t=PACK), ACT.Copy, scale=sign,
@@ -183,15 +183,15 @@ def tile_list_track_phase_board_kernel(
                 tiles.append(tile)
             return tiles
 
-        def times_in_phase(h, tiles, codes, planes, name):
+        def times_in_phase(h, tiles, codes, planes, results):
             for jj in range(TILES_PER_HALF):
-                bank = product(h, jj, codes, planes, False, f"{name}_bank{h}_{jj}")
-                nc.vector.tensor_tensor(tiles[jj][:], bank[:], tiles[jj][:], ALU.mult)
+                bank = product(h, jj, codes, planes, False, "")
+                nc.vector.tensor_tensor(results[jj][:], bank[:], tiles[jj][:], ALU.mult)
 
         def weave_weight(raw, name, vector_share):
             tile = woven(name)
-            dst = tile[:].rearrange("p (t m i) -> p m i t", t=PACK, i=PACK)
-            src = raw[:].rearrange("p i (m t) -> p m i t", t=PACK)
+            dst = tile[:].rearrange("p (t m i) -> p m t i", t=PACK, i=PACK)
+            src = raw[:].rearrange("p i (m t) -> p m t i", t=PACK)
             if vector_share > 0:
                 nc.vector.tensor_copy(dst[:, :vector_share], src[:, :vector_share])
             if vector_share < P:
@@ -215,8 +215,8 @@ def tile_list_track_phase_board_kernel(
 
         cross = [kept([P, S], F32, f"cross{t}") for t in range(PACK)]
 
-        def turn(t, first, count):
-            bank = next_bank(turn_banks)
+        def turn(t, first, count, rotation, result):
+            bank = next_bank(rotation)
             for k in reversed(range(count // P)):
                 h, jj = divmod(first // P + k, TILES_PER_HALF)
                 for n, term in enumerate((term_a, term_b)):
@@ -224,36 +224,38 @@ def tile_list_track_phase_board_kernel(
                         bank[:, P * k : P * (k + 1)], term[h][jj][:, P * t : P * (t + 1)], ident[:],
                         start=(n == 0), stop=(n == 1), is_transpose=True,
                     )
-            nc.scalar.copy(cross[t][:, first : first + count], bank[:, :count])
+            nc.scalar.copy(result, bank[:, :count])
 
-        def scatter(t, first, count):
-            cols = slice(first, first + count)
+        def scatter(t, first, count, values):
             nc.vector.tensor_tensor(
-                page[t][:].indirect(entries(list3, first, count)), cross[t][:, cols], weight[t][:, cols], ALU.mult
+                page[t][:].indirect(entries(list3, first, count)), values, weight[t][:, first : first + count], ALU.mult
             )
 
         w4_c, w4_p = quantize_weight(w4_raw, (P, P), "w4")
-        term_b = [quadrature(0, w3_c, w3_p, False, -1.0, "term_b")]
-        term_a = [quadrature(0, w2_c, w2_p, True, 1.0, "term_a")]
-        times_in_phase(0, term_b[0], w4_c, w4_p, "i1")
-        term_b.append(quadrature(1, w3_c, w3_p, False, -1.0, "term_b"))
+        term_b = [quadrature(0, w3_c, w3_p, False, -1.0, "term_b", 0)]
+        term_a = [quadrature(0, w2_c, w2_p, True, 1.0, "term_a", 8)]
+        times_in_phase(0, term_b[0], w4_c, w4_p, term_b[0])
+        term_b.append(quadrature(1, w3_c, w3_p, False, -1.0, "term_b", 4))
         w1_c, w1_p = quantize_weight(w1_raw, (P, 64), "w1")
-        times_in_phase(0, term_a[0], w1_c, w1_p, "i0")
-        turn(0, 0, N // 2)
-        turn(0, N // 2, N // 2)
-        scatter(0, 0, N // 2)
-        scatter(0, N // 2, N // 2)
-        times_in_phase(1, term_b[1], w4_c, w4_p, "i1")
-        term_a.append(quadrature(1, w2_c, w2_p, True, 1.0, "term_a"))
-        times_in_phase(1, term_a[1], w1_c, w1_p, "i0")
-        turn(1, 0, N)
-        scatter(1, 0, N)
+        times_in_phase(0, term_a[0], w1_c, w1_p, term_a[0])
+        for first in (0, N // 2):
+            turn(0, first, N // 2, turn_banks, cross[0][:, first : first + N // 2])
+        for first in (0, N // 2):
+            scatter(0, first, N // 2, cross[0][:, first : first + N // 2])
+        times_in_phase(1, term_b[1], w4_c, w4_p, term_b[1])
+        factor = quadrature(1, w2_c, w2_p, True, 1.0, "factor", 12)
+        term_a.append([piece([P, H], F32, f"term_a1_{jj}", 16 + jj) for jj in range(TILES_PER_HALF)])
+        times_in_phase(1, factor, w1_c, w1_p, term_a[1])
+        held = piece([P, N], F32, "held", 13)
+        turn(1, 0, N, turn_banks, held[:])
+        scatter(1, 0, N, held[:])
         for t in range(2):
-            turn(t, N, N)
-            scatter(t, N, N)
+            turn(t, N, N, banks, cross[t][:, N:])
         for t in range(2, PACK):
-            turn(t, 0, N)
-            turn(t, N, N)
+            for first in (0, N):
+                turn(t, first, N, banks, cross[t][:, first : first + N])
+        for t in range(2):
+            scatter(t, N, N, cross[t][:, N:])
 
         board = [woven(f"board{c}") for c in range(CHUNKS)]
 
@@ -266,17 +268,17 @@ def tile_list_track_phase_board_kernel(
                 pair[:].rearrange("p i c -> p c i"),
             )
 
-        low = [piece([P, 2, N], BF16, f"low{c}") for c in range(CHUNKS)]
-        high = [piece([P, 2, N], BF16, f"high{c}") for c in range(CHUNKS)]
+        low = [piece([P, 2, N], BF16, f"low{c}", 4 + c) for c in range(CHUNKS)]
+        high = [piece([P, 2, N], BF16, f"high{c}", c) for c in range(CHUNKS)]
         for t in range(2):
             for c in range(CHUNKS):
                 round_rows(nc.scalar.copy, low[c], t, c)
         for c in range(CHUNKS):
             weave_pair(nc.scalar.copy, low[c], 0, c)
-        scatter(2, 0, S)
+        scatter(2, 0, S, cross[2][:])
         for c in range(CHUNKS):
             round_rows(nc.scalar.copy, high[c], 2, c)
-        scatter(3, 0, S)
+        scatter(3, 0, S, cross[3][:])
         copies = (nc.vector.tensor_copy, nc.vector.tensor_copy, nc.scalar.copy, nc.scalar.copy)
         for c in (0, 1):
             round_rows(copies[c], high[c], 3, c)
@@ -292,22 +294,23 @@ def tile_list_track_phase_board_kernel(
             rows = slice(P * n, P * (n + 1))
             match.append(slab([P, T2], f"match{n}"))
             for c in range(CHUNKS):
-                bank = banks[CHUNKS * (n % 2) + (c if n < 2 else CHUNKS - 1 - c)]
+                bank = match_banks[c]
                 nc.tensor.matmul_mx(
                     out=bank[:], lhsT=v2_codes[:, rows].bitcast(FP8X4), lhsT_scale=v2_plane[:, rows],
                     rhs=board_q[c][0], rhs_scale=board_q[c][1], start=True, stop=True,
                 )
                 nc.scalar.copy(match[n][:, N * c : N * (c + 1)], bank[:])
 
+        done = 0
         for n in range(S2 // P):
             rows = slice(P * n, P * (n + 1))
             offset = phase[:, n : n + 1]
             widths = (N, N // 2, N // 2) if n == S2 // P - 1 else (N, N)
             first = 0
             for k, width in enumerate(widths):
-                picked = piece([P, width], F32, f"picked{n}_{k}")
-                turns = piece([P, width], I32, f"turns{n}_{k}")
-                angle = piece([P, width], F32, f"angle{n}_{k}")
+                picked = piece([P, width], F32, f"picked{n}_{k}", done % 4)
+                turns = piece([P, width], I32, f"turns{n}_{k}", 4 + done % 4)
+                angle = piece([P, width], F32, f"angle{n}_{k}", 8 + done)
                 nc.vector.tensor_copy(picked[:], match[n][:].indirect(entries(list4, first, width)))
                 nc.vector.tensor_scalar(turns[:], picked[:], offset, 1.0 / TWO_PI, ALU.add, ALU.mult)
                 nc.vector.scalar_tensor_tensor(angle[:], turns[:], -TWO_PI, picked[:], ALU.mult, ALU.add)
@@ -315,3 +318,4 @@ def tile_list_track_phase_board_kernel(
                 nc.scalar.activation(angle[:], angle[:], ACT.Sin, bias=math.pi / 2, scale=-1.0)
                 nc.sync.dma_start(out[rows, first : first + width], angle[:])
                 first = first + width
+                done = done + 1

@@ -47,8 +47,8 @@ def tile_list_track_phase_board_kernel(
         def slab(shape, name):
             return ring.tile(shape, F32, name=name, tag="slab", bufs=4, align_bytes=64)
 
-        def woven(name):
-            return ring.tile([P, PACK * N], BF16, name=name, tag="woven", bufs=4, align_bytes=64)
+        def woven(name, place):
+            return ring.tile([P, PACK * N], BF16, name=name, tag=f"woven{place}", align_bytes=64)
 
         def piece(shape, dtype, name, place):
             return ring.tile(shape, dtype, name=name, tag=f"place{place}", align_bytes=64)
@@ -65,14 +65,14 @@ def tile_list_track_phase_board_kernel(
             nc.sync.dma_start(tile[:], source)
             return tile
 
-        def zeroed_plane(shape, name):
+        def zeroed_plane(shape, name, engine):
             tile = kept(shape, U8, name)
-            nc.vector.memset(tile[:].bitcast(I32), 0)
+            engine.memset(tile[:].bitcast(I32), 0)
             return tile
 
-        def load_weight_scales(tile, source):
+        def load_weight_scales(tile, source, queue):
             for q in range(4):
-                nc.sync.dma_start(
+                queue.dma_start(
                     tile[32 * q : 32 * q + 4, :, :].bitcast(I32),
                     source[:, 4 * q : 4 * q + 4, :].rearrange("a r c -> r a c").bitcast(I32),
                 )
@@ -80,11 +80,11 @@ def tile_list_track_phase_board_kernel(
         def entries(tile, first, count):
             return tile[:, first // PER_COL : (first + count) // PER_COL]
 
-        tab_plane = zeroed_plane([P, T], "tab_plane")
-        w3_plane = zeroed_plane([P, PASSES, H], "w3_plane")
-        w2_plane = zeroed_plane([P, PASSES, H], "w2_plane")
-        tab2_plane = zeroed_plane([P, T3], "tab2_plane")
-        v_plane1 = zeroed_plane([P, S], "v_plane1")
+        tab_plane = zeroed_plane([P, T], "tab_plane", nc.gpsimd)
+        w3_plane = zeroed_plane([P, PASSES, H], "w3_plane", nc.vector)
+        w2_plane = zeroed_plane([P, PASSES, H], "w2_plane", nc.vector)
+        tab2_plane = zeroed_plane([P, T3], "tab2_plane", nc.vector)
+        v_plane1 = zeroed_plane([P, S], "v_plane1", nc.vector)
         ident = kept([P, P], F32, "ident")
         make_identity(nc, ident[:])
         warm = kept([P, 1], F32, "warm")
@@ -110,33 +110,36 @@ def tile_list_track_phase_board_kernel(
             for q in (0, 2, 1, 3):
                 nc.sync.dma_start(weight[t][32 * q : 32 * q + 32, :], wgs_rows[t])
 
-        list2 = load_list(offs2, "list2")
-        tab2 = load_words(tab2_words[0], T3, "tab2")
         list1 = load_list(offs, "list1")
-        tab = [load_words(tab_words[0], T, "tab0")]
         for q in range(4):
             nc.sync.dma_start(
                 tab_plane[32 * q : 32 * q + 4 * PASSES, :].bitcast(I32),
                 tab_scales[:, 4 * q : 4 * q + 4, :].bitcast(I32),
             )
+        tab = [load_words(tab_words[0], T, "tab0")]
+        w4_raw = [load_raw(w4, 0, "w4_raw0")]
         tab.append(load_words(tab_words[1], T, "tab1"))
         w3_codes = kept([P, PASSES, H], U32, "w3_codes")
         nc.sync.dma_start(w3_codes[:].bitcast(I32), w3_words.rearrange("a p n i -> p a (n i)").bitcast(I32))
-        load_weight_scales(w3_plane, w3_scales)
-        w4_raw = [load_raw(w4, 0, "w4_raw0")]
+        load_weight_scales(w3_plane, w3_scales, nc.sync)
+        v_plane = kept([P, S], U8, "v_plane")
+        nc.vector.tensor_copy(v_plane[:], tab_plane[:].indirect(list1[:]))
+        nc.sync.dma_start(v_plane1[0:112, :].bitcast(I32), v_plane[4:116, :].bitcast(I32))
+        w4_raw.append(load_raw(w4, 1, "w4_raw1"))
         w2_codes = kept([P, PASSES, 2 * H], U8, "w2_codes")
         nc.sync.dma_start(w2_codes[:].bitcast(I32), w2_words.rearrange("a p n -> p a n").bitcast(I32))
-        load_weight_scales(w2_plane, w2_scales)
-        w4_raw.append(load_raw(w4, 1, "w4_raw1"))
-        for q in range(4):
-            nc.sync.dma_start(
-                tab2_plane[32 * q : 32 * q + 4, :].bitcast(I32), tab2_scales[0, 4 * q : 4 * q + 4, :].bitcast(I32)
-            )
+        load_weight_scales(w2_plane, w2_scales, nc.sync)
         w1_raw = [load_raw(w1, 0, "w1_raw0")]
         w1_raw.append(load_raw(w1, 1, "w1_raw1"))
         list3 = load_list(offs3, "list3")
         load_board(0)
         load_board(1)
+        list2 = load_list(offs2, "list2")
+        tab2 = load_words(tab2_words[0], T3, "tab2")
+        for q in range(4):
+            nc.sync.dma_start(
+                tab2_plane[32 * q : 32 * q + 4, :].bitcast(I32), tab2_scales[0, 4 * q : 4 * q + 4, :].bitcast(I32)
+            )
         load_board(2)
         load_board(3)
         list4 = load_list(offs4, "list4")
@@ -144,13 +147,6 @@ def tile_list_track_phase_board_kernel(
         with nc.allow_non_contiguous_dma(reason="one phase offset a partition"):
             nc.sync.dma_start(phase[:], mode.rearrange("(n p) -> p n", p=P))
 
-        v2_codes = kept([P, S2], U32, "v2_codes")
-        v2_plane = kept([P, S2], U8, "v2_plane")
-        nc.vector.tensor_copy(v2_codes[:], tab2[:].bitcast(U32).indirect(list2[:]))
-        v_plane = kept([P, S], U8, "v_plane")
-        nc.vector.tensor_copy(v_plane[:], tab_plane[:].indirect(list1[:]))
-        nc.scalar.dma_start(v_plane1[0:112, :].bitcast(I32), v_plane[4:116, :].bitcast(I32))
-        nc.vector.tensor_copy(v2_plane[:], tab2_plane[:].indirect(list2[:]))
         v_codes = [[None] * HALVES for a in range(PASSES)]
         for h in range(HALVES):
             for a in range(PASSES):
@@ -177,8 +173,8 @@ def tile_list_track_phase_board_kernel(
                 bank = product(h, jj, codes, planes, fp4, f"{name}_bank{h}_{jj}")
                 tile = piece([P, H], F32, f"{name}{h}_{jj}", place + jj)
                 nc.scalar.activation(
-                    tile[:].rearrange("p (t m) -> p m t", t=PACK),
-                    bank[:].rearrange("p (m t) -> p m t", t=PACK), ACT.Copy, scale=sign,
+                    tile[:].rearrange("p (t g e) -> p g t e", t=PACK, e=PACK),
+                    bank[:].rearrange("p (g e t) -> p g t e", t=PACK, e=PACK), ACT.Copy, scale=sign,
                 )
                 tiles.append(tile)
             return tiles
@@ -188,8 +184,8 @@ def tile_list_track_phase_board_kernel(
                 bank = product(h, jj, codes, planes, False, "")
                 nc.vector.tensor_tensor(results[jj][:], bank[:], tiles[jj][:], ALU.mult)
 
-        def weave_weight(raw, name, vector_share):
-            tile = woven(name)
+        def weave_weight(raw, name, vector_share, place):
+            tile = woven(name, place)
             dst = tile[:].rearrange("p (t m i) -> p m t i", t=PACK, i=PACK)
             src = raw[:].rearrange("p i (m t) -> p m t i", t=PACK)
             if vector_share > 0:
@@ -209,9 +205,14 @@ def tile_list_track_phase_board_kernel(
         w3_c = [w3_codes[:, a, :].bitcast(FP8X4) for a in range(PASSES)]
         w3_p = [w3_plane[:, a, :] for a in range(PASSES)]
 
-        def quantize_weight(raws, shares, name):
-            both = [quantize(weave_weight(raws[a], f"{name}_woven{a}", shares[a]), f"{name}_{a}") for a in range(PASSES)]
+        def quantize_weight(raws, shares, name, place):
+            both = [quantize(weave_weight(raws[a], f"{name}_woven{a}", shares[a], place + a), f"{name}_{a}") for a in range(PASSES)]
             return [x[0] for x in both], [x[1] for x in both]
+
+        def pick_modes(codes, plane, first, count):
+            nc.vector.tensor_copy(codes[:], tab2[:].bitcast(U32).indirect(entries(list2, first, count)))
+            nc.vector.tensor_copy(plane[:], tab2_plane[:].indirect(entries(list2, first, count)))
+            return codes, plane
 
         cross = [kept([P, S], F32, f"cross{t}") for t in range(PACK)]
 
@@ -231,12 +232,12 @@ def tile_list_track_phase_board_kernel(
                 page[t][:].indirect(entries(list3, first, count)), values, weight[t][:, first : first + count], ALU.mult
             )
 
-        w4_c, w4_p = quantize_weight(w4_raw, (P, P), "w4")
+        w4_c, w4_p = quantize_weight(w4_raw, (0, P), "w4", 0)
         term_b = [quadrature(0, w3_c, w3_p, False, -1.0, "term_b", 0)]
         term_a = [quadrature(0, w2_c, w2_p, True, 1.0, "term_a", 8)]
         times_in_phase(0, term_b[0], w4_c, w4_p, term_b[0])
         term_b.append(quadrature(1, w3_c, w3_p, False, -1.0, "term_b", 4))
-        w1_c, w1_p = quantize_weight(w1_raw, (P, 64), "w1")
+        w1_c, w1_p = quantize_weight(w1_raw, (P, 0), "w1", 2)
         times_in_phase(0, term_a[0], w1_c, w1_p, term_a[0])
         for first in (0, N // 2):
             turn(0, first, N // 2, turn_banks, cross[0][:, first : first + N // 2])
@@ -246,7 +247,8 @@ def tile_list_track_phase_board_kernel(
         factor = quadrature(1, w2_c, w2_p, True, 1.0, "factor", 12)
         term_a.append([piece([P, H], F32, f"term_a1_{jj}", 16 + jj) for jj in range(TILES_PER_HALF)])
         times_in_phase(1, factor, w1_c, w1_p, term_a[1])
-        held = piece([P, N], F32, "held", 13)
+        modes_first = pick_modes(piece([P, P], U32, "modes_first_codes", 14), piece([P, P], U8, "modes_first_plane", 15), 0, P)
+        held = piece([P, N], F32, "held", 12)
         turn(1, 0, N, turn_banks, held[:])
         scatter(1, 0, N, held[:])
         for t in range(2):
@@ -257,7 +259,7 @@ def tile_list_track_phase_board_kernel(
         for t in range(2):
             scatter(t, N, N, cross[t][:, N:])
 
-        board = [woven(f"board{c}") for c in range(CHUNKS)]
+        board = [woven(f"board{c}", c) for c in range(CHUNKS)]
 
         def round_rows(engine_copy, pair, t, c):
             engine_copy(pair[:, t % 2, :], page[t][:, N * c : N * (c + 1)])
@@ -279,24 +281,32 @@ def tile_list_track_phase_board_kernel(
         for c in range(CHUNKS):
             round_rows(nc.scalar.copy, high[c], 2, c)
         scatter(3, 0, S, cross[3][:])
-        copies = (nc.vector.tensor_copy, nc.vector.tensor_copy, nc.scalar.copy, nc.scalar.copy)
-        for c in (0, 1):
-            round_rows(copies[c], high[c], 3, c)
-        for c in (0, 1):
-            weave_pair(copies[c], high[c], 1, c)
-        for c in (2, 3):
-            round_rows(copies[c], high[c], 3, c)
-            weave_pair(copies[c], high[c], 1, c)
-        board_q = [quantize(board[c], f"board{c}") for c in range(CHUNKS)]
-
+        board_q = [None] * CHUNKS
+        round_rows(nc.vector.tensor_copy, high[0], 3, 0)
+        round_rows(nc.vector.tensor_copy, high[1], 3, 1)
+        round_rows(nc.scalar.copy, high[2], 3, 2)
+        weave_pair(nc.scalar.copy, high[2], 1, 2)
+        round_rows(nc.scalar.copy, high[3], 3, 3)
+        weave_pair(nc.scalar.copy, high[3], 1, 3)
+        weave_pair(nc.vector.tensor_copy, high[0], 1, 0)
+        weave_pair(nc.vector.tensor_copy, high[1], 1, 1)
+        board_q[0] = quantize(board[0], "board0")
+        board_q[1] = quantize(board[1], "board1")
+        board_q[2] = quantize(board[2], "board2")
+        board_q[3] = quantize(board[3], "board3")
+        modes_rest = pick_modes(
+            piece([P, S2 - P], U32, "modes_rest_codes", CHUNKS - 1),
+            ring.tile([P, S2 - P], U8, name="modes_rest_plane", tag=f"woven{CHUNKS - 1}", align_bytes=64), P, S2 - P,
+        )
         match = []
         for n in range(S2 // P):
-            rows = slice(P * n, P * (n + 1))
+            codes, plane = modes_first if n == 0 else modes_rest
+            cols = slice(0, P) if n == 0 else slice(P * (n - 1), P * n)
             match.append(slab([P, T2], f"match{n}"))
             for c in range(CHUNKS):
                 bank = match_banks[c]
                 nc.tensor.matmul_mx(
-                    out=bank[:], lhsT=v2_codes[:, rows].bitcast(FP8X4), lhsT_scale=v2_plane[:, rows],
+                    out=bank[:], lhsT=codes[:, cols].bitcast(FP8X4), lhsT_scale=plane[:, cols],
                     rhs=board_q[c][0], rhs_scale=board_q[c][1], start=True, stop=True,
                 )
                 nc.scalar.copy(match[n][:, N * c : N * (c + 1)], bank[:])
@@ -305,14 +315,13 @@ def tile_list_track_phase_board_kernel(
         for n in range(S2 // P):
             rows = slice(P * n, P * (n + 1))
             offset = phase[:, n : n + 1]
-            widths = (N, N // 2, N // 2) if n == S2 // P - 1 else (N, N)
             first = 0
-            for k, width in enumerate(widths):
-                picked = piece([P, width], F32, f"picked{n}_{k}", done % 4)
+            for k, width in enumerate((N, N // 2, N // 2) if n == S2 // P - 1 else (N, N)):
+                picked = piece([P, width], F32, f"picked{n}_{k}", 16 + done % 4)
                 turns = piece([P, width], I32, f"turns{n}_{k}", 4 + done % 4)
-                angle = piece([P, width], F32, f"angle{n}_{k}", 8 + done)
+                angle = piece([P, width], F32, f"angle{n}_{k}", 8 + done % 8)
                 nc.vector.tensor_copy(picked[:], match[n][:].indirect(entries(list4, first, width)))
-                nc.vector.tensor_scalar(turns[:], picked[:], offset, 1.0 / TWO_PI, ALU.add, ALU.mult)
+                nc.vector.tensor_scalar(turns[:], picked[:], phase[:, n : n + 1], 1.0 / TWO_PI, ALU.add, ALU.mult)
                 nc.vector.scalar_tensor_tensor(angle[:], turns[:], -TWO_PI, picked[:], ALU.mult, ALU.add)
                 nc.scalar.activation(angle[:], angle[:], ACT.Abs, bias=offset)
                 nc.scalar.activation(angle[:], angle[:], ACT.Sin, bias=math.pi / 2, scale=-1.0)

@@ -27,7 +27,6 @@ TILES_PER_HALF = N // P
 CHUNKS = T2 // N
 PER_COL = 16
 BANKS = 8
-PRODUCT_BANKS = 6
 TWO_PI = 2.0 * math.pi
 
 
@@ -53,12 +52,11 @@ def tile_list_track_phase_board_kernel(
         def piece(shape, dtype, name, place):
             return ring.tile(shape, dtype, name=name, tag=f"place{place}", align_bytes=64)
 
-        banks = [psum.tile([P, N], F32, name=f"bank{b}") for b in range(BANKS)]
-        product_banks, turn_banks, match_banks = banks[:PRODUCT_BANKS], banks[PRODUCT_BANKS:], banks[:]
+        def wide(dtype, name, place):
+            return ring.tile([P, S], dtype, name=name, tag=f"wide{place}", align_bytes=64)
 
-        def next_bank(rotation):
-            rotation.append(rotation.pop(0))
-            return rotation[-1]
+        banks = [psum.tile([P, N], F32, name=f"bank{b}") for b in range(BANKS)]
+        lower, upper = banks[: BANKS // 2], banks[BANKS // 2 :]
 
         def load_list(source, name):
             tile = keep.tile(list(source.shape), U16, name=name)
@@ -103,7 +101,7 @@ def tile_list_track_phase_board_kernel(
         page_rows = page0.rearrange("(p t) c -> t p c", t=PACK)
         wgs_rows = wgs.rearrange("(m t) j -> t m j", t=PACK)
         page = [kept([P, T2], F32, f"page{t}") for t in range(PACK)]
-        weight = [kept([P, S], F32, f"weight{t}") for t in range(PACK)]
+        weight = [wide(F32, f"weight{t}", PACK + t) for t in range(PACK)]
 
         def load_board(t):
             nc.sync.dma_start(page[t][:], page_rows[t])
@@ -111,37 +109,33 @@ def tile_list_track_phase_board_kernel(
                 nc.sync.dma_start(weight[t][32 * q : 32 * q + 32, :], wgs_rows[t])
 
         list1 = load_list(offs, "list1")
+        list3 = load_list(offs3, "list3")
         for q in range(4):
             nc.sync.dma_start(
                 tab_plane[32 * q : 32 * q + 4 * PASSES, :].bitcast(I32),
                 tab_scales[:, 4 * q : 4 * q + 4, :].bitcast(I32),
             )
-        tab = [load_words(tab_words[0], T, "tab0")]
-        w4_raw = [load_raw(w4, 0, "w4_raw0")]
-        tab.append(load_words(tab_words[1], T, "tab1"))
+        tab = [load_words(tab_words[a], T, f"tab{a}") for a in range(PASSES)]
         w3_codes = kept([P, PASSES, H], U32, "w3_codes")
         nc.sync.dma_start(w3_codes[:].bitcast(I32), w3_words.rearrange("a p n i -> p a (n i)").bitcast(I32))
         load_weight_scales(w3_plane, w3_scales, nc.sync)
         v_plane = kept([P, S], U8, "v_plane")
         nc.vector.tensor_copy(v_plane[:], tab_plane[:].indirect(list1[:]))
-        nc.sync.dma_start(v_plane1[0:112, :].bitcast(I32), v_plane[4:116, :].bitcast(I32))
-        w4_raw.append(load_raw(w4, 1, "w4_raw1"))
+        w4_raw = [load_raw(w4, a, f"w4_raw{a}") for a in range(PASSES)]
         w2_codes = kept([P, PASSES, 2 * H], U8, "w2_codes")
         nc.sync.dma_start(w2_codes[:].bitcast(I32), w2_words.rearrange("a p n -> p a n").bitcast(I32))
         load_weight_scales(w2_plane, w2_scales, nc.sync)
-        w1_raw = [load_raw(w1, 0, "w1_raw0")]
-        w1_raw.append(load_raw(w1, 1, "w1_raw1"))
-        list3 = load_list(offs3, "list3")
+        nc.sync.dma_start(v_plane1[0:112, :].bitcast(I32), v_plane[4:116, :].bitcast(I32))
+        w1_raw = [load_raw(w1, a, f"w1_raw{a}") for a in range(PASSES)]
         load_board(0)
-        load_board(1)
         list2 = load_list(offs2, "list2")
         tab2 = load_words(tab2_words[0], T3, "tab2")
         for q in range(4):
             nc.sync.dma_start(
                 tab2_plane[32 * q : 32 * q + 4, :].bitcast(I32), tab2_scales[0, 4 * q : 4 * q + 4, :].bitcast(I32)
             )
-        load_board(2)
-        load_board(3)
+        for t in range(1, PACK):
+            load_board(t)
         list4 = load_list(offs4, "list4")
         phase = kept([P, S2 // P], F32, "phase")
         with nc.allow_non_contiguous_dma(reason="one phase offset a partition"):
@@ -153,8 +147,7 @@ def tile_list_track_phase_board_kernel(
                 v_codes[a][h] = kept([P, N], U32, f"v_codes{a}_{h}")
                 nc.vector.tensor_copy(v_codes[a][h][:], tab[a][:].bitcast(U32).indirect(entries(list1, N * h, N)))
 
-        def product(h, jj, codes, planes, fp4, name):
-            bank = next_bank(product_banks)
+        def product(bank, h, jj, codes, planes, fp4):
             cols = slice(P * jj, P * (jj + 1))
             for a in range(PASSES):
                 if fp4 and a == 1:
@@ -167,10 +160,10 @@ def tile_list_track_phase_board_kernel(
                 )
             return bank
 
-        def quadrature(h, codes, planes, fp4, sign, name, place):
+        def quadrature(into, h, codes, planes, fp4, sign, name, place):
             tiles = []
             for jj in range(TILES_PER_HALF):
-                bank = product(h, jj, codes, planes, fp4, f"{name}_bank{h}_{jj}")
+                bank = product(into[jj], h, jj, codes, planes, fp4)
                 tile = piece([P, H], F32, f"{name}{h}_{jj}", place + jj)
                 nc.scalar.activation(
                     tile[:].rearrange("p (t g e) -> p g t e", t=PACK, e=PACK),
@@ -179,19 +172,21 @@ def tile_list_track_phase_board_kernel(
                 tiles.append(tile)
             return tiles
 
-        def times_in_phase(h, tiles, codes, planes, results):
-            for jj in range(TILES_PER_HALF):
-                bank = product(h, jj, codes, planes, False, "")
-                nc.vector.tensor_tensor(results[jj][:], bank[:], tiles[jj][:], ALU.mult)
+        def in_phase(into, h, codes, planes):
+            return [product(into[jj], h, jj, codes, planes, False) for jj in range(TILES_PER_HALF)]
 
-        def weave_weight(raw, name, vector_share, place):
+        def times(held, tiles, results=None):
+            for bank, tile, result in zip(held, tiles, results or tiles):
+                nc.vector.tensor_tensor(result[:], bank[:], tile[:], ALU.mult)
+
+        def gpsimd_copy(dst, src):
+            nc.gpsimd.tensor_scalar(dst, src, 1.0, 0.0, ALU.mult, ALU.add)
+
+        def weave_weight(raw, name, engine_copy, place):
             tile = woven(name, place)
             dst = tile[:].rearrange("p (t m i) -> p m t i", t=PACK, i=PACK)
             src = raw[:].rearrange("p i (m t) -> p m t i", t=PACK)
-            if vector_share > 0:
-                nc.vector.tensor_copy(dst[:, :vector_share], src[:, :vector_share])
-            if vector_share < P:
-                nc.scalar.copy(dst[:, vector_share:], src[:, vector_share:])
+            engine_copy(dst, src)
             return tile
 
         def quantize(tile, name):
@@ -214,10 +209,9 @@ def tile_list_track_phase_board_kernel(
             nc.vector.tensor_copy(plane[:], tab2_plane[:].indirect(entries(list2, first, count)))
             return codes, plane
 
-        cross = [kept([P, S], F32, f"cross{t}") for t in range(PACK)]
+        cross = [wide(F32, f"cross{t}", t) for t in range(PACK)]
 
-        def turn(t, first, count, rotation, result):
-            bank = next_bank(rotation)
+        def turn(bank, t, first, count, result):
             for k in reversed(range(count // P)):
                 h, jj = divmod(first // P + k, TILES_PER_HALF)
                 for n, term in enumerate((term_a, term_b)):
@@ -232,34 +226,30 @@ def tile_list_track_phase_board_kernel(
                 page[t][:].indirect(entries(list3, first, count)), values, weight[t][:, first : first + count], ALU.mult
             )
 
-        w4_c, w4_p = quantize_weight(w4_raw, (0, P), "w4", 0)
-        term_b = [quadrature(0, w3_c, w3_p, False, -1.0, "term_b", 0)]
-        term_a = [quadrature(0, w2_c, w2_p, True, 1.0, "term_a", 8)]
-        times_in_phase(0, term_b[0], w4_c, w4_p, term_b[0])
-        term_b.append(quadrature(1, w3_c, w3_p, False, -1.0, "term_b", 4))
-        w1_c, w1_p = quantize_weight(w1_raw, (P, 0), "w1", 2)
-        times_in_phase(0, term_a[0], w1_c, w1_p, term_a[0])
-        for first in (0, N // 2):
-            turn(0, first, N // 2, turn_banks, cross[0][:, first : first + N // 2])
-        for first in (0, N // 2):
-            scatter(0, first, N // 2, cross[0][:, first : first + N // 2])
-        times_in_phase(1, term_b[1], w4_c, w4_p, term_b[1])
-        factor = quadrature(1, w2_c, w2_p, True, 1.0, "factor", 12)
+        term_b = [quadrature((lower, upper)[h], h, w3_c, w3_p, False, -1.0, "term_b", 4 * h) for h in range(HALVES)]
+        w4_c, w4_p = quantize_weight(w4_raw, (gpsimd_copy, nc.vector.tensor_copy), "w4", 0)
+        times(in_phase(lower, 0, w4_c, w4_p), term_b[0])
+        w1_c, w1_p = quantize_weight(w1_raw, (nc.scalar.copy, nc.vector.tensor_copy), "w1", 2)
+        term_a = [quadrature(upper, 0, w2_c, w2_p, True, 1.0, "term_a", 8)]
+        waiting = in_phase(lower, 1, w4_c, w4_p)
+        times(in_phase(upper, 0, w1_c, w1_p), term_a[0])
+        times(waiting, term_b[1])
+        turn(upper[0], 0, 0, N, cross[0][:, :N])
+        scatter(0, 0, N, cross[0][:, :N])
+        factor = quadrature(upper[1:] + lower[:1], 1, w2_c, w2_p, True, 1.0, "factor", 12)
         term_a.append([piece([P, H], F32, f"term_a1_{jj}", 16 + jj) for jj in range(TILES_PER_HALF)])
-        times_in_phase(1, factor, w1_c, w1_p, term_a[1])
+        times(in_phase(lower[1:] + upper[:1], 1, w1_c, w1_p), factor, term_a[1])
+        held = piece([P, N], F32, "held", 13)
+        turn(upper[1], 1, 0, N, held[:])
+        later = [(0, N), (1, N)] + [(t, first) for t in range(2, PACK) for first in (0, N)]
+        for (t, first), bank in zip(later, upper[2:] + lower):
+            turn(bank, t, first, N, cross[t][:, first : first + N])
         modes_first = pick_modes(piece([P, P], U32, "modes_first_codes", 14), piece([P, P], U8, "modes_first_plane", 15), 0, P)
-        held = piece([P, N], F32, "held", 12)
-        turn(1, 0, N, turn_banks, held[:])
-        scatter(1, 0, N, held[:])
-        for t in range(2):
-            turn(t, N, N, banks, cross[t][:, N:])
-        for t in range(2, PACK):
-            for first in (0, N):
-                turn(t, first, N, banks, cross[t][:, first : first + N])
-        for t in range(2):
-            scatter(t, N, N, cross[t][:, N:])
 
-        board = [woven(f"board{c}", c) for c in range(CHUNKS)]
+        board = [piece([P, PACK * N], BF16, f"board{c}", 4 + c) for c in range(CHUNKS)]
+
+        def round_into_slot(t, c):
+            nc.scalar.copy(board[c][:].rearrange("p (c i) -> p c i", i=PACK)[:, :, t], page[t][:, N * c : N * (c + 1)])
 
         def round_rows(engine_copy, pair, t, c):
             engine_copy(pair[:, t % 2, :], page[t][:, N * c : N * (c + 1)])
@@ -270,61 +260,90 @@ def tile_list_track_phase_board_kernel(
                 pair[:].rearrange("p i c -> p c i"),
             )
 
-        low = [piece([P, 2, N], BF16, f"low{c}", 4 + c) for c in range(CHUNKS)]
-        high = [piece([P, 2, N], BF16, f"high{c}", c) for c in range(CHUNKS)]
-        for t in range(2):
-            for c in range(CHUNKS):
-                round_rows(nc.scalar.copy, low[c], t, c)
+        def weave_three(planes, c):
+            nc.scalar.copy(
+                board[c][:].rearrange("p (g e i) -> p g i e", i=PACK, e=PACK)[:, :, 0:3, :],
+                planes[:].rearrange("p i (g e) -> p g i e", e=PACK),
+            )
+
+        def round_plane(planes, t, c):
+            nc.scalar.copy(planes[:, t, :], page[t][:, N * c : N * (c + 1)])
+
+        low = [piece([P, 2, N], BF16, f"low{c}", 8 + c) for c in range(2)]
+        low = low + [piece([P, 3, N], BF16, f"low{c}", 8 + c) for c in range(2, CHUNKS)]
+        high = [piece([P, 2, N], BF16, f"high{c}", c) for c in range(2)]
+        scatter(1, 0, N, held[:])
+        scatter(0, N, N, cross[0][:, N:])
         for c in range(CHUNKS):
+            round_plane(low[c], 0, c)
+        scatter(1, N, N, cross[1][:, N:])
+        for c in range(CHUNKS):
+            round_plane(low[c], 1, c)
+        for c in range(2):
             weave_pair(nc.scalar.copy, low[c], 0, c)
         scatter(2, 0, S, cross[2][:])
-        for c in range(CHUNKS):
+        for c in range(2):
             round_rows(nc.scalar.copy, high[c], 2, c)
+        for c in range(2, CHUNKS):
+            round_plane(low[c], 2, c)
+        for c in range(2, CHUNKS):
+            weave_three(low[c], c)
         scatter(3, 0, S, cross[3][:])
         board_q = [None] * CHUNKS
         round_rows(nc.vector.tensor_copy, high[0], 3, 0)
         round_rows(nc.vector.tensor_copy, high[1], 3, 1)
-        round_rows(nc.scalar.copy, high[2], 3, 2)
-        weave_pair(nc.scalar.copy, high[2], 1, 2)
-        round_rows(nc.scalar.copy, high[3], 3, 3)
-        weave_pair(nc.scalar.copy, high[3], 1, 3)
+        round_into_slot(3, 2)
+        round_into_slot(3, 3)
         weave_pair(nc.vector.tensor_copy, high[0], 1, 0)
         weave_pair(nc.vector.tensor_copy, high[1], 1, 1)
         board_q[0] = quantize(board[0], "board0")
         board_q[1] = quantize(board[1], "board1")
         board_q[2] = quantize(board[2], "board2")
         board_q[3] = quantize(board[3], "board3")
+        modes_second = pick_modes(
+            piece([P, P], U32, "modes_second_codes", 7),
+            piece([P, P], U8, "modes_second_plane", 6), P, P,
+        )
         modes_rest = pick_modes(
-            piece([P, S2 - P], U32, "modes_rest_codes", CHUNKS - 1),
-            ring.tile([P, S2 - P], U8, name="modes_rest_plane", tag=f"woven{CHUNKS - 1}", align_bytes=64), P, S2 - P,
+            piece([P, 2 * P], U32, "modes_rest_codes", 14),
+            piece([P, 2 * P], U8, "modes_rest_plane", 15), 2 * P, 2 * P,
         )
         match = []
         for n in range(S2 // P):
-            codes, plane = modes_first if n == 0 else modes_rest
-            cols = slice(0, P) if n == 0 else slice(P * (n - 1), P * n)
+            codes, plane = (modes_first, modes_second, modes_rest, modes_rest)[n]
+            cols = slice(P * max(n - 2, 0), P * max(n - 1, 1))
             match.append(slab([P, T2], f"match{n}"))
             for c in range(CHUNKS):
-                bank = match_banks[c]
+                bank = banks[(CHUNKS * n + c) % BANKS]
                 nc.tensor.matmul_mx(
                     out=bank[:], lhsT=codes[:, cols].bitcast(FP8X4), lhsT_scale=plane[:, cols],
                     rhs=board_q[c][0], rhs_scale=board_q[c][1], start=True, stop=True,
                 )
                 nc.scalar.copy(match[n][:, N * c : N * (c + 1)], bank[:])
 
-        done = 0
-        for n in range(S2 // P):
-            rows = slice(P * n, P * (n + 1))
+        def pick(n, first, width, picked):
+            nc.vector.tensor_copy(picked[:, first : first + width], match[n][:].indirect(entries(list4, first, width)))
+
+        def cosine(n, cuts, picked, turns, angle):
             offset = phase[:, n : n + 1]
-            first = 0
-            for k, width in enumerate((N, N // 2, N // 2) if n == S2 // P - 1 else (N, N)):
-                picked = piece([P, width], F32, f"picked{n}_{k}", 16 + done % 4)
-                turns = piece([P, width], I32, f"turns{n}_{k}", 4 + done % 4)
-                angle = piece([P, width], F32, f"angle{n}_{k}", 8 + done % 8)
-                nc.vector.tensor_copy(picked[:], match[n][:].indirect(entries(list4, first, width)))
-                nc.vector.tensor_scalar(turns[:], picked[:], phase[:, n : n + 1], 1.0 / TWO_PI, ALU.add, ALU.mult)
-                nc.vector.scalar_tensor_tensor(angle[:], turns[:], -TWO_PI, picked[:], ALU.mult, ALU.add)
-                nc.scalar.activation(angle[:], angle[:], ACT.Abs, bias=offset)
-                nc.scalar.activation(angle[:], angle[:], ACT.Sin, bias=math.pi / 2, scale=-1.0)
-                nc.sync.dma_start(out[rows, first : first + width], angle[:])
-                first = first + width
-                done = done + 1
+            for cols in cuts:
+                nc.vector.tensor_scalar(turns[:, cols], picked[:, cols], offset, 1.0 / TWO_PI, ALU.add, ALU.mult)
+            for cols in cuts:
+                nc.vector.scalar_tensor_tensor(angle[:, cols], turns[:, cols], -TWO_PI, picked[:, cols], ALU.mult, ALU.add)
+            folded = []
+            for k, cols in enumerate(cuts):
+                folded.append(piece([P, cols.stop - cols.start], F32, f"folded{n}_{cols.start}", 16 + k))
+                nc.scalar.activation(folded[k][:], angle[:, cols], ACT.Abs, bias=offset)
+            for k, cols in enumerate(cuts):
+                nc.scalar.activation(angle[:, cols], folded[k][:], ACT.Sin, bias=math.pi / 2, scale=-1.0)
+                nc.sync.dma_start(out[P * n : P * (n + 1), cols], angle[:, cols])
+
+        def halves(first, width):
+            return [slice(first, first + width // 2), slice(first + width // 2, first + width)]
+
+        last = S2 // P - 1
+        for n in range(S2 // P):
+            picked, turns, angle = wide(F32, f"picked{n}", n % 2), wide(I32, f"turns{n}", 2 + n % 2), wide(F32, f"angle{n}", PACK + n)
+            for first, width in ((0, PICK),) if n < last else ((0, N), (N, N)):
+                pick(n, first, width, picked)
+                cosine(n, halves(first, width), picked, turns, angle)

@@ -115,18 +115,19 @@ def tile_list_track_phase_board_kernel(
                 tab_plane[32 * q : 32 * q + 4 * PASSES, :].bitcast(I32),
                 tab_scales[:, 4 * q : 4 * q + 4, :].bitcast(I32),
             )
+        w4_raw = [load_raw(w4, 0, "w4_raw0")]
         tab = [load_words(tab_words[a], T, f"tab{a}") for a in range(PASSES)]
         w3_codes = kept([P, PASSES, H], U32, "w3_codes")
         nc.sync.dma_start(w3_codes[:].bitcast(I32), w3_words.rearrange("a p n i -> p a (n i)").bitcast(I32))
         load_weight_scales(w3_plane, w3_scales, nc.sync)
-        v_plane = kept([P, S], U8, "v_plane")
-        nc.vector.tensor_copy(v_plane[:], tab_plane[:].indirect(list1[:]))
-        w4_raw = [load_raw(w4, a, f"w4_raw{a}") for a in range(PASSES)]
+        w4_raw.append(load_raw(w4, 1, "w4_raw1"))
+        w1_raw = [load_raw(w1, a, f"w1_raw{a}") for a in range(PASSES)]
         w2_codes = kept([P, PASSES, 2 * H], U8, "w2_codes")
         nc.sync.dma_start(w2_codes[:].bitcast(I32), w2_words.rearrange("a p n -> p a n").bitcast(I32))
         load_weight_scales(w2_plane, w2_scales, nc.sync)
+        v_plane = kept([P, S], U8, "v_plane")
+        nc.vector.tensor_copy(v_plane[:], tab_plane[:].indirect(list1[:]))
         nc.sync.dma_start(v_plane1[0:112, :].bitcast(I32), v_plane[4:116, :].bitcast(I32))
-        w1_raw = [load_raw(w1, a, f"w1_raw{a}") for a in range(PASSES)]
         load_board(0)
         list2 = load_list(offs2, "list2")
         tab2 = load_words(tab2_words[0], T3, "tab2")
@@ -141,11 +142,10 @@ def tile_list_track_phase_board_kernel(
         with nc.allow_non_contiguous_dma(reason="one phase offset a partition"):
             nc.sync.dma_start(phase[:], mode.rearrange("(n p) -> p n", p=P))
 
-        v_codes = [[None] * HALVES for a in range(PASSES)]
-        for h in range(HALVES):
-            for a in range(PASSES):
-                v_codes[a][h] = kept([P, N], U32, f"v_codes{a}_{h}")
-                nc.vector.tensor_copy(v_codes[a][h][:], tab[a][:].bitcast(U32).indirect(entries(list1, N * h, N)))
+        v_codes = [[kept([P, N], U32, f"v_codes{a}_{h}") for h in range(HALVES)] for a in range(PASSES)]
+
+        def pick_tracks(a, h):
+            nc.vector.tensor_copy(v_codes[a][h][:], tab[a][:].bitcast(U32).indirect(entries(list1, N * h, N)))
 
         def product(bank, h, jj, codes, planes, fp4):
             cols = slice(P * jj, P * (jj + 1))
@@ -160,10 +160,10 @@ def tile_list_track_phase_board_kernel(
                 )
             return bank
 
-        def quadrature(into, h, codes, planes, fp4, sign, name, place):
+        def quadrature(into, h, codes, planes, fp4, sign, name, place, first=0):
             tiles = []
-            for jj in range(TILES_PER_HALF):
-                bank = product(into[jj], h, jj, codes, planes, fp4)
+            for jj, bank in enumerate(into, first):
+                product(bank, h, jj, codes, planes, fp4)
                 tile = piece([P, H], F32, f"{name}{h}_{jj}", place + jj)
                 nc.scalar.activation(
                     tile[:].rearrange("p (t g e) -> p g t e", t=PACK, e=PACK),
@@ -172,20 +172,20 @@ def tile_list_track_phase_board_kernel(
                 tiles.append(tile)
             return tiles
 
-        def in_phase(into, h, codes, planes):
-            return [product(into[jj], h, jj, codes, planes, False) for jj in range(TILES_PER_HALF)]
+        def in_phase(into, h, codes, planes, first=0):
+            return [product(bank, h, jj, codes, planes, False) for jj, bank in enumerate(into, first)]
 
         def times(held, tiles, results=None):
             for bank, tile, result in zip(held, tiles, results or tiles):
-                nc.vector.tensor_tensor(result[:], bank[:], tile[:], ALU.mult)
-
-        def gpsimd_copy(dst, src):
-            nc.gpsimd.tensor_scalar(dst, src, 1.0, 0.0, ALU.mult, ALU.add)
+                nc.vector.tensor_tensor(
+                    result[:].rearrange("p (t m) -> p t m", t=PACK), bank[:].rearrange("p (m t) -> p t m", t=PACK),
+                    tile[:].rearrange("p (t m) -> p t m", t=PACK), ALU.mult,
+                )
 
         def weave_weight(raw, name, engine_copy, place):
             tile = woven(name, place)
-            dst = tile[:].rearrange("p (t m i) -> p m t i", t=PACK, i=PACK)
-            src = raw[:].rearrange("p i (m t) -> p m t i", t=PACK)
+            dst = tile[:].rearrange("p (g e i) -> p g i e", e=PACK, i=PACK)
+            src = raw[:].rearrange("p i (g e) -> p g i e", e=PACK)
             engine_copy(dst, src)
             return tile
 
@@ -226,23 +226,36 @@ def tile_list_track_phase_board_kernel(
                 page[t][:].indirect(entries(list3, first, count)), values, weight[t][:, first : first + count], ALU.mult
             )
 
-        term_b = [quadrature((lower, upper)[h], h, w3_c, w3_p, False, -1.0, "term_b", 4 * h) for h in range(HALVES)]
-        w4_c, w4_p = quantize_weight(w4_raw, (gpsimd_copy, nc.vector.tensor_copy), "w4", 0)
+        w4_q = [quantize(weave_weight(w4_raw[0], "w4_woven0", nc.vector.tensor_copy, 0), "w4_0")]
+        for h in range(HALVES):
+            for a in range(PASSES):
+                pick_tracks(a, h)
+        w4_q.append(quantize(weave_weight(w4_raw[1], "w4_woven1", nc.vector.tensor_copy, 1), "w4_1"))
+        w4_c, w4_p = [x[0] for x in w4_q], [x[1] for x in w4_q]
+        term_b = [quadrature(upper, 0, w3_c, w3_p, False, -1.0, "term_b", 0)]
         times(in_phase(lower, 0, w4_c, w4_p), term_b[0])
+        term_b.append(quadrature(upper, 1, w3_c, w3_p, False, -1.0, "term_b", 4))
         w1_c, w1_p = quantize_weight(w1_raw, (nc.scalar.copy, nc.vector.tensor_copy), "w1", 2)
         term_a = [quadrature(upper, 0, w2_c, w2_p, True, 1.0, "term_a", 8)]
-        waiting = in_phase(lower, 1, w4_c, w4_p)
-        times(in_phase(upper, 0, w1_c, w1_p), term_a[0])
-        times(waiting, term_b[1])
-        turn(upper[0], 0, 0, N, cross[0][:, :N])
-        scatter(0, 0, N, cross[0][:, :N])
-        factor = quadrature(upper[1:] + lower[:1], 1, w2_c, w2_p, True, 1.0, "factor", 12)
+        times(in_phase(lower[:2], 1, w4_c, w4_p), term_b[1][:2])
+        waiting = in_phase(upper[:2], 1, w4_c, w4_p, 2)
+        first_a = [piece([P, H], F32, f"term_a0_result{jj}", 20 + jj) for jj in range(2)] + term_a[0][2:]
+        times(in_phase(lower[2:] + lower[:2], 0, w1_c, w1_p), term_a[0], first_a)
+        term_a[0] = first_a
+        for first, bank in zip((0, N // 2), (lower[2], lower[0])):
+            turn(bank, 0, first, N // 2, cross[0][:, first : first + N // 2])
+        late_b = [piece([P, H], F32, f"term_b1_result{jj}", 8 + jj) for jj in range(2)]
+        times(waiting, term_b[1][2:], late_b)
+        term_b[1] = term_b[1][:2] + late_b
+        for first in (0, N // 2):
+            scatter(0, first, N // 2, cross[0][:, first : first + N // 2])
+        factor = quadrature(upper[2:] + upper[:2], 1, w2_c, w2_p, True, 1.0, "factor", 12)
         term_a.append([piece([P, H], F32, f"term_a1_{jj}", 16 + jj) for jj in range(TILES_PER_HALF)])
-        times(in_phase(lower[1:] + upper[:1], 1, w1_c, w1_p), factor, term_a[1])
+        times(in_phase((lower[3], lower[1], lower[2], lower[0]), 1, w1_c, w1_p), factor, term_a[1])
         held = piece([P, N], F32, "held", 13)
-        turn(upper[1], 1, 0, N, held[:])
+        turn(upper[2], 1, 0, N, held[:])
         later = [(0, N), (1, N)] + [(t, first) for t in range(2, PACK) for first in (0, N)]
-        for (t, first), bank in zip(later, upper[2:] + lower):
+        for (t, first), bank in zip(later, (upper[3], upper[0], upper[1], lower[3], lower[1], lower[2])):
             turn(bank, t, first, N, cross[t][:, first : first + N])
         modes_first = pick_modes(piece([P, P], U32, "modes_first_codes", 14), piece([P, P], U8, "modes_first_plane", 15), 0, P)
 
@@ -269,8 +282,8 @@ def tile_list_track_phase_board_kernel(
         def round_plane(planes, t, c):
             nc.scalar.copy(planes[:, t, :], page[t][:, N * c : N * (c + 1)])
 
-        low = [piece([P, 2, N], BF16, f"low{c}", 8 + c) for c in range(2)]
-        low = low + [piece([P, 3, N], BF16, f"low{c}", 8 + c) for c in range(2, CHUNKS)]
+        low = [piece([P, 2, N], BF16, f"low{c}", 16 + c) for c in range(2)]
+        low = low + [piece([P, 3, N], BF16, f"low{c}", 16 + c) for c in range(2, CHUNKS)]
         high = [piece([P, 2, N], BF16, f"high{c}", c) for c in range(2)]
         scatter(1, 0, N, held[:])
         scatter(0, N, N, cross[0][:, N:])
@@ -282,10 +295,10 @@ def tile_list_track_phase_board_kernel(
         for c in range(2):
             weave_pair(nc.scalar.copy, low[c], 0, c)
         scatter(2, 0, S, cross[2][:])
-        for c in range(2):
-            round_rows(nc.scalar.copy, high[c], 2, c)
         for c in range(2, CHUNKS):
             round_plane(low[c], 2, c)
+        for c in range(2):
+            round_rows(nc.scalar.copy, high[c], 2, c)
         for c in range(2, CHUNKS):
             weave_three(low[c], c)
         scatter(3, 0, S, cross[3][:])
@@ -321,15 +334,17 @@ def tile_list_track_phase_board_kernel(
                 )
                 nc.scalar.copy(match[n][:, N * c : N * (c + 1)], bank[:])
 
-        def pick(n, first, width, picked):
-            nc.vector.tensor_copy(picked[:, first : first + width], match[n][:].indirect(entries(list4, first, width)))
+        def pick(n, cols, picked):
+            nc.vector.tensor_copy(picked[:, cols], match[n][:].indirect(entries(list4, cols.start, cols.stop - cols.start)))
 
-        def cosine(n, cuts, picked, turns, angle):
+        def count(n, cols, picked, turns):
+            nc.vector.tensor_scalar(turns[:, cols], picked[:, cols], phase[:, n : n + 1], 1.0 / TWO_PI, ALU.add, ALU.mult)
+
+        def reduce(cols, picked, turns, angle):
+            nc.vector.scalar_tensor_tensor(angle[:, cols], turns[:, cols], -TWO_PI, picked[:, cols], ALU.mult, ALU.add)
+
+        def cosine(n, cuts, angle):
             offset = phase[:, n : n + 1]
-            for cols in cuts:
-                nc.vector.tensor_scalar(turns[:, cols], picked[:, cols], offset, 1.0 / TWO_PI, ALU.add, ALU.mult)
-            for cols in cuts:
-                nc.vector.scalar_tensor_tensor(angle[:, cols], turns[:, cols], -TWO_PI, picked[:, cols], ALU.mult, ALU.add)
             folded = []
             for k, cols in enumerate(cuts):
                 folded.append(piece([P, cols.stop - cols.start], F32, f"folded{n}_{cols.start}", 16 + k))
@@ -345,5 +360,11 @@ def tile_list_track_phase_board_kernel(
         for n in range(S2 // P):
             picked, turns, angle = wide(F32, f"picked{n}", n % 2), wide(I32, f"turns{n}", 2 + n % 2), wide(F32, f"angle{n}", PACK + n)
             for first, width in ((0, PICK),) if n < last else ((0, N), (N, N)):
-                pick(n, first, width, picked)
-                cosine(n, halves(first, width), picked, turns, angle)
+                cuts = halves(first, width)
+                for cols in cuts:
+                    pick(n, cols, picked)
+                for cols in cuts:
+                    count(n, cols, picked, turns)
+                for cols in cuts:
+                    reduce(cols, picked, turns, angle)
+                cosine(n, cuts, angle)

@@ -127,7 +127,7 @@ def tile_list_track_phase_board_kernel(
         load_weight_scales(w2_plane, w2_scales, nc.sync)
         v_plane = kept([P, S], U8, "v_plane")
         nc.vector.tensor_copy(v_plane[:], tab_plane[:].indirect(list1[:]))
-        nc.sync.dma_start(v_plane1[0:112, :].bitcast(I32), v_plane[4:116, :].bitcast(I32))
+        nc.sync.dma_start(v_plane1[0:100, :].bitcast(I32), v_plane[4:104, :].bitcast(I32))
         load_board(0)
         list2 = load_list(offs2, "list2")
         tab2 = load_words(tab2_words[0], T3, "tab2")
@@ -238,24 +238,26 @@ def tile_list_track_phase_board_kernel(
         w1_c, w1_p = quantize_weight(w1_raw, (nc.scalar.copy, nc.vector.tensor_copy), "w1", 2)
         term_a = [quadrature(upper, 0, w2_c, w2_p, True, 1.0, "term_a", 8)]
         times(in_phase(lower[:2], 1, w4_c, w4_p), term_b[1][:2])
-        waiting = in_phase(upper[:2], 1, w4_c, w4_p, 2)
-        first_a = [piece([P, H], F32, f"term_a0_result{jj}", 20 + jj) for jj in range(2)] + term_a[0][2:]
+        waiting = in_phase(upper[:1], 1, w4_c, w4_p, 2)
+        first_a = [piece([P, H], F32, "term_a0_result", 20)] + term_a[0][1:]
         times(in_phase(lower[2:] + lower[:2], 0, w1_c, w1_p), term_a[0], first_a)
         term_a[0] = first_a
-        for first, bank in zip((0, N // 2), (lower[2], lower[0])):
-            turn(bank, 0, first, N // 2, cross[0][:, first : first + N // 2])
-        late_b = [piece([P, H], F32, f"term_b1_result{jj}", 8 + jj) for jj in range(2)]
-        times(waiting, term_b[1][2:], late_b)
-        term_b[1] = term_b[1][:2] + late_b
-        for first in (0, N // 2):
-            scatter(0, first, N // 2, cross[0][:, first : first + N // 2])
-        factor = quadrature(upper[2:] + upper[:2], 1, w2_c, w2_p, True, 1.0, "factor", 12)
+        for t, bank in enumerate((lower[2], upper[1])):
+            turn(bank, t, 0, N // 2, cross[t][:, : N // 2])
+        late_b = [piece([P, H], F32, "term_b1_result", 8)]
+        times(waiting, term_b[1][2:3], late_b)
+        term_b[1] = term_b[1][:2] + late_b + term_b[1][3:]
+        for t in range(2):
+            scatter(t, 0, N // 2, cross[t][:, : N // 2])
+        times(in_phase(lower[3:], 1, w4_c, w4_p, 3), term_b[1][3:])
+        factor = quadrature((upper[2], upper[3], upper[0], lower[2]), 1, w2_c, w2_p, True, 1.0, "factor", 12)
         term_a.append([piece([P, H], F32, f"term_a1_{jj}", 16 + jj) for jj in range(TILES_PER_HALF)])
-        times(in_phase((lower[3], lower[1], lower[2], lower[0]), 1, w1_c, w1_p), factor, term_a[1])
-        held = piece([P, N], F32, "held", 13)
-        turn(upper[2], 1, 0, N, held[:])
+        times(in_phase((lower[0], lower[1], upper[1], lower[3]), 1, w1_c, w1_p), factor, term_a[1])
+        held = [piece([P, N // 2], F32, f"held{t}", 12 + t) for t in range(2)]
+        for t in range(2):
+            turn(upper[2 + t], t, N // 2, N // 2, held[t][:])
         later = [(0, N), (1, N)] + [(t, first) for t in range(2, PACK) for first in (0, N)]
-        for (t, first), bank in zip(later, (upper[3], upper[0], upper[1], lower[3], lower[1], lower[2])):
+        for (t, first), bank in zip(later, (upper[0], lower[2], lower[0], lower[1], upper[1], lower[3])):
             turn(bank, t, first, N, cross[t][:, first : first + N])
         modes_first = pick_modes(piece([P, P], U32, "modes_first_codes", 14), piece([P, P], U8, "modes_first_plane", 15), 0, P)
 
@@ -285,7 +287,8 @@ def tile_list_track_phase_board_kernel(
         low = [piece([P, 2, N], BF16, f"low{c}", 16 + c) for c in range(2)]
         low = low + [piece([P, 3, N], BF16, f"low{c}", 16 + c) for c in range(2, CHUNKS)]
         high = [piece([P, 2, N], BF16, f"high{c}", c) for c in range(2)]
-        scatter(1, 0, N, held[:])
+        for t in range(2):
+            scatter(t, N // 2, N // 2, held[t][:])
         scatter(0, N, N, cross[0][:, N:])
         for c in range(CHUNKS):
             round_plane(low[c], 0, c)

@@ -38,6 +38,7 @@ def tile_list_track_phase_board_kernel(
     with ExitStack() as ctx:
         keep = ctx.enter_context(tc.tile_pool(name="keep", bufs=1))
         ring = ctx.enter_context(tc.tile_pool(name="ring", bufs=1))
+        shared = ctx.enter_context(tc.tile_pool(name="shared", bufs=1))
         psum = ctx.enter_context(tc.psum_pool(name="psum", bufs=1))
 
         def kept(shape, dtype, name):
@@ -85,8 +86,6 @@ def tile_list_track_phase_board_kernel(
         v_plane1 = zeroed_plane([P, S], "v_plane1", nc.vector)
         ident = kept([P, P], F32, "ident")
         make_identity(nc, ident[:])
-        warm = kept([P, 1], F32, "warm")
-        nc.scalar.activation(warm[:], ident[:, 0:1], ACT.Sin)
 
         def load_raw(w, a, name):
             raw = slab([P, PACK, H], name)
@@ -99,14 +98,17 @@ def tile_list_track_phase_board_kernel(
             return tile
 
         page_rows = page0.rearrange("(p t) c -> t p c", t=PACK)
-        wgs_rows = wgs.rearrange("(m t) j -> t m j", t=PACK)
+        wgs_rows = wgs.rearrange("(m t) j -> m t j", t=PACK)
         page = [kept([P, T2], F32, f"page{t}") for t in range(PACK)]
-        weight = [wide(F32, f"weight{t}", PACK + t) for t in range(PACK)]
 
-        def load_board(t):
+        def load_page(t):
             nc.sync.dma_start(page[t][:], page_rows[t])
+
+        def load_weights(tiles, cols, name, place):
+            tile = ring.tile([P, 2, cols.stop - cols.start], F32, name=name, tag=f"wide{place}", align_bytes=64)
             for q in (0, 2, 1, 3):
-                nc.sync.dma_start(weight[t][32 * q : 32 * q + 32, :], wgs_rows[t])
+                nc.sync.dma_start(tile[32 * q : 32 * (q + 1), :, :], wgs_rows[:, tiles, cols])
+            return tile
 
         list1 = load_list(offs, "list1")
         list3 = load_list(offs3, "list3")
@@ -128,21 +130,29 @@ def tile_list_track_phase_board_kernel(
         v_plane = kept([P, S], U8, "v_plane")
         nc.vector.tensor_copy(v_plane[:], tab_plane[:].indirect(list1[:]))
         nc.sync.dma_start(v_plane1[0:100, :].bitcast(I32), v_plane[4:104, :].bitcast(I32))
-        load_board(0)
+        load_page(0)
+        weight_first = load_weights(slice(0, 2), slice(0, N), "weight_first", PACK)
+        load_page(1)
         list2 = load_list(offs2, "list2")
         tab2 = load_words(tab2_words[0], T3, "tab2")
         for q in range(4):
             nc.sync.dma_start(
                 tab2_plane[32 * q : 32 * q + 4, :].bitcast(I32), tab2_scales[0, 4 * q : 4 * q + 4, :].bitcast(I32)
             )
-        for t in range(1, PACK):
-            load_board(t)
+        weight_second = load_weights(slice(0, 2), slice(N, S), "weight_second", PACK + 1)
+        load_page(2)
+        weight_rest = load_weights(slice(2, PACK), slice(0, S), "weight_rest", PACK + 2)
+        load_page(3)
         list4 = load_list(offs4, "list4")
         phase = kept([P, S2 // P], F32, "phase")
         with nc.allow_non_contiguous_dma(reason="one phase offset a partition"):
             nc.sync.dma_start(phase[:], mode.rearrange("(n p) -> p n", p=P))
 
-        v_codes = [[kept([P, N], U32, f"v_codes{a}_{h}") for h in range(HALVES)] for a in range(PASSES)]
+        first_woven = shared.tile([P, PACK * H], BF16, name="w4_woven0", offset=4096, align_bytes=64)
+        v_codes = [
+            [shared.tile([P, N], U32, name=f"v_codes0_{h}", offset=4096 + 2048 * h, align_bytes=64) for h in range(HALVES)],
+            [kept([P, N], U32, f"v_codes1_{h}") for h in range(HALVES)],
+        ]
 
         def pick_tracks(a, h):
             nc.vector.tensor_copy(v_codes[a][h][:], tab[a][:].bitcast(U32).indirect(entries(list1, N * h, N)))
@@ -182,8 +192,12 @@ def tile_list_track_phase_board_kernel(
                     tile[:].rearrange("p (t m) -> p t m", t=PACK), ALU.mult,
                 )
 
-        def weave_weight(raw, name, engine_copy, place):
-            tile = woven(name, place)
+        def shared_copy(dst, src):
+            cut = dst.shape[1] // 2
+            nc.vector.tensor_copy(dst[:, :cut], src[:, :cut])
+            nc.scalar.copy(dst[:, cut:], src[:, cut:])
+
+        def weave_weight(raw, tile, engine_copy):
             dst = tile[:].rearrange("p (g e i) -> p g i e", e=PACK, i=PACK)
             src = raw[:].rearrange("p i (g e) -> p g i e", e=PACK)
             engine_copy(dst, src)
@@ -201,7 +215,8 @@ def tile_list_track_phase_board_kernel(
         w3_p = [w3_plane[:, a, :] for a in range(PASSES)]
 
         def quantize_weight(raws, shares, name, place):
-            both = [quantize(weave_weight(raws[a], f"{name}_woven{a}", shares[a], place + a), f"{name}_{a}") for a in range(PASSES)]
+            tiles = [weave_weight(raws[a], woven(f"{name}_woven{a}", place + a), shares[a]) for a in range(PASSES)]
+            both = [quantize(tiles[a], f"{name}_{a}") for a in range(PASSES)]
             return [x[0] for x in both], [x[1] for x in both]
 
         def pick_modes(codes, plane, first, count):
@@ -222,18 +237,21 @@ def tile_list_track_phase_board_kernel(
             nc.scalar.copy(result, bank[:, :count])
 
         def scatter(t, first, count, values):
-            nc.vector.tensor_tensor(
-                page[t][:].indirect(entries(list3, first, count)), values, weight[t][:, first : first + count], ALU.mult
-            )
+            if t >= 2:
+                weight = weight_rest[:, t - 2, first : first + count]
+            else:
+                weight = (weight_first if first < N else weight_second)[:, t, first % N : first % N + count]
+            nc.vector.tensor_tensor(page[t][:].indirect(entries(list3, first, count)), values, weight, ALU.mult)
 
-        w4_q = [quantize(weave_weight(w4_raw[0], "w4_woven0", nc.vector.tensor_copy, 0), "w4_0")]
+        w4_q = [quantize(weave_weight(w4_raw[0], first_woven, shared_copy), "w4_0")]
         for h in range(HALVES):
             for a in range(PASSES):
                 pick_tracks(a, h)
-        w4_q.append(quantize(weave_weight(w4_raw[1], "w4_woven1", nc.vector.tensor_copy, 1), "w4_1"))
+        w4_q.append(quantize(weave_weight(w4_raw[1], woven("w4_woven1", 1), nc.vector.tensor_copy), "w4_1"))
         w4_c, w4_p = [x[0] for x in w4_q], [x[1] for x in w4_q]
         term_b = [quadrature(upper, 0, w3_c, w3_p, False, -1.0, "term_b", 0)]
         times(in_phase(lower, 0, w4_c, w4_p), term_b[0])
+        lower, upper = upper[3:] + lower[1:], upper[:3] + lower[:1]
         term_b.append(quadrature(upper, 1, w3_c, w3_p, False, -1.0, "term_b", 4))
         w1_c, w1_p = quantize_weight(w1_raw, (nc.scalar.copy, nc.vector.tensor_copy), "w1", 2)
         term_a = [quadrature(upper, 0, w2_c, w2_p, True, 1.0, "term_a", 8)]
@@ -247,9 +265,9 @@ def tile_list_track_phase_board_kernel(
         late_b = [piece([P, H], F32, "term_b1_result", 8)]
         times(waiting, term_b[1][2:3], late_b)
         term_b[1] = term_b[1][:2] + late_b + term_b[1][3:]
-        for t in range(2):
-            scatter(t, 0, N // 2, cross[t][:, : N // 2])
+        scatter(0, 0, N // 2, cross[0][:, : N // 2])
         times(in_phase(lower[3:], 1, w4_c, w4_p, 3), term_b[1][3:])
+        scatter(1, 0, N // 2, cross[1][:, : N // 2])
         factor = quadrature((upper[2], upper[3], upper[0], lower[2]), 1, w2_c, w2_p, True, 1.0, "factor", 12)
         term_a.append([piece([P, H], F32, f"term_a1_{jj}", 16 + jj) for jj in range(TILES_PER_HALF)])
         times(in_phase((lower[0], lower[1], upper[1], lower[3]), 1, w1_c, w1_p), factor, term_a[1])
@@ -261,7 +279,8 @@ def tile_list_track_phase_board_kernel(
             turn(bank, t, first, N, cross[t][:, first : first + N])
         modes_first = pick_modes(piece([P, P], U32, "modes_first_codes", 14), piece([P, P], U8, "modes_first_plane", 15), 0, P)
 
-        board = [piece([P, PACK * N], BF16, f"board{c}", 4 + c) for c in range(CHUNKS)]
+        board = [piece([P, PACK * N], BF16, f"board{c}", 4 + c) for c in range(CHUNKS - 1)]
+        board.append(shared.tile([P, PACK * N], BF16, name="board_last", offset=0, align_bytes=64))
 
         def round_into_slot(t, c):
             nc.scalar.copy(board[c][:].rearrange("p (c i) -> p c i", i=PACK)[:, :, t], page[t][:, N * c : N * (c + 1)])
@@ -317,12 +336,12 @@ def tile_list_track_phase_board_kernel(
         board_q[2] = quantize(board[2], "board2")
         board_q[3] = quantize(board[3], "board3")
         modes_second = pick_modes(
-            piece([P, P], U32, "modes_second_codes", 7),
-            piece([P, P], U8, "modes_second_plane", 6), P, P,
+            shared.tile([P, P], U32, name="modes_second_codes", offset=0, align_bytes=64),
+            shared.tile([P, P], U8, name="modes_second_plane", offset=512, align_bytes=64), P, P,
         )
         modes_rest = pick_modes(
-            piece([P, 2 * P], U32, "modes_rest_codes", 14),
-            piece([P, 2 * P], U8, "modes_rest_plane", 15), 2 * P, 2 * P,
+            shared.tile([P, 2 * P], U32, name="modes_rest_codes", offset=1024, align_bytes=64),
+            shared.tile([P, 2 * P], U8, name="modes_rest_plane", offset=2048, align_bytes=64), 2 * P, 2 * P,
         )
         match = []
         for n in range(S2 // P):

@@ -57,7 +57,9 @@ def tile_list_track_phase_board_kernel(
             return ring.tile([P, S], dtype, name=name, tag=f"wide{place}", align_bytes=64)
 
         banks = [psum.tile([P, N], F32, name=f"bank{b}") for b in range(BANKS)]
-        lower, upper = banks[: BANKS // 2], banks[BANKS // 2 :]
+
+        def at(*numbers):
+            return [banks[b] for b in numbers]
 
         def load_list(source, name):
             tile = keep.tile(list(source.shape), U16, name=name)
@@ -249,33 +251,32 @@ def tile_list_track_phase_board_kernel(
                 pick_tracks(a, h)
         w4_q.append(quantize(weave_weight(w4_raw[1], woven("w4_woven1", 1), nc.vector.tensor_copy), "w4_1"))
         w4_c, w4_p = [x[0] for x in w4_q], [x[1] for x in w4_q]
-        term_b = [quadrature(upper, 0, w3_c, w3_p, False, -1.0, "term_b", 0)]
-        times(in_phase(lower, 0, w4_c, w4_p), term_b[0])
-        lower, upper = upper[3:] + lower[1:], upper[:3] + lower[:1]
-        term_b.append(quadrature(upper, 1, w3_c, w3_p, False, -1.0, "term_b", 4))
+        term_b = [quadrature(at(4, 5, 6, 7), 0, w3_c, w3_p, False, -1.0, "term_b", 0)]
+        times(in_phase(at(0, 1, 2, 3), 0, w4_c, w4_p), term_b[0])
+        term_b.append(quadrature(at(4, 5, 6, 0), 1, w3_c, w3_p, False, -1.0, "term_b", 4))
         w1_c, w1_p = quantize_weight(w1_raw, (nc.scalar.copy, nc.vector.tensor_copy), "w1", 2)
-        term_a = [quadrature(upper, 0, w2_c, w2_p, True, 1.0, "term_a", 8)]
-        times(in_phase(lower[:2], 1, w4_c, w4_p), term_b[1][:2])
-        waiting = in_phase(upper[:1], 1, w4_c, w4_p, 2)
+        term_a = [quadrature(at(4, 5, 6, 0), 0, w2_c, w2_p, True, 1.0, "term_a", 8)]
+        times(in_phase(at(7, 1), 1, w4_c, w4_p), term_b[1][:2])
+        waiting = in_phase(at(2), 1, w4_c, w4_p, 2)
         first_a = [piece([P, H], F32, "term_a0_result", 20)] + term_a[0][1:]
-        times(in_phase(lower[2:] + lower[:2], 0, w1_c, w1_p), term_a[0], first_a)
+        times(in_phase(at(4, 5, 6, 0), 0, w1_c, w1_p), term_a[0], first_a)
         term_a[0] = first_a
-        for t, bank in enumerate((lower[2], upper[1])):
+        for t, bank in enumerate(at(3, 7)):
             turn(bank, t, 0, N // 2, cross[t][:, : N // 2])
         late_b = [piece([P, H], F32, "term_b1_result", 8)]
         times(waiting, term_b[1][2:3], late_b)
         term_b[1] = term_b[1][:2] + late_b + term_b[1][3:]
         scatter(0, 0, N // 2, cross[0][:, : N // 2])
-        times(in_phase(lower[3:], 1, w4_c, w4_p, 3), term_b[1][3:])
+        times(in_phase(at(5), 1, w4_c, w4_p, 3), term_b[1][3:])
         scatter(1, 0, N // 2, cross[1][:, : N // 2])
-        factor = quadrature((upper[2], upper[3], upper[0], lower[2]), 1, w2_c, w2_p, True, 1.0, "factor", 12)
+        factor = quadrature(at(1, 4, 2, 3), 1, w2_c, w2_p, True, 1.0, "factor", 12)
         term_a.append([piece([P, H], F32, f"term_a1_{jj}", 16 + jj) for jj in range(TILES_PER_HALF)])
-        times(in_phase((lower[0], lower[1], upper[1], lower[3]), 1, w1_c, w1_p), factor, term_a[1])
+        times(in_phase(at(6, 0, 7, 5), 1, w1_c, w1_p), factor, term_a[1])
         held = [piece([P, N // 2], F32, f"held{t}", 12 + t) for t in range(2)]
-        for t in range(2):
-            turn(upper[2 + t], t, N // 2, N // 2, held[t][:])
+        for t, bank in enumerate(at(1, 4)):
+            turn(bank, t, N // 2, N // 2, held[t][:])
         later = [(0, N), (1, N)] + [(t, first) for t in range(2, PACK) for first in (0, N)]
-        for (t, first), bank in zip(later, (upper[0], lower[2], lower[0], lower[1], upper[1], lower[3])):
+        for (t, first), bank in zip(later, at(2, 3, 6, 0, 7, 5)):
             turn(bank, t, first, N, cross[t][:, first : first + N])
         modes_first = pick_modes(piece([P, P], U32, "modes_first_codes", 14), piece([P, P], U8, "modes_first_plane", 15), 0, P)
 

@@ -82,8 +82,8 @@ def tile_list_track_phase_board_kernel(
             return tile[:, first // PER_COL : (first + count) // PER_COL]
 
         tab_plane = zeroed_plane([P, T], "tab_plane", nc.gpsimd)
-        w3_plane = zeroed_plane([P, PASSES, H], "w3_plane", nc.vector)
         w2_plane = zeroed_plane([P, PASSES, H], "w2_plane", nc.vector)
+        w3_plane = zeroed_plane([P, PASSES, H], "w3_plane", nc.vector)
         tab2_plane = zeroed_plane([P, T3], "tab2_plane", nc.vector)
         v_plane1 = zeroed_plane([P, S], "v_plane1", nc.vector)
         ident = kept([P, P], F32, "ident")
@@ -119,19 +119,19 @@ def tile_list_track_phase_board_kernel(
                 tab_plane[32 * q : 32 * q + 4 * PASSES, :].bitcast(I32),
                 tab_scales[:, 4 * q : 4 * q + 4, :].bitcast(I32),
             )
-        w4_raw = [load_raw(w4, 0, "w4_raw0")]
+        w1_raw = [load_raw(w1, 0, "w1_raw0")]
         tab = [load_words(tab_words[a], T, f"tab{a}") for a in range(PASSES)]
-        w3_codes = kept([P, PASSES, H], U32, "w3_codes")
-        nc.sync.dma_start(w3_codes[:].bitcast(I32), w3_words.rearrange("a p n i -> p a (n i)").bitcast(I32))
-        load_weight_scales(w3_plane, w3_scales, nc.sync)
-        w4_raw.append(load_raw(w4, 1, "w4_raw1"))
-        w1_raw = [load_raw(w1, a, f"w1_raw{a}") for a in range(PASSES)]
-        w2_codes = kept([P, PASSES, 2 * H], U8, "w2_codes")
-        nc.sync.dma_start(w2_codes[:].bitcast(I32), w2_words.rearrange("a p n -> p a n").bitcast(I32))
-        load_weight_scales(w2_plane, w2_scales, nc.sync)
         v_plane = kept([P, S], U8, "v_plane")
         nc.vector.tensor_copy(v_plane[:], tab_plane[:].indirect(list1[:]))
         nc.sync.dma_start(v_plane1[0:100, :].bitcast(I32), v_plane[4:104, :].bitcast(I32))
+        w2_codes = kept([P, PASSES, 2 * H], U8, "w2_codes")
+        nc.sync.dma_start(w2_codes[:].bitcast(I32), w2_words.rearrange("a p n -> p a n").bitcast(I32))
+        load_weight_scales(w2_plane, w2_scales, nc.sync)
+        w1_raw.append(load_raw(w1, 1, "w1_raw4"))
+        w4_raw = [load_raw(w4, a, f"w4_raw{a}") for a in range(PASSES)]
+        w3_codes = kept([P, PASSES, H], U32, "w3_codes")
+        nc.sync.dma_start(w3_codes[:].bitcast(I32), w3_words.rearrange("a p n i -> p a (n i)").bitcast(I32))
+        load_weight_scales(w3_plane, w3_scales, nc.sync)
         load_page(0)
         weight_first = load_weights(slice(0, 2), slice(0, N), "weight_first", PACK)
         load_page(1)
@@ -150,7 +150,7 @@ def tile_list_track_phase_board_kernel(
         with nc.allow_non_contiguous_dma(reason="one phase offset a partition"):
             nc.sync.dma_start(phase[:], mode.rearrange("(n p) -> p n", p=P))
 
-        first_woven = shared.tile([P, PACK * H], BF16, name="w4_woven0", offset=4096, align_bytes=64)
+        first_woven = shared.tile([P, PACK * H], BF16, name="w1_woven0", offset=4096, align_bytes=64)
         v_codes = [
             [shared.tile([P, N], U32, name=f"v_codes0_{h}", offset=4096 + 2048 * h, align_bytes=64) for h in range(HALVES)],
             [kept([P, N], U32, f"v_codes1_{h}") for h in range(HALVES)],
@@ -245,21 +245,21 @@ def tile_list_track_phase_board_kernel(
                 weight = (weight_first if first < N else weight_second)[:, t, first % N : first % N + count]
             nc.vector.tensor_tensor(page[t][:].indirect(entries(list3, first, count)), values, weight, ALU.mult)
 
-        w4_q = [quantize(weave_weight(w4_raw[0], first_woven, shared_copy), "w4_0")]
+        w1_q = [quantize(weave_weight(w1_raw[0], first_woven, shared_copy), "w1_0")]
         for h in range(HALVES):
             for a in range(PASSES):
                 pick_tracks(a, h)
-        w4_q.append(quantize(weave_weight(w4_raw[1], woven("w4_woven1", 1), nc.vector.tensor_copy), "w4_1"))
-        w4_c, w4_p = [x[0] for x in w4_q], [x[1] for x in w4_q]
-        term_b = [quadrature(at(4, 5, 6, 7), 0, w3_c, w3_p, False, -1.0, "term_b", 0)]
-        times(in_phase(at(0, 1, 2, 3), 0, w4_c, w4_p), term_b[0])
-        term_b.append(quadrature(at(4, 5, 6, 0), 1, w3_c, w3_p, False, -1.0, "term_b", 4))
-        w1_c, w1_p = quantize_weight(w1_raw, (nc.scalar.copy, nc.vector.tensor_copy), "w1", 2)
-        term_a = [quadrature(at(4, 5, 6, 0), 0, w2_c, w2_p, True, 1.0, "term_a", 8)]
-        times(in_phase(at(7, 1), 1, w4_c, w4_p), term_b[1][:2])
-        waiting = in_phase(at(2), 1, w4_c, w4_p, 2)
+        w1_q.append(quantize(weave_weight(w1_raw[1], woven("w1_woven1", 1), nc.vector.tensor_copy), "w1_1"))
+        w1_c, w1_p = [x[0] for x in w1_q], [x[1] for x in w1_q]
+        term_b = [quadrature(at(4, 5, 6, 7), 0, w2_c, w2_p, True, 1.0, "term_b", 0)]
+        times(in_phase(at(0, 1, 2, 3), 0, w1_c, w1_p), term_b[0])
+        term_b.append(quadrature(at(4, 5, 6, 0), 1, w2_c, w2_p, True, 1.0, "term_b", 4))
+        w4_c, w4_p = quantize_weight(w4_raw, (nc.scalar.copy, nc.vector.tensor_copy), "w4", 2)
+        term_a = [quadrature(at(4, 5, 6, 0), 0, w3_c, w3_p, False, -1.0, "term_a", 8)]
+        times(in_phase(at(7, 1), 1, w1_c, w1_p), term_b[1][:2])
+        waiting = in_phase(at(2), 1, w1_c, w1_p, 2)
         first_a = [piece([P, H], F32, "term_a0_result", 20)] + term_a[0][1:]
-        times(in_phase(at(4, 5, 6, 0), 0, w1_c, w1_p), term_a[0], first_a)
+        times(in_phase(at(4, 5, 6, 0), 0, w4_c, w4_p), term_a[0], first_a)
         term_a[0] = first_a
         for t, bank in enumerate(at(3, 7)):
             turn(bank, t, 0, N // 2, cross[t][:, : N // 2])
@@ -267,17 +267,19 @@ def tile_list_track_phase_board_kernel(
         times(waiting, term_b[1][2:3], late_b)
         term_b[1] = term_b[1][:2] + late_b + term_b[1][3:]
         scatter(0, 0, N // 2, cross[0][:, : N // 2])
-        times(in_phase(at(5), 1, w4_c, w4_p, 3), term_b[1][3:])
+        times(in_phase(at(5), 1, w1_c, w1_p, 3), term_b[1][3:])
         scatter(1, 0, N // 2, cross[1][:, : N // 2])
-        factor = quadrature(at(1, 4, 2, 3), 1, w2_c, w2_p, True, 1.0, "factor", 12)
+        turn(banks[3], 0, N // 2, N // 2, cross[0][:, N // 2 : N])
+        scatter(0, N // 2, N // 2, cross[0][:, N // 2 : N])
+        factor = quadrature(at(1, 4, 2, 3), 1, w3_c, w3_p, False, -1.0, "factor", 12)
         term_a.append([piece([P, H], F32, f"term_a1_{jj}", 16 + jj) for jj in range(TILES_PER_HALF)])
-        times(in_phase(at(6, 0, 7, 5), 1, w1_c, w1_p), factor, term_a[1])
-        held = [piece([P, N // 2], F32, f"held{t}", 12 + t) for t in range(2)]
-        for t, bank in enumerate(at(1, 4)):
-            turn(bank, t, N // 2, N // 2, held[t][:])
-        later = [(0, N), (1, N)] + [(t, first) for t in range(2, PACK) for first in (0, N)]
-        for (t, first), bank in zip(later, at(2, 3, 6, 0, 7, 5)):
-            turn(bank, t, first, N, cross[t][:, first : first + N])
+        times(in_phase(at(6, 0, 7, 5), 1, w4_c, w4_p), factor, term_a[1])
+        held = piece([P, N // 2], F32, "held", 13)
+        turn(banks[1], 1, N // 2, N // 2, held[:])
+        later = [(0, N, N // 2), (1, N, N), (0, N + N // 2, N // 2)]
+        later = later + [(t, first, N) for t in range(2, PACK) for first in (0, N)]
+        for (t, first, count), bank in zip(later, at(4, 2, 3, 6, 0, 7, 5)):
+            turn(bank, t, first, count, cross[t][:, first : first + count])
         modes_first = pick_modes(piece([P, P], U32, "modes_first_codes", 14), piece([P, P], U8, "modes_first_plane", 15), 0, P)
 
         board = [piece([P, PACK * N], BF16, f"board{c}", 4 + c) for c in range(CHUNKS - 1)]
@@ -307,14 +309,12 @@ def tile_list_track_phase_board_kernel(
         low = [piece([P, 2, N], BF16, f"low{c}", 16 + c) for c in range(2)]
         low = low + [piece([P, 3, N], BF16, f"low{c}", 16 + c) for c in range(2, CHUNKS)]
         high = [piece([P, 2, N], BF16, f"high{c}", c) for c in range(2)]
-        for t in range(2):
-            scatter(t, N // 2, N // 2, held[t][:])
-        scatter(0, N, N, cross[0][:, N:])
-        for c in range(CHUNKS):
-            round_plane(low[c], 0, c)
-        scatter(1, N, N, cross[1][:, N:])
-        for c in range(CHUNKS):
-            round_plane(low[c], 1, c)
+        scatter(1, N // 2, N // 2, held[:])
+        for t, first, count in later[:3]:
+            scatter(t, first, count, cross[t][:, first : first + count])
+        for t in (1, 0):
+            for c in range(CHUNKS):
+                round_plane(low[c], t, c)
         for c in range(2):
             weave_pair(nc.scalar.copy, low[c], 0, c)
         scatter(2, 0, S, cross[2][:])
@@ -357,37 +357,35 @@ def tile_list_track_phase_board_kernel(
                 )
                 nc.scalar.copy(match[n][:, N * c : N * (c + 1)], bank[:])
 
+        shift = kept([P, S2 // P], F32, "shift")
+        nc.gpsimd.tensor_scalar(shift[:], phase[:], 1.0 / TWO_PI, None, ALU.mult)
+
         def pick(n, cols, picked):
-            nc.vector.tensor_copy(picked[:, cols], match[n][:].indirect(entries(list4, cols.start, cols.stop - cols.start)))
+            window = match[n][:].indirect(entries(list4, cols.start, cols.stop - cols.start))
+            nc.vector.tensor_scalar(picked[:, cols], window, 1.0 / TWO_PI, 0.25, ALU.mult, ALU.add)
 
         def count(n, cols, picked, turns):
-            nc.vector.tensor_scalar(turns[:, cols], picked[:, cols], phase[:, n : n + 1], 1.0 / TWO_PI, ALU.add, ALU.mult)
+            nc.vector.tensor_scalar(turns[:, cols], picked[:, cols], shift[:, n : n + 1], None, ALU.add)
 
-        def reduce(cols, picked, turns, angle):
-            nc.vector.scalar_tensor_tensor(angle[:, cols], turns[:, cols], -TWO_PI, picked[:, cols], ALU.mult, ALU.add)
+        def reduce(n, cols, picked, turns, part):
+            nc.vector.scalar_tensor_tensor(
+                part[:, cols], picked[:, cols], shift[:, n : n + 1], turns[:, cols], ALU.add, ALU.subtract
+            )
 
-        def cosine(n, cuts, angle):
-            offset = phase[:, n : n + 1]
-            folded = []
-            for k, cols in enumerate(cuts):
-                folded.append(piece([P, cols.stop - cols.start], F32, f"folded{n}_{cols.start}", 16 + k))
-                nc.scalar.activation(folded[k][:], angle[:, cols], ACT.Abs, bias=offset)
-            for k, cols in enumerate(cuts):
-                nc.scalar.activation(angle[:, cols], folded[k][:], ACT.Sin, bias=math.pi / 2, scale=-1.0)
-                nc.sync.dma_start(out[P * n : P * (n + 1), cols], angle[:, cols])
-
-        def halves(first, width):
-            return [slice(first, first + width // 2), slice(first + width // 2, first + width)]
+        def cosine(n, cols, part, value):
+            nc.scalar.activation(value[:, cols], part[:, cols], ACT.Sin, scale=TWO_PI)
+            nc.sync.dma_start(out[P * n : P * (n + 1), cols], value[:, cols])
 
         last = S2 // P - 1
         for n in range(S2 // P):
-            picked, turns, angle = wide(F32, f"picked{n}", n % 2), wide(I32, f"turns{n}", 2 + n % 2), wide(F32, f"angle{n}", PACK + n)
-            for first, width in ((0, PICK),) if n < last else ((0, N), (N, N)):
-                cuts = halves(first, width)
-                for cols in cuts:
-                    pick(n, cols, picked)
-                for cols in cuts:
-                    count(n, cols, picked, turns)
-                for cols in cuts:
-                    reduce(cols, picked, turns, angle)
-                cosine(n, cuts, angle)
+            picked, turns, part = wide(F32, f"picked{n}", n % 2), wide(I32, f"turns{n}", 2 + n % 2), wide(F32, f"part{n}", PACK + n)
+            halves = [slice(0, N), slice(N, PICK)]
+            for cols in halves:
+                pick(n, cols, picked)
+            for cols in halves:
+                count(n, cols, picked, turns)
+            width = N if n < last else N // 2
+            for first in range(0, PICK, width):
+                cols = slice(first, first + width)
+                reduce(n, cols, picked, turns, part)
+                cosine(n, cols, part, part)

@@ -28,6 +28,15 @@ CHUNKS = T2 // N
 PER_COL = 16
 BANKS = 8
 TWO_PI = 2.0 * math.pi
+TILES = S // P
+QUARTER = S // 4
+RAW = 0
+TAB = RAW + 4 * 8192
+WOVEN = TAB + 2 * 8192
+TERM = WOVEN + 4 * 4096 + 1024
+CROSS = TERM + 22 * 2048
+WGS = CROSS + 13312
+PLANE = WGS + 4 * 4096
 
 
 def tile_list_track_phase_board_kernel(
@@ -37,29 +46,16 @@ def tile_list_track_phase_board_kernel(
     nc = tc.nc
     with ExitStack() as ctx:
         keep = ctx.enter_context(tc.tile_pool(name="keep", bufs=1))
-        ring = ctx.enter_context(tc.tile_pool(name="ring", bufs=1))
-        shared = ctx.enter_context(tc.tile_pool(name="shared", bufs=1))
+        arena = ctx.enter_context(tc.tile_pool(name="arena", bufs=1))
         psum = ctx.enter_context(tc.psum_pool(name="psum", bufs=1))
 
         def kept(shape, dtype, name):
             return keep.tile(shape, dtype, name=name, align_bytes=64)
 
-        def slab(shape, name):
-            return ring.tile(shape, F32, name=name, tag="slab", bufs=4, align_bytes=64)
-
-        def woven(name, place):
-            return ring.tile([P, PACK * N], BF16, name=name, tag=f"woven{place}", align_bytes=64)
-
-        def piece(shape, dtype, name, place):
-            return ring.tile(shape, dtype, name=name, tag=f"place{place}", align_bytes=64)
-
-        def wide(dtype, name, place):
-            return ring.tile([P, S], dtype, name=name, tag=f"wide{place}", align_bytes=64)
+        def placed(shape, dtype, name, offset):
+            return arena.tile(shape, dtype, name=name, offset=offset, align_bytes=64)
 
         banks = [psum.tile([P, N], F32, name=f"bank{b}") for b in range(BANKS)]
-
-        def at(*numbers):
-            return [banks[b] for b in numbers]
 
         def load_list(source, name):
             tile = keep.tile(list(source.shape), U16, name=name)
@@ -71,9 +67,9 @@ def tile_list_track_phase_board_kernel(
             engine.memset(tile[:].bitcast(I32), 0)
             return tile
 
-        def load_weight_scales(tile, source, queue):
+        def load_weight_scales(tile, source):
             for q in range(4):
-                queue.dma_start(
+                nc.sync.dma_start(
                     tile[32 * q : 32 * q + 4, :, :].bitcast(I32),
                     source[:, 4 * q : 4 * q + 4, :].rearrange("a r c -> r a c").bitcast(I32),
                 )
@@ -81,7 +77,8 @@ def tile_list_track_phase_board_kernel(
         def entries(tile, first, count):
             return tile[:, first // PER_COL : (first + count) // PER_COL]
 
-        tab_plane = zeroed_plane([P, T], "tab_plane", nc.gpsimd)
+        tab_plane = placed([P, T], U8, "tab_plane", PLANE)
+        nc.gpsimd.memset(tab_plane[:].bitcast(I32), 0)
         w2_plane = zeroed_plane([P, PASSES, H], "w2_plane", nc.vector)
         w3_plane = zeroed_plane([P, PASSES, H], "w3_plane", nc.vector)
         tab2_plane = zeroed_plane([P, T3], "tab2_plane", nc.vector)
@@ -89,13 +86,12 @@ def tile_list_track_phase_board_kernel(
         ident = kept([P, P], F32, "ident")
         make_identity(nc, ident[:])
 
-        def load_raw(w, a, name):
-            raw = slab([P, PACK, H], name)
+        def load_raw(w, a, name, place):
+            raw = placed([P, PACK, H], F32, name, RAW + 8192 * place)
             nc.sync.dma_start(raw[:], w[N * a : N * (a + 1), :].rearrange("(p i) c -> p i c", i=PACK))
             return raw
 
-        def load_words(source, columns, name):
-            tile = kept([P, columns], I32, name)
+        def load_words(source, tile):
             nc.sync.dma_start(tile[:], source.rearrange("p n i -> p (n i)").bitcast(I32))
             return tile
 
@@ -106,8 +102,8 @@ def tile_list_track_phase_board_kernel(
         def load_page(t):
             nc.sync.dma_start(page[t][:], page_rows[t])
 
-        def load_weights(tiles, cols, name, place):
-            tile = ring.tile([P, 2, cols.stop - cols.start], F32, name=name, tag=f"wide{place}", align_bytes=64)
+        def load_weights(tiles, cols, name, offset):
+            tile = placed([P, 2, cols.stop - cols.start], F32, name, WGS + offset)
             for q in (0, 2, 1, 3):
                 nc.sync.dma_start(tile[32 * q : 32 * (q + 1), :, :], wgs_rows[:, tiles, cols])
             return tile
@@ -119,177 +115,207 @@ def tile_list_track_phase_board_kernel(
                 tab_plane[32 * q : 32 * q + 4 * PASSES, :].bitcast(I32),
                 tab_scales[:, 4 * q : 4 * q + 4, :].bitcast(I32),
             )
-        w1_raw = [load_raw(w1, 0, "w1_raw0")]
-        tab = [load_words(tab_words[a], T, f"tab{a}") for a in range(PASSES)]
+        tab = [load_words(tab_words[0], placed([P, T], I32, "tab0", TAB))]
+        w2_codes = kept([P, PASSES, 2 * H], U8, "w2_codes")
+        nc.sync.dma_start(w2_codes[:].bitcast(I32), w2_words.rearrange("a p n -> p a n").bitcast(I32))
+        load_weight_scales(w2_plane, w2_scales)
+        tab.append(load_words(tab_words[1], placed([P, T], I32, "tab1", TAB + 8192)))
+        list2 = load_list(offs2, "list2")
         v_plane = kept([P, S], U8, "v_plane")
         nc.vector.tensor_copy(v_plane[:], tab_plane[:].indirect(list1[:]))
         nc.sync.dma_start(v_plane1[0:100, :].bitcast(I32), v_plane[4:104, :].bitcast(I32))
-        w2_codes = kept([P, PASSES, 2 * H], U8, "w2_codes")
-        nc.sync.dma_start(w2_codes[:].bitcast(I32), w2_words.rearrange("a p n -> p a n").bitcast(I32))
-        load_weight_scales(w2_plane, w2_scales, nc.sync)
-        w1_raw.append(load_raw(w1, 1, "w1_raw4"))
-        w4_raw = [load_raw(w4, a, f"w4_raw{a}") for a in range(PASSES)]
+        w1_raw = [load_raw(w1, a, f"w1_raw{a}", a) for a in range(PASSES)]
+        w4_raw = [load_raw(w4, 0, "w4_raw0", 2)]
         w3_codes = kept([P, PASSES, H], U32, "w3_codes")
         nc.sync.dma_start(w3_codes[:].bitcast(I32), w3_words.rearrange("a p n i -> p a (n i)").bitcast(I32))
-        load_weight_scales(w3_plane, w3_scales, nc.sync)
+        load_weight_scales(w3_plane, w3_scales)
+        w4_raw.append(load_raw(w4, 1, "w4_raw1", 3))
         load_page(0)
-        weight_first = load_weights(slice(0, 2), slice(0, N), "weight_first", PACK)
+        weights = [load_weights(slice(0, 2), slice(0, QUARTER), "weight_first", 0)]
         load_page(1)
-        list2 = load_list(offs2, "list2")
-        tab2 = load_words(tab2_words[0], T3, "tab2")
+        weights.append(load_weights(slice(0, 2), slice(QUARTER, N), "weight_second", 2048))
+        tab2 = load_words(tab2_words[0], kept([P, T3], I32, "tab2"))
         for q in range(4):
             nc.sync.dma_start(
                 tab2_plane[32 * q : 32 * q + 4, :].bitcast(I32), tab2_scales[0, 4 * q : 4 * q + 4, :].bitcast(I32)
             )
-        weight_second = load_weights(slice(0, 2), slice(N, S), "weight_second", PACK + 1)
+        weights.append(load_weights(slice(0, 2), slice(N, S), "weight_third", 4096))
         load_page(2)
-        weight_rest = load_weights(slice(2, PACK), slice(0, S), "weight_rest", PACK + 2)
+        weight_rest = load_weights(slice(2, PACK), slice(0, S), "weight_rest", 8192)
         load_page(3)
         list4 = load_list(offs4, "list4")
         phase = kept([P, S2 // P], F32, "phase")
         with nc.allow_non_contiguous_dma(reason="one phase offset a partition"):
             nc.sync.dma_start(phase[:], mode.rearrange("(n p) -> p n", p=P))
 
-        first_woven = shared.tile([P, PACK * H], BF16, name="w1_woven0", offset=4096, align_bytes=64)
-        v_codes = [
-            [shared.tile([P, N], U32, name=f"v_codes0_{h}", offset=4096 + 2048 * h, align_bytes=64) for h in range(HALVES)],
-            [kept([P, N], U32, f"v_codes1_{h}") for h in range(HALVES)],
-        ]
+        def one_pass(bank, j, a, weight, fp4=False):
+            h, jj = divmod(j, TILES_PER_HALF)
+            cols = slice(P * j, P * (j + 1))
+            v_scale = v_plane1[:, cols] if fp4 and a == 1 else v_plane[4 * a : P, cols]
+            nc.tensor.matmul_mx(
+                out=banks[bank][:], lhsT=v_codes[a][h][:, P * jj : P * (jj + 1)].bitcast(FP8X4), lhsT_scale=v_scale,
+                rhs=weight[a][0], rhs_scale=weight[a][1], start=(a == 0), stop=(a == PASSES - 1),
+            )
 
-        def pick_tracks(a, h):
-            nc.vector.tensor_copy(v_codes[a][h][:], tab[a][:].bitcast(U32).indirect(entries(list1, N * h, N)))
+        def piece(name, place):
+            return placed([P, H], F32, name, TERM + 2048 * place)
 
-        def product(bank, h, jj, codes, planes, fp4):
-            cols = slice(P * jj, P * (jj + 1))
-            for a in range(PASSES):
-                if fp4 and a == 1:
-                    v_scale = v_plane1[:, N * h + P * jj : N * h + P * (jj + 1)]
-                else:
-                    v_scale = v_plane[4 * a : P, N * h + P * jj : N * h + P * (jj + 1)]
-                nc.tensor.matmul_mx(
-                    out=bank[:], lhsT=v_codes[a][h][:, cols].bitcast(FP8X4), lhsT_scale=v_scale,
-                    rhs=codes[a], rhs_scale=planes[a], start=(a == 0), stop=(a == PASSES - 1),
-                )
-            return bank
+        def take_out(bank, name, offset, sign):
+            tile = placed([P, H], F32, name, offset)
+            nc.scalar.activation(
+                tile[:].rearrange("p (t g e) -> p g t e", t=PACK, e=PACK),
+                banks[bank][:].rearrange("p (g e t) -> p g t e", t=PACK, e=PACK), ACT.Copy, scale=sign,
+            )
+            return tile
 
-        def quadrature(into, h, codes, planes, fp4, sign, name, place, first=0):
-            tiles = []
-            for jj, bank in enumerate(into, first):
-                product(bank, h, jj, codes, planes, fp4)
-                tile = piece([P, H], F32, f"{name}{h}_{jj}", place + jj)
-                nc.scalar.activation(
-                    tile[:].rearrange("p (t g e) -> p g t e", t=PACK, e=PACK),
-                    bank[:].rearrange("p (g e t) -> p g t e", t=PACK, e=PACK), ACT.Copy, scale=sign,
-                )
-                tiles.append(tile)
-            return tiles
-
-        def in_phase(into, h, codes, planes, first=0):
-            return [product(bank, h, jj, codes, planes, False) for jj, bank in enumerate(into, first)]
-
-        def times(held, tiles, results=None):
-            for bank, tile, result in zip(held, tiles, results or tiles):
-                nc.vector.tensor_tensor(
-                    result[:].rearrange("p (t m) -> p t m", t=PACK), bank[:].rearrange("p (m t) -> p t m", t=PACK),
-                    tile[:].rearrange("p (t m) -> p t m", t=PACK), ALU.mult,
-                )
+        def times(bank, tile, result):
+            nc.vector.tensor_tensor(
+                result[:].rearrange("p (t m) -> p t m", t=PACK), banks[bank][:].rearrange("p (m t) -> p t m", t=PACK),
+                tile[:].rearrange("p (t m) -> p t m", t=PACK), ALU.mult,
+            )
+            return result
 
         def shared_copy(dst, src):
             cut = dst.shape[1] // 2
             nc.vector.tensor_copy(dst[:, :cut], src[:, :cut])
             nc.scalar.copy(dst[:, cut:], src[:, cut:])
 
-        def weave_weight(raw, tile, engine_copy):
-            dst = tile[:].rearrange("p (g e i) -> p g i e", e=PACK, i=PACK)
-            src = raw[:].rearrange("p i (g e) -> p g i e", e=PACK)
-            engine_copy(dst, src)
+        def weave_weight(raw, place, name, engine_copy):
+            tile = placed([P, PACK * N], BF16, name, WOVEN + 4096 * place)
+            engine_copy(
+                tile[:].rearrange("p (g e i) -> p g i e", e=PACK, i=PACK),
+                raw[:].rearrange("p i (g e) -> p g i e", e=PACK),
+            )
             return tile
 
-        def quantize(tile, name):
-            codes = kept([P, N], U32, f"{name}_codes")
+        def quantize(tile, name, offset=None):
+            codes = kept([P, N], U32, f"{name}_codes") if offset is None else placed([P, N], U32, f"{name}_codes", offset)
             plane = kept([P, N], U8, f"{name}_plane")
             nc.vector.quantize_mx(out=codes[:].bitcast(FP8X4), scales=plane[:], in_=tile[:])
             return codes[:].bitcast(FP8X4), plane[:]
 
-        w2_c = [w2_codes[:, a, :].bitcast(FP4X4) for a in range(PASSES)]
-        w2_p = [w2_plane[:, a, :] for a in range(PASSES)]
-        w3_c = [w3_codes[:, a, :].bitcast(FP8X4) for a in range(PASSES)]
-        w3_p = [w3_plane[:, a, :] for a in range(PASSES)]
+        w2_q = [(w2_codes[:, a, :].bitcast(FP4X4), w2_plane[:, a, :]) for a in range(PASSES)]
+        w3_q = [(w3_codes[:, a, :].bitcast(FP8X4), w3_plane[:, a, :]) for a in range(PASSES)]
 
-        def quantize_weight(raws, shares, name, place):
-            tiles = [weave_weight(raws[a], woven(f"{name}_woven{a}", place + a), shares[a]) for a in range(PASSES)]
-            both = [quantize(tiles[a], f"{name}_{a}") for a in range(PASSES)]
-            return [x[0] for x in both], [x[1] for x in both]
+        term_a = [None] * TILES
+        term_b = [None] * TILES
+
+        def turn(bank, t, first, count, result):
+            for k in reversed(range(count // P)):
+                j = first // P + k
+                for n, term in enumerate((term_b, term_a)):
+                    nc.tensor.matmul(
+                        banks[bank][:, P * k : P * (k + 1)], term[j][:, P * t : P * (t + 1)], ident[:],
+                        start=(n == 0), stop=(n == 1), is_transpose=True,
+                    )
+            nc.scalar.copy(result, banks[bank][:, :count])
+            return result
+
+        def scatter(t, first, count, values):
+            if t >= 2:
+                weight = weight_rest[:, t - 2, first : first + count]
+            else:
+                weight = weights[first // QUARTER][:, t, :] if first < N else weights[2][:, t, first - N : first - N + count]
+            nc.vector.tensor_tensor(page[t][:].indirect(entries(list3, first, count)), values, weight, ALU.mult)
+
+        def place_of(number):
+            return TERM + 2048 * number
+
+        def group(bank, j, weight, fp4=False):
+            for a in range(PASSES):
+                one_pass(bank, j, a, weight, fp4)
+
+        def turned(t, first, count, bank, offset):
+            tile = placed([P, count], F32, f"cross{t}_{first}", offset)
+            return turn(bank, t, first, count, tile[:])
+
+        v_codes = [[kept([P, N], U32, f"v_codes{a}_{h}") for h in range(HALVES)] for a in range(PASSES)]
+        for a in range(PASSES):
+            for h in range(HALVES):
+                nc.vector.tensor_copy(v_codes[a][h][:], tab[a][:].bitcast(U32).indirect(entries(list1, N * h, N)))
+        factor_a = []
+        for j in range(TILES):
+            group(j, j, w2_q, True)
+            factor_a.append(take_out(j, f"factor_a{j}", place_of(j), 1.0))
+        w1_q = [quantize(weave_weight(w1_raw[a], a, f"w1_woven{a}", nc.vector.tensor_copy), f"w1_{a}") for a in range(PASSES)]
+        for j in range(TILES):
+            group(j, j, w1_q)
+        w4_woven = [weave_weight(w4_raw[0], 2, "w4_woven0", nc.scalar.copy)]
+        aside = {6: take_out(6, "aside6", RAW + 2 * 8192, 1.0)}
+        for j in range(4):
+            term_a[j] = times(j, factor_a[j], factor_a[j])
+        w4_q = [quantize(w4_woven[0], "w4_0")]
+        w4_q.append(quantize(weave_weight(w4_raw[1], 3, "w4_woven1", nc.vector.tensor_copy), "w4_1"))
+        aside[7] = take_out(7, "aside7", RAW + 3 * 8192, 1.0)
+        term_a[4] = times(4, factor_a[4], placed([P, H], F32, "term_a4", WOVEN + 4096 * 3 - 1024))
+        term_a[6] = placed([P, H], F32, "term_a6", WOVEN + 4096 * 3 + 1024)
+        term_a[7] = placed([P, H], F32, "term_a7", WOVEN + 4096 * 3 + 3072)
+        for j in (6, 7):
+            nc.gpsimd.tensor_tensor(term_a[j][:], aside[j][:], factor_a[j][:], ALU.mult)
+
+        factor_b = [None] * TILES
+
+        def quadrature(j, bank):
+            group(bank, j, w3_q)
+            factor_b[j] = take_out(bank, f"factor_b{j}", place_of(TILES + j), -1.0)
+
+        for j in range(4):
+            quadrature(j, j)
+        for j in range(4):
+            group(j, j, w4_q)
+        term_b[0] = times(0, factor_b[0], piece("term_b0", 21))
+        for j in range(1, 4):
+            term_b[j] = times(j, factor_b[j], factor_b[j])
+        term_a[5] = times(5, factor_a[5], piece("term_a5", TILES))
+        quarters = ((6, CROSS), (7, place_of(19)), (0, place_of(17) + 1536))
+        values = [turned(k % 2, QUARTER * (k // 2), QUARTER, bank, offset) for k, (bank, offset) in enumerate(quarters)]
+        for k, value in enumerate(values):
+            scatter(k % 2, QUARTER * (k // 2), QUARTER, value)
+        second_banks = {4: 1, 5: 2, 6: 3, 7: 6}
+        for j in range(4, TILES):
+            quadrature(j, second_banks[j])
+        group(3, 6, w4_q)
+        both = take_out(3, "both", place_of(16), 1.0)
+        for j in (4, 5, 7):
+            group(second_banks[j], j, w4_q)
+        term_b[6] = piece("term_b6", 19)
+        nc.gpsimd.tensor_tensor(term_b[6][:], both[:], factor_b[6][:], ALU.mult)
+        for j, place in ((4, 17), (5, 18)):
+            term_b[j] = times(second_banks[j], factor_b[j], piece(f"term_b{j}", place))
+        term_b[7] = times(second_banks[7], factor_b[7], factor_b[7])
+        later = (
+            (1, QUARTER, QUARTER, 4, place_of(13)), (0, N, QUARTER, 5, CROSS + 2048), (1, N, QUARTER, 7, CROSS + 3072),
+            (0, N + QUARTER, QUARTER, 0, CROSS + 1024), (1, N + QUARTER, QUARTER, 5, CROSS + 4096),
+        )
+        values = [turned(t, first, count, bank, offset) for t, first, count, bank, offset in later]
+        cross = [placed([P, S], F32, f"cross{t}", CROSS + 5120 + 4096 * (t - 2)) for t in range(2, PACK)]
+        for t, h, bank in ((2, 0, 6), (2, 1, 3), (3, 0, 7), (3, 1, 2)):
+            turn(bank, t, N * h, N, cross[t - 2][:, N * h : N * (h + 1)])
 
         def pick_modes(codes, plane, first, count):
             nc.vector.tensor_copy(codes[:], tab2[:].bitcast(U32).indirect(entries(list2, first, count)))
             nc.vector.tensor_copy(plane[:], tab2_plane[:].indirect(entries(list2, first, count)))
             return codes, plane
 
-        cross = [wide(F32, f"cross{t}", t) for t in range(PACK)]
+        modes_first = pick_modes(
+            placed([P, P], U32, "modes_first_codes", place_of(12)), placed([P, P], U8, "modes_first_plane", place_of(12) + 512), 0, P
+        )
+        for (t, first, count, bank, offset), value in zip(later, values):
+            scatter(t, first, count, value)
 
-        def turn(bank, t, first, count, result):
-            for k in reversed(range(count // P)):
-                h, jj = divmod(first // P + k, TILES_PER_HALF)
-                for n, term in enumerate((term_a, term_b)):
-                    nc.tensor.matmul(
-                        bank[:, P * k : P * (k + 1)], term[h][jj][:, P * t : P * (t + 1)], ident[:],
-                        start=(n == 0), stop=(n == 1), is_transpose=True,
-                    )
-            nc.scalar.copy(result, bank[:, :count])
+        board = [placed([P, PACK * N], BF16, f"board{c}", WOVEN + 4096 * c) for c in range(CHUNKS)]
 
-        def scatter(t, first, count, values):
-            if t >= 2:
-                weight = weight_rest[:, t - 2, first : first + count]
-            else:
-                weight = (weight_first if first < N else weight_second)[:, t, first % N : first % N + count]
-            nc.vector.tensor_tensor(page[t][:].indirect(entries(list3, first, count)), values, weight, ALU.mult)
+        def round_into_pair(t, c):
+            nc.scalar.copy(low[c][:, t // 2, :, t % 2], page[t][:, N * c : N * (c + 1)])
 
-        w1_q = [quantize(weave_weight(w1_raw[0], first_woven, shared_copy), "w1_0")]
-        for h in range(HALVES):
-            for a in range(PASSES):
-                pick_tracks(a, h)
-        w1_q.append(quantize(weave_weight(w1_raw[1], woven("w1_woven1", 1), nc.vector.tensor_copy), "w1_1"))
-        w1_c, w1_p = [x[0] for x in w1_q], [x[1] for x in w1_q]
-        term_b = [quadrature(at(4, 5, 6, 7), 0, w2_c, w2_p, True, 1.0, "term_b", 0)]
-        times(in_phase(at(0, 1, 2, 3), 0, w1_c, w1_p), term_b[0])
-        term_b.append(quadrature(at(4, 5, 6, 0), 1, w2_c, w2_p, True, 1.0, "term_b", 4))
-        w4_c, w4_p = quantize_weight(w4_raw, (nc.scalar.copy, nc.vector.tensor_copy), "w4", 2)
-        term_a = [quadrature(at(4, 5, 6, 0), 0, w3_c, w3_p, False, -1.0, "term_a", 8)]
-        times(in_phase(at(7, 1), 1, w1_c, w1_p), term_b[1][:2])
-        waiting = in_phase(at(2), 1, w1_c, w1_p, 2)
-        first_a = [piece([P, H], F32, "term_a0_result", 20)] + term_a[0][1:]
-        times(in_phase(at(4, 5, 6, 0), 0, w4_c, w4_p), term_a[0], first_a)
-        term_a[0] = first_a
-        for t, bank in enumerate(at(3, 7)):
-            turn(bank, t, 0, N // 2, cross[t][:, : N // 2])
-        late_b = [piece([P, H], F32, "term_b1_result", 8)]
-        times(waiting, term_b[1][2:3], late_b)
-        term_b[1] = term_b[1][:2] + late_b + term_b[1][3:]
-        scatter(0, 0, N // 2, cross[0][:, : N // 2])
-        times(in_phase(at(5), 1, w1_c, w1_p, 3), term_b[1][3:])
-        scatter(1, 0, N // 2, cross[1][:, : N // 2])
-        turn(banks[3], 0, N // 2, N // 2, cross[0][:, N // 2 : N])
-        scatter(0, N // 2, N // 2, cross[0][:, N // 2 : N])
-        factor = quadrature(at(1, 4, 2, 3), 1, w3_c, w3_p, False, -1.0, "factor", 12)
-        term_a.append([piece([P, H], F32, f"term_a1_{jj}", 16 + jj) for jj in range(TILES_PER_HALF)])
-        times(in_phase(at(6, 0, 7, 5), 1, w4_c, w4_p), factor, term_a[1])
-        held = piece([P, N // 2], F32, "held", 13)
-        turn(banks[1], 1, N // 2, N // 2, held[:])
-        later = [(0, N, N // 2), (1, N, N), (0, N + N // 2, N // 2)]
-        later = later + [(t, first, N) for t in range(2, PACK) for first in (0, N)]
-        for (t, first, count), bank in zip(later, at(4, 2, 3, 6, 0, 7, 5)):
-            turn(bank, t, first, count, cross[t][:, first : first + count])
-        modes_first = pick_modes(piece([P, P], U32, "modes_first_codes", 14), piece([P, P], U8, "modes_first_plane", 15), 0, P)
+        def weave_words(c):
+            nc.scalar.copy(
+                board[c][:].bitcast(F32).rearrange("p (c u) -> p c u", u=2),
+                low[c][:].rearrange("p u c i -> p u (c i)").bitcast(F32).rearrange("p u c -> p c u"),
+            )
 
-        board = [piece([P, PACK * N], BF16, f"board{c}", 4 + c) for c in range(CHUNKS - 1)]
-        board.append(shared.tile([P, PACK * N], BF16, name="board_last", offset=0, align_bytes=64))
-
-        def round_into_slot(t, c):
-            nc.scalar.copy(board[c][:].rearrange("p (c i) -> p c i", i=PACK)[:, :, t], page[t][:, N * c : N * (c + 1)])
-
-        def round_rows(engine_copy, pair, t, c):
-            engine_copy(pair[:, t % 2, :], page[t][:, N * c : N * (c + 1)])
+        def round_plane(engine_copy, planes, row, t, c):
+            engine_copy(planes[:, row, :], page[t][:, N * c : N * (c + 1)])
 
         def weave_pair(engine_copy, pair, u, c):
             engine_copy(
@@ -297,58 +323,44 @@ def tile_list_track_phase_board_kernel(
                 pair[:].rearrange("p i c -> p c i"),
             )
 
-        def weave_three(planes, c):
-            nc.scalar.copy(
-                board[c][:].rearrange("p (g e i) -> p g i e", i=PACK, e=PACK)[:, :, 0:3, :],
-                planes[:].rearrange("p i (g e) -> p g i e", e=PACK),
-            )
-
-        def round_plane(planes, t, c):
-            nc.scalar.copy(planes[:, t, :], page[t][:, N * c : N * (c + 1)])
-
-        low = [piece([P, 2, N], BF16, f"low{c}", 16 + c) for c in range(2)]
-        low = low + [piece([P, 3, N], BF16, f"low{c}", 16 + c) for c in range(2, CHUNKS)]
-        high = [piece([P, 2, N], BF16, f"high{c}", c) for c in range(2)]
-        scatter(1, N // 2, N // 2, held[:])
-        for t, first, count in later[:3]:
-            scatter(t, first, count, cross[t][:, first : first + count])
-        for t in (1, 0):
-            for c in range(CHUNKS):
-                round_plane(low[c], t, c)
+        low = [placed([P, 2, N], BF16, f"low{c}", place_of(number)) for c, number in ((0, 15), (1, 8))]
+        low = low + [placed([P, 2, N, 2], BF16, f"low{c}", place_of(number)) for c, number in ((2, 17), (3, 19))]
+        high = [placed([P, 2, N], BF16, f"high{c}", place_of(c)) for c in range(2)]
+        for t in range(2):
+            for c in range(2):
+                round_plane(nc.scalar.copy, low[c], t, t, c)
+            for c in range(2, CHUNKS):
+                round_into_pair(t, c)
         for c in range(2):
             weave_pair(nc.scalar.copy, low[c], 0, c)
-        scatter(2, 0, S, cross[2][:])
-        for c in range(2, CHUNKS):
-            round_plane(low[c], 2, c)
+        scatter(2, 0, S, cross[0][:])
         for c in range(2):
-            round_rows(nc.scalar.copy, high[c], 2, c)
+            round_plane(nc.scalar.copy, high[c], 0, 2, c)
         for c in range(2, CHUNKS):
-            weave_three(low[c], c)
-        scatter(3, 0, S, cross[3][:])
-        board_q = [None] * CHUNKS
-        round_rows(nc.vector.tensor_copy, high[0], 3, 0)
-        round_rows(nc.vector.tensor_copy, high[1], 3, 1)
-        round_into_slot(3, 2)
-        round_into_slot(3, 3)
-        weave_pair(nc.vector.tensor_copy, high[0], 1, 0)
-        weave_pair(nc.vector.tensor_copy, high[1], 1, 1)
-        board_q[0] = quantize(board[0], "board0")
-        board_q[1] = quantize(board[1], "board1")
-        board_q[2] = quantize(board[2], "board2")
-        board_q[3] = quantize(board[3], "board3")
+            round_into_pair(2, c)
+        scatter(3, 0, S, cross[1][:])
+        for c in range(2):
+            round_plane(nc.vector.tensor_copy, high[c], 1, 3, c)
+        for c in range(2, CHUNKS):
+            round_into_pair(3, c)
+            weave_words(c)
+        for c in range(2):
+            weave_pair(nc.vector.tensor_copy, high[c], 1, c)
+        board_q = [quantize(board[c], f"board{c}") for c in range(CHUNKS)]
+        last_board = WOVEN + 4096 * (CHUNKS - 2)
         modes_second = pick_modes(
-            shared.tile([P, P], U32, name="modes_second_codes", offset=0, align_bytes=64),
-            shared.tile([P, P], U8, name="modes_second_plane", offset=512, align_bytes=64), P, P,
+            placed([P, P], U32, "modes_second_codes", last_board),
+            placed([P, P], U8, "modes_second_plane", last_board + 512), P, P,
         )
         modes_rest = pick_modes(
-            shared.tile([P, 2 * P], U32, name="modes_rest_codes", offset=1024, align_bytes=64),
-            shared.tile([P, 2 * P], U8, name="modes_rest_plane", offset=2048, align_bytes=64), 2 * P, 2 * P,
+            placed([P, 2 * P], U32, "modes_rest_codes", last_board + 4096),
+            placed([P, 2 * P], U8, "modes_rest_plane", last_board + 4096 + 1024), 2 * P, 2 * P,
         )
         match = []
         for n in range(S2 // P):
             codes, plane = (modes_first, modes_second, modes_rest, modes_rest)[n]
             cols = slice(P * max(n - 2, 0), P * max(n - 1, 1))
-            match.append(slab([P, T2], f"match{n}"))
+            match.append(placed([P, T2], F32, f"match{n}", RAW + 8192 * n))
             for c in range(CHUNKS):
                 bank = banks[(CHUNKS * n + c) % BANKS]
                 nc.tensor.matmul_mx(
@@ -378,7 +390,9 @@ def tile_list_track_phase_board_kernel(
 
         last = S2 // P - 1
         for n in range(S2 // P):
-            picked, turns, part = wide(F32, f"picked{n}", n % 2), wide(I32, f"turns{n}", 2 + n % 2), wide(F32, f"part{n}", PACK + n)
+            picked = placed([P, PICK], F32, f"picked{n}", TAB + 4096 * (n % 2))
+            turns = placed([P, PICK], I32, f"turns{n}", TAB + 4096 * (2 + n % 2))
+            part = placed([P, PICK], F32, f"part{n}", WGS + 4096 * n)
             halves = [slice(0, N), slice(N, PICK)]
             for cols in halves:
                 pick(n, cols, picked)

@@ -194,6 +194,22 @@ def tile_list_track_phase_board_kernel(
             nc.vector.quantize_mx(out=codes[:].bitcast(FP8X4), scales=plane[:], in_=tile[:])
             return codes[:].bitcast(FP8X4), plane[:]
 
+        def weave_and_quantize_halves(raw, place, name):
+            tile = placed([P, PACK * N], BF16, f"{name}_woven", WOVEN + 4096 * place)
+            codes = kept([P, N], U32, f"{name}_codes")
+            plane = kept([P, N], U8, f"{name}_plane")
+            halves = [slice(0, N // 2), slice(N // 2, N)]
+            for cols in halves:
+                nc.vector.tensor_copy(
+                    tile[:, PACK * cols.start : PACK * cols.stop].rearrange("p (g e i) -> p g i e", e=PACK, i=PACK),
+                    raw[:, :, cols].rearrange("p i (g e) -> p g i e", e=PACK),
+                )
+            for cols in halves:
+                nc.vector.quantize_mx(
+                    out=codes[:, cols].bitcast(FP8X4), scales=plane[:, cols], in_=tile[:, PACK * cols.start : PACK * cols.stop]
+                )
+            return codes[:].bitcast(FP8X4), plane[:]
+
         w2_q = [(w2_codes[:, a, :].bitcast(FP4X4), w2_plane[:, a, :]) for a in range(PASSES)]
         w3_q = [(w3_codes[:, a, :].bitcast(FP8X4), w3_plane[:, a, :]) for a in range(PASSES)]
 
@@ -238,16 +254,16 @@ def tile_list_track_phase_board_kernel(
             group(j, j, w2_q, True)
             factor_a.append(take_out(j, f"factor_a{j}", place_of(j), 1.0))
         w1_q = [quantize(weave_weight(w1_raw[a], a, f"w1_woven{a}", nc.vector.tensor_copy), f"w1_{a}") for a in range(PASSES)]
-        for j in range(TILES):
+        for j in (0, 1, 2, 3, 4, 6, 7):
             group(j, j, w1_q)
         w4_woven = [weave_weight(w4_raw[0], 2, "w4_woven0", nc.scalar.copy)]
         aside = {6: take_out(6, "aside6", RAW + 2 * 8192, 1.0)}
         for j in range(4):
             term_a[j] = times(j, factor_a[j], factor_a[j])
         w4_q = [quantize(w4_woven[0], "w4_0")]
-        w4_q.append(quantize(weave_weight(w4_raw[1], 3, "w4_woven1", nc.vector.tensor_copy), "w4_1"))
+        w4_q.append(weave_and_quantize_halves(w4_raw[1], 3, "w4_1"))
         aside[7] = take_out(7, "aside7", RAW + 3 * 8192, 1.0)
-        term_a[4] = times(4, factor_a[4], placed([P, H], F32, "term_a4", WOVEN + 4096 * 3 - 1024))
+        term_a[4] = times(4, factor_a[4], placed([P, H], F32, "term_a4", RAW + 3 * 8192 + 2048))
         term_a[6] = placed([P, H], F32, "term_a6", WOVEN + 4096 * 3 + 1024)
         term_a[7] = placed([P, H], F32, "term_a7", WOVEN + 4096 * 3 + 3072)
         for j in (6, 7):
@@ -263,10 +279,11 @@ def tile_list_track_phase_board_kernel(
             quadrature(j, j)
         for j in range(4):
             group(j, j, w4_q)
+        group(4, 5, w1_q)
         term_b[0] = times(0, factor_b[0], piece("term_b0", 21))
         for j in range(1, 4):
             term_b[j] = times(j, factor_b[j], factor_b[j])
-        term_a[5] = times(5, factor_a[5], piece("term_a5", TILES))
+        term_a[5] = times(4, factor_a[5], piece("term_a5", TILES))
         quarters = ((6, CROSS), (7, place_of(19)), (0, place_of(17) + 1536))
         values = [turned(k % 2, QUARTER * (k // 2), QUARTER, bank, offset) for k, (bank, offset) in enumerate(quarters)]
         for k, value in enumerate(values):
@@ -282,7 +299,7 @@ def tile_list_track_phase_board_kernel(
         nc.gpsimd.tensor_tensor(term_b[6][:], both[:], factor_b[6][:], ALU.mult)
         for j, place in ((4, 17), (5, 18)):
             term_b[j] = times(second_banks[j], factor_b[j], piece(f"term_b{j}", place))
-        term_b[7] = times(second_banks[7], factor_b[7], factor_b[7])
+        term_b[7] = times(second_banks[7], factor_b[7], piece("term_b7", 12))
         later = (
             (1, QUARTER, QUARTER, 4, place_of(13)), (0, N, QUARTER, 5, CROSS + 2048), (1, N, QUARTER, 7, CROSS + 3072),
             (0, N + QUARTER, QUARTER, 0, CROSS + 1024), (1, N + QUARTER, QUARTER, 5, CROSS + 4096),
@@ -298,7 +315,7 @@ def tile_list_track_phase_board_kernel(
             return codes, plane
 
         modes_first = pick_modes(
-            placed([P, P], U32, "modes_first_codes", place_of(12)), placed([P, P], U8, "modes_first_plane", place_of(12) + 512), 0, P
+            placed([P, P], U32, "modes_first_codes", place_of(13) + 1024), placed([P, P], U8, "modes_first_plane", place_of(13) + 1536), 0, P
         )
         for (t, first, count, bank, offset), value in zip(later, values):
             scatter(t, first, count, value)
@@ -323,7 +340,7 @@ def tile_list_track_phase_board_kernel(
                 pair[:].rearrange("p i c -> p c i"),
             )
 
-        low = [placed([P, 2, N], BF16, f"low{c}", place_of(number)) for c, number in ((0, 15), (1, 8))]
+        low = [placed([P, 2, N], BF16, f"low{c}", place_of(number)) for c, number in ((0, 12), (1, 8))]
         low = low + [placed([P, 2, N, 2], BF16, f"low{c}", place_of(number)) for c, number in ((2, 17), (3, 19))]
         high = [placed([P, 2, N], BF16, f"high{c}", place_of(c)) for c in range(2)]
         for t in range(2):
@@ -347,14 +364,14 @@ def tile_list_track_phase_board_kernel(
         for c in range(2):
             weave_pair(nc.vector.tensor_copy, high[c], 1, c)
         board_q = [quantize(board[c], f"board{c}") for c in range(CHUNKS)]
-        last_board = WOVEN + 4096 * (CHUNKS - 2)
+        last_board = WOVEN + 4096 * (CHUNKS - 1)
         modes_second = pick_modes(
             placed([P, P], U32, "modes_second_codes", last_board),
             placed([P, P], U8, "modes_second_plane", last_board + 512), P, P,
         )
         modes_rest = pick_modes(
-            placed([P, 2 * P], U32, "modes_rest_codes", last_board + 4096),
-            placed([P, 2 * P], U8, "modes_rest_plane", last_board + 4096 + 1024), 2 * P, 2 * P,
+            placed([P, 2 * P], U32, "modes_rest_codes", last_board + 1024),
+            placed([P, 2 * P], U8, "modes_rest_plane", last_board + 2048), 2 * P, 2 * P,
         )
         match = []
         for n in range(S2 // P):

@@ -30,6 +30,7 @@ BANKS = 8
 TWO_PI = 2.0 * math.pi
 TILES = S // P
 QUARTER = S // 4
+QUADRANTS = (0, 2, 1, 3)
 RAW = 0
 TAB = RAW + 4 * 8192
 WOVEN = TAB + 2 * 8192
@@ -68,7 +69,7 @@ def tile_list_track_phase_board_kernel(
             return tile
 
         def load_weight_scales(tile, source):
-            for q in range(4):
+            for q in QUADRANTS:
                 nc.sync.dma_start(
                     tile[32 * q : 32 * q + 4, :, :].bitcast(I32),
                     source[:, 4 * q : 4 * q + 4, :].rearrange("a r c -> r a c").bitcast(I32),
@@ -104,13 +105,13 @@ def tile_list_track_phase_board_kernel(
 
         def load_weights(tiles, cols, name, offset):
             tile = placed([P, 2, cols.stop - cols.start], F32, name, WGS + offset)
-            for q in (0, 2, 1, 3):
+            for q in QUADRANTS:
                 nc.sync.dma_start(tile[32 * q : 32 * (q + 1), :, :], wgs_rows[:, tiles, cols])
             return tile
 
         list1 = load_list(offs, "list1")
         list3 = load_list(offs3, "list3")
-        for q in range(4):
+        for q in QUADRANTS:
             nc.sync.dma_start(
                 tab_plane[32 * q : 32 * q + 4 * PASSES, :].bitcast(I32),
                 tab_scales[:, 4 * q : 4 * q + 4, :].bitcast(I32),
@@ -123,19 +124,20 @@ def tile_list_track_phase_board_kernel(
         list2 = load_list(offs2, "list2")
         v_plane = kept([P, S], U8, "v_plane")
         nc.vector.tensor_copy(v_plane[:], tab_plane[:].indirect(list1[:]))
-        nc.sync.dma_start(v_plane1[0:100, :].bitcast(I32), v_plane[4:104, :].bitcast(I32))
+        for q in QUADRANTS:
+            nc.sync.dma_start(v_plane1[32 * q : 32 * q + 4, :].bitcast(I32), v_plane[32 * q + 4 : 32 * q + 8, :].bitcast(I32))
         w1_raw = [load_raw(w1, a, f"w1_raw{a}", a) for a in range(PASSES)]
         w4_raw = [load_raw(w4, 0, "w4_raw0", 2)]
-        w3_codes = kept([P, PASSES, H], U32, "w3_codes")
-        nc.sync.dma_start(w3_codes[:].bitcast(I32), w3_words.rearrange("a p n i -> p a (n i)").bitcast(I32))
+        w3_codes = [load_words(w3_words[0], kept([P, H], I32, "w3_codes0"))]
         load_weight_scales(w3_plane, w3_scales)
         w4_raw.append(load_raw(w4, 1, "w4_raw1", 3))
+        w3_codes.append(load_words(w3_words[1], kept([P, H], I32, "w3_codes1")))
         load_page(0)
         weights = [load_weights(slice(0, 2), slice(0, QUARTER), "weight_first", 0)]
         load_page(1)
         weights.append(load_weights(slice(0, 2), slice(QUARTER, N), "weight_second", 2048))
         tab2 = load_words(tab2_words[0], kept([P, T3], I32, "tab2"))
-        for q in range(4):
+        for q in QUADRANTS:
             nc.sync.dma_start(
                 tab2_plane[32 * q : 32 * q + 4, :].bitcast(I32), tab2_scales[0, 4 * q : 4 * q + 4, :].bitcast(I32)
             )
@@ -211,7 +213,7 @@ def tile_list_track_phase_board_kernel(
             return codes[:].bitcast(FP8X4), plane[:]
 
         w2_q = [(w2_codes[:, a, :].bitcast(FP4X4), w2_plane[:, a, :]) for a in range(PASSES)]
-        w3_q = [(w3_codes[:, a, :].bitcast(FP8X4), w3_plane[:, a, :]) for a in range(PASSES)]
+        w3_q = [(w3_codes[a][:].bitcast(FP8X4), w3_plane[:, a, :]) for a in range(PASSES)]
 
         term_a = [None] * TILES
         term_b = [None] * TILES
@@ -253,16 +255,16 @@ def tile_list_track_phase_board_kernel(
         for j in range(TILES):
             group(j, j, w2_q, True)
             factor_a.append(take_out(j, f"factor_a{j}", place_of(j), 1.0))
-        w1_q = [quantize(weave_weight(w1_raw[a], a, f"w1_woven{a}", nc.vector.tensor_copy), f"w1_{a}") for a in range(PASSES)]
+        w1_q = [quantize(weave_weight(w1_raw[0], 0, "w1_woven0", nc.vector.tensor_copy), "w1_0")]
+        w1_q.append(weave_and_quantize_halves(w1_raw[1], 1, "w1_1"))
         for j in (0, 1, 2, 3, 4, 6, 7):
             group(j, j, w1_q)
         w4_woven = [weave_weight(w4_raw[0], 2, "w4_woven0", nc.scalar.copy)]
-        aside = {6: take_out(6, "aside6", RAW + 2 * 8192, 1.0)}
+        aside = {j: take_out(j, f"aside{j}", RAW + 2 * 8192 + 2048 * (j - 6), 1.0) for j in (6, 7)}
         for j in range(4):
             term_a[j] = times(j, factor_a[j], factor_a[j])
         w4_q = [quantize(w4_woven[0], "w4_0")]
         w4_q.append(weave_and_quantize_halves(w4_raw[1], 3, "w4_1"))
-        aside[7] = take_out(7, "aside7", RAW + 3 * 8192, 1.0)
         term_a[4] = times(4, factor_a[4], placed([P, H], F32, "term_a4", RAW + 3 * 8192 + 2048))
         term_a[6] = placed([P, H], F32, "term_a6", WOVEN + 4096 * 3 + 1024)
         term_a[7] = placed([P, H], F32, "term_a7", WOVEN + 4096 * 3 + 3072)
@@ -277,22 +279,23 @@ def tile_list_track_phase_board_kernel(
 
         for j in range(4):
             quadrature(j, j)
-        for j in range(4):
-            group(j, j, w4_q)
-        group(4, 5, w1_q)
-        term_b[0] = times(0, factor_b[0], piece("term_b0", 21))
+        first_banks = (5, 6, 7, 4)
+        for j, bank in enumerate(first_banks):
+            group(bank, j, w4_q)
+        term_b[0] = times(5, factor_b[0], piece("term_b0", 21))
+        group(5, 5, w1_q)
         for j in range(1, 4):
-            term_b[j] = times(j, factor_b[j], factor_b[j])
-        term_a[5] = times(4, factor_a[5], piece("term_a5", TILES))
-        quarters = ((6, CROSS), (7, place_of(19)), (0, place_of(17) + 1536))
+            term_b[j] = times(first_banks[j], factor_b[j], factor_b[j])
+        term_a[5] = times(5, factor_a[5], piece("term_a5", TILES))
+        quarters = ((0, CROSS), (1, place_of(19)), (2, place_of(17) + 1536))
         values = [turned(k % 2, QUARTER * (k // 2), QUARTER, bank, offset) for k, (bank, offset) in enumerate(quarters)]
         for k, value in enumerate(values):
             scatter(k % 2, QUARTER * (k // 2), QUARTER, value)
-        second_banks = {4: 1, 5: 2, 6: 3, 7: 6}
+        second_banks = {4: 6, 5: 7, 6: 4, 7: 0}
         for j in range(4, TILES):
             quadrature(j, second_banks[j])
-        group(3, 6, w4_q)
-        both = take_out(3, "both", place_of(16), 1.0)
+        group(4, 6, w4_q)
+        both = take_out(4, "both", place_of(16), 1.0)
         for j in (4, 5, 7):
             group(second_banks[j], j, w4_q)
         term_b[6] = piece("term_b6", 19)
@@ -301,12 +304,12 @@ def tile_list_track_phase_board_kernel(
             term_b[j] = times(second_banks[j], factor_b[j], piece(f"term_b{j}", place))
         term_b[7] = times(second_banks[7], factor_b[7], piece("term_b7", 12))
         later = (
-            (1, QUARTER, QUARTER, 4, place_of(13)), (0, N, QUARTER, 5, CROSS + 2048), (1, N, QUARTER, 7, CROSS + 3072),
-            (0, N + QUARTER, QUARTER, 0, CROSS + 1024), (1, N + QUARTER, QUARTER, 5, CROSS + 4096),
+            (1, QUARTER, QUARTER, 3, place_of(13)), (0, N, QUARTER, 5, CROSS + 2048), (1, N, QUARTER, 1, CROSS + 3072),
+            (0, N + QUARTER, QUARTER, 2, CROSS + 1024), (1, N + QUARTER, QUARTER, 5, CROSS + 4096),
         )
         values = [turned(t, first, count, bank, offset) for t, first, count, bank, offset in later]
         cross = [placed([P, S], F32, f"cross{t}", CROSS + 5120 + 4096 * (t - 2)) for t in range(2, PACK)]
-        for t, h, bank in ((2, 0, 6), (2, 1, 3), (3, 0, 7), (3, 1, 2)):
+        for t, h, bank in ((2, 0, 0), (2, 1, 4), (3, 0, 1), (3, 1, 7)):
             turn(bank, t, N * h, N, cross[t - 2][:, N * h : N * (h + 1)])
 
         def pick_modes(codes, plane, first, count):

@@ -86,6 +86,8 @@ def tile_list_track_phase_board_kernel(
         v_plane1 = zeroed_plane([P, S], "v_plane1", nc.vector)
         ident = kept([P, P], F32, "ident")
         make_identity(nc, ident[:])
+        ready = kept([P, 1], F32, "ready")
+        nc.scalar.activation(ready[:], ident[:, 0:1], ACT.Sin)
 
         def load_raw(w, a, name, place):
             raw = placed([P, PACK, H], F32, name, RAW + 8192 * place)
@@ -408,18 +410,44 @@ def tile_list_track_phase_board_kernel(
             nc.scalar.activation(value[:, cols], part[:, cols], ACT.Sin, scale=TWO_PI)
             nc.sync.dma_start(out[P * n : P * (n + 1), cols], value[:, cols])
 
-        last = S2 // P - 1
-        for n in range(S2 // P):
-            picked = placed([P, PICK], F32, f"picked{n}", TAB + 4096 * (n % 2))
-            turns = placed([P, PICK], I32, f"turns{n}", TAB + 4096 * (2 + n % 2))
-            part = placed([P, PICK], F32, f"part{n}", WGS + 4096 * n)
-            halves = [slice(0, N), slice(N, PICK)]
+        centre = kept([P, S2 // P], F32, "centre")
+        nc.gpsimd.tensor_scalar(centre[:], phase[:], 1.0 / TWO_PI, -0.25, ALU.mult, ALU.add)
+        halves = [slice(0, N), slice(N, PICK)]
+        parts = [placed([P, PICK], F32, f"part{n}", WGS + 4096 * n) for n in range(S2 // P)]
+
+        def pick_row(n, offset):
+            picked = placed([P, PICK], F32, f"picked{n}", offset)
             for cols in halves:
                 pick(n, cols, picked)
+            return picked
+
+        def finish_row(n, picked, offset, width):
+            turns = placed([P, PICK], I32, f"turns{n}", offset)
             for cols in halves:
                 count(n, cols, picked, turns)
-            width = N if n < last else N // 2
             for first in range(0, PICK, width):
                 cols = slice(first, first + width)
-                reduce(n, cols, picked, turns, part)
-                cosine(n, cols, part, part)
+                reduce(n, cols, picked, turns, parts[n])
+                cosine(n, cols, parts[n], parts[n])
+
+        def fold_row(n, picked, offsets):
+            whole = [placed([P, N], U32, f"whole{n}_{k}", offset) for k, offset in enumerate(offsets)]
+            for k, cols in enumerate(halves):
+                nc.scalar.activation(picked[:, cols], picked[:, cols], ACT.Abs, bias=centre[:, n : n + 1])
+                nc.scalar.activation(whole[k][:], picked[:, cols], ACT.Copy, bias=0.25)
+            return whole
+
+        def finish_folded(n, folded, whole):
+            for k, cols in enumerate(halves):
+                nc.vector.scalar_tensor_tensor(
+                    parts[n][:, cols], folded[:, cols], 0.25, whole[k][:].bitcast(I32), ALU.add, ALU.subtract
+                )
+                cosine(n, cols, parts[n], parts[n])
+
+        finish_row(0, pick_row(0, TAB), TAB + 8192, N)
+        folded = [pick_row(1, CROSS), pick_row(2, TAB + 4096)]
+        whole = [fold_row(1, folded[0], (CROSS + 4096, CROSS + 6144)), fold_row(2, folded[1], (TAB + 12288, CROSS + 8192))]
+        last = pick_row(3, TAB)
+        for n in (1, 2):
+            finish_folded(n, folded[n - 1], whole[n - 1])
+        finish_row(3, last, TAB + 12288 - 2048, QUARTER)

@@ -34,9 +34,9 @@ QUADRANTS = (0, 2, 1, 3)
 RAW = 0
 TAB = RAW + 4 * 8192
 WOVEN = TAB + 2 * 8192
-TERM = WOVEN + 4 * 4096 + 1024
-CROSS = TERM + 22 * 2048
-WGS = CROSS + 13312
+TERM = WOVEN + 4 * 4096
+CROSS = TERM + 16 * 2048
+WGS = CROSS + 26 * 1024
 PLANE = WGS + 4 * 4096
 
 
@@ -68,9 +68,9 @@ def tile_list_track_phase_board_kernel(
             engine.memset(tile[:].bitcast(I32), 0)
             return tile
 
-        def load_weight_scales(tile, source):
+        def load_weight_scales(queue, tile, source):
             for q in QUADRANTS:
-                nc.sync.dma_start(
+                queue.dma_start(
                     tile[32 * q : 32 * q + 4, :, :].bitcast(I32),
                     source[:, 4 * q : 4 * q + 4, :].rearrange("a r c -> r a c").bitcast(I32),
                 )
@@ -80,8 +80,8 @@ def tile_list_track_phase_board_kernel(
 
         tab_plane = placed([P, T], U8, "tab_plane", PLANE)
         nc.gpsimd.memset(tab_plane[:].bitcast(I32), 0)
-        w2_plane = zeroed_plane([P, PASSES, H], "w2_plane", nc.vector)
         w3_plane = zeroed_plane([P, PASSES, H], "w3_plane", nc.vector)
+        w2_plane = zeroed_plane([P, PASSES, H], "w2_plane", nc.vector)
         tab2_plane = zeroed_plane([P, T3], "tab2_plane", nc.vector)
         v_plane1 = zeroed_plane([P, S], "v_plane1", nc.vector)
         ident = kept([P, P], F32, "ident")
@@ -105,11 +105,15 @@ def tile_list_track_phase_board_kernel(
         def load_page(t):
             nc.sync.dma_start(page[t][:], page_rows[t])
 
-        def load_weights(tiles, cols, name, offset):
-            tile = placed([P, 2, cols.stop - cols.start], F32, name, WGS + offset)
+        def load_weights(tiles, first, count, offset):
+            tile = placed([P, len(tiles), count], F32, f"weight{tiles[0]}_{first}", WGS + offset)
             for q in QUADRANTS:
-                nc.sync.dma_start(tile[32 * q : 32 * (q + 1), :, :], wgs_rows[:, tiles, cols])
-            return tile
+                nc.sync.dma_start(
+                    tile[32 * q : 32 * (q + 1), :, :], wgs_rows[:, tiles[0] : tiles[-1] + 1, first : first + count]
+                )
+            for k, t in enumerate(tiles):
+                for column in range(0, count, QUARTER):
+                    weights[t, first + column] = (tile, k, column)
 
         list1 = load_list(offs, "list1")
         list3 = load_list(offs3, "list3")
@@ -119,34 +123,45 @@ def tile_list_track_phase_board_kernel(
                 tab_scales[:, 4 * q : 4 * q + 4, :].bitcast(I32),
             )
         tab = [load_words(tab_words[0], placed([P, T], I32, "tab0", TAB))]
-        w2_codes = kept([P, PASSES, 2 * H], U8, "w2_codes")
-        nc.sync.dma_start(w2_codes[:].bitcast(I32), w2_words.rearrange("a p n -> p a n").bitcast(I32))
-        load_weight_scales(w2_plane, w2_scales)
+        w3_codes = [load_words(w3_words[0], kept([P, H], I32, "w3_codes0"))]
+        load_weight_scales(nc.sync, w3_plane, w3_scales)
+        load_weight_scales(nc.gpsimd, w2_plane, w2_scales)
         tab.append(load_words(tab_words[1], placed([P, T], I32, "tab1", TAB + 8192)))
-        list2 = load_list(offs2, "list2")
+        w3_codes.append(load_words(w3_words[1], kept([P, H], I32, "w3_codes1")))
+        w4_raw = [load_raw(w4, a, f"w4_raw{a}", a) for a in range(PASSES)]
+        w1_raw = [load_raw(w1, 0, "w1_raw0", 2)]
+
+        v_codes = [[kept([P, N], U32, f"v_codes{a}_{h}") for h in range(HALVES)] for a in range(PASSES)]
         v_plane = kept([P, S], U8, "v_plane")
+
+        def pick_tracks(a, h, first, count):
+            nc.vector.tensor_copy(
+                v_codes[a][h][:, first : first + count], tab[a][:].bitcast(U32).indirect(entries(list1, N * h + first, count))
+            )
+
         nc.vector.tensor_copy(v_plane[:], tab_plane[:].indirect(list1[:]))
         for q in QUADRANTS:
             nc.sync.dma_start(v_plane1[32 * q : 32 * q + 4, :].bitcast(I32), v_plane[32 * q + 4 : 32 * q + 8, :].bitcast(I32))
-        w1_raw = [load_raw(w1, a, f"w1_raw{a}", a) for a in range(PASSES)]
-        w4_raw = [load_raw(w4, 0, "w4_raw0", 2)]
-        w3_codes = [load_words(w3_words[0], kept([P, H], I32, "w3_codes0"))]
-        load_weight_scales(w3_plane, w3_scales)
-        w4_raw.append(load_raw(w4, 1, "w4_raw1", 3))
-        w3_codes.append(load_words(w3_words[1], kept([P, H], I32, "w3_codes1")))
+        w1_raw.append(load_raw(w1, 1, "w1_raw1", 3))
+        w2_codes = kept([P, PASSES, 2 * H], U8, "w2_codes")
+        nc.sync.dma_start(w2_codes[:].bitcast(I32), w2_words.rearrange("a p n -> p a n").bitcast(I32))
         load_page(0)
-        weights = [load_weights(slice(0, 2), slice(0, QUARTER), "weight_first", 0)]
+        weights = {}
+        load_weights((0, 1, 2), 0, QUARTER, 0)
         load_page(1)
-        weights.append(load_weights(slice(0, 2), slice(QUARTER, N), "weight_second", 2048))
+        load_page(2)
+        load_weights((0, 1, 2), QUARTER, QUARTER, 3072)
+        load_weights((0, 1), N, QUARTER, 6144)
         tab2 = load_words(tab2_words[0], kept([P, T3], I32, "tab2"))
         for q in QUADRANTS:
             nc.sync.dma_start(
                 tab2_plane[32 * q : 32 * q + 4, :].bitcast(I32), tab2_scales[0, 4 * q : 4 * q + 4, :].bitcast(I32)
             )
-        weights.append(load_weights(slice(0, 2), slice(N, S), "weight_third", 4096))
-        load_page(2)
-        weight_rest = load_weights(slice(2, PACK), slice(0, S), "weight_rest", 8192)
+        list2 = load_list(offs2, "list2")
+        load_weights((0, 1), N + QUARTER, QUARTER, 10240)
+        load_weights((2,), N, N, 8192)
         load_page(3)
+        load_weights((3,), 0, S, 12288)
         list4 = load_list(offs4, "list4")
         phase = kept([P, S2 // P], F32, "phase")
         with nc.allow_non_contiguous_dma(reason="one phase offset a partition"):
@@ -160,9 +175,6 @@ def tile_list_track_phase_board_kernel(
                 out=banks[bank][:], lhsT=v_codes[a][h][:, P * jj : P * (jj + 1)].bitcast(FP8X4), lhsT_scale=v_scale,
                 rhs=weight[a][0], rhs_scale=weight[a][1], start=(a == 0), stop=(a == PASSES - 1),
             )
-
-        def piece(name, place):
-            return placed([P, H], F32, name, TERM + 2048 * place)
 
         def take_out(bank, name, offset, sign):
             tile = placed([P, H], F32, name, offset)
@@ -179,10 +191,12 @@ def tile_list_track_phase_board_kernel(
             )
             return result
 
-        def shared_copy(dst, src):
-            cut = dst.shape[1] // 2
-            nc.vector.tensor_copy(dst[:, :cut], src[:, :cut])
-            nc.scalar.copy(dst[:, cut:], src[:, cut:])
+        def shared_copy(cut):
+            def both(dst, src):
+                nc.vector.tensor_copy(dst[:, :cut], src[:, :cut])
+                nc.scalar.copy(dst[:, cut:], src[:, cut:])
+
+            return both
 
         def weave_weight(raw, place, name, engine_copy):
             tile = placed([P, PACK * N], BF16, name, WOVEN + 4096 * place)
@@ -198,45 +212,34 @@ def tile_list_track_phase_board_kernel(
             nc.vector.quantize_mx(out=codes[:].bitcast(FP8X4), scales=plane[:], in_=tile[:])
             return codes[:].bitcast(FP8X4), plane[:]
 
-        def weave_and_quantize_halves(raw, place, name):
-            tile = placed([P, PACK * N], BF16, f"{name}_woven", WOVEN + 4096 * place)
-            codes = kept([P, N], U32, f"{name}_codes")
-            plane = kept([P, N], U8, f"{name}_plane")
-            halves = [slice(0, N // 2), slice(N // 2, N)]
-            for cols in halves:
-                nc.vector.tensor_copy(
-                    tile[:, PACK * cols.start : PACK * cols.stop].rearrange("p (g e i) -> p g i e", e=PACK, i=PACK),
-                    raw[:, :, cols].rearrange("p i (g e) -> p g i e", e=PACK),
-                )
-            for cols in halves:
-                nc.vector.quantize_mx(
-                    out=codes[:, cols].bitcast(FP8X4), scales=plane[:, cols], in_=tile[:, PACK * cols.start : PACK * cols.stop]
-                )
-            return codes[:].bitcast(FP8X4), plane[:]
-
         w2_q = [(w2_codes[:, a, :].bitcast(FP4X4), w2_plane[:, a, :]) for a in range(PASSES)]
         w3_q = [(w3_codes[a][:].bitcast(FP8X4), w3_plane[:, a, :]) for a in range(PASSES)]
 
         term_a = [None] * TILES
         term_b = [None] * TILES
 
-        def turn(bank, t, first, count, result):
+        def turn(bank, t, first, count, column=0):
             for k in reversed(range(count // P)):
                 j = first // P + k
-                for n, term in enumerate((term_b, term_a)):
+                for n, term in enumerate((term_a, term_b)):
                     nc.tensor.matmul(
-                        banks[bank][:, P * k : P * (k + 1)], term[j][:, P * t : P * (t + 1)], ident[:],
+                        banks[bank][:, column + P * k : column + P * (k + 1)], term[j][:, P * t : P * (t + 1)], ident[:],
                         start=(n == 0), stop=(n == 1), is_transpose=True,
                     )
-            nc.scalar.copy(result, banks[bank][:, :count])
-            return result
+            return banks[bank][:, column : column + count]
+
+        def weight_of(t, first, count):
+            tile, k, column = weights[t, first]
+            return tile[:, k, column : column + count]
+
+        def window(t, first, count):
+            return page[t][:].indirect(entries(list3, first, count))
 
         def scatter(t, first, count, values):
-            if t >= 2:
-                weight = weight_rest[:, t - 2, first : first + count]
-            else:
-                weight = weights[first // QUARTER][:, t, :] if first < N else weights[2][:, t, first - N : first - N + count]
-            nc.vector.tensor_tensor(page[t][:].indirect(entries(list3, first, count)), values, weight, ALU.mult)
+            nc.vector.tensor_tensor(window(t, first, count), values, weight_of(t, first, count), ALU.mult)
+
+        def put(t, first, count, values):
+            nc.vector.tensor_copy(window(t, first, count), values)
 
         def place_of(number):
             return TERM + 2048 * number
@@ -245,74 +248,134 @@ def tile_list_track_phase_board_kernel(
             for a in range(PASSES):
                 one_pass(bank, j, a, weight, fp4)
 
-        def turned(t, first, count, bank, offset):
-            tile = placed([P, count], F32, f"cross{t}_{first}", offset)
-            return turn(bank, t, first, count, tile[:])
+        def copied(source, name, offset):
+            tile = placed([P, source.shape[1]], F32, name, offset)
+            nc.scalar.copy(tile[:], source)
+            return tile
 
-        v_codes = [[kept([P, N], U32, f"v_codes{a}_{h}") for h in range(HALVES)] for a in range(PASSES)]
-        for a in range(PASSES):
-            for h in range(HALVES):
-                nc.vector.tensor_copy(v_codes[a][h][:], tab[a][:].bitcast(U32).indirect(entries(list1, N * h, N)))
-        factor_a = []
-        for j in range(TILES):
-            group(j, j, w2_q, True)
-            factor_a.append(take_out(j, f"factor_a{j}", place_of(j), 1.0))
-        w1_q = [quantize(weave_weight(w1_raw[0], 0, "w1_woven0", nc.vector.tensor_copy), "w1_0")]
-        w1_q.append(weave_and_quantize_halves(w1_raw[1], 1, "w1_1"))
-        for j in (0, 1, 2, 3, 4, 6, 7):
-            group(j, j, w1_q)
-        w4_woven = [weave_weight(w4_raw[0], 2, "w4_woven0", nc.scalar.copy)]
-        aside = {j: take_out(j, f"aside{j}", RAW + 2 * 8192 + 2048 * (j - 6), 1.0) for j in (6, 7)}
-        for j in range(4):
-            term_a[j] = times(j, factor_a[j], factor_a[j])
-        w4_q = [quantize(w4_woven[0], "w4_0")]
-        w4_q.append(weave_and_quantize_halves(w4_raw[1], 3, "w4_1"))
-        term_a[4] = times(4, factor_a[4], placed([P, H], F32, "term_a4", RAW + 3 * 8192 + 2048))
-        term_a[6] = placed([P, H], F32, "term_a6", WOVEN + 4096 * 3 + 1024)
-        term_a[7] = placed([P, H], F32, "term_a7", WOVEN + 4096 * 3 + 3072)
-        for j in (6, 7):
-            nc.gpsimd.tensor_tensor(term_a[j][:], aside[j][:], factor_a[j][:], ALU.mult)
 
+        factor_a = [None] * TILES
         factor_b = [None] * TILES
 
-        def quadrature(j, bank):
+        def before(j, bank):
             group(bank, j, w3_q)
-            factor_b[j] = take_out(bank, f"factor_b{j}", place_of(TILES + j), -1.0)
+            factor_b[j] = take_out(bank, f"factor_b{j}", place_of(j), -1.0)
 
-        for j in range(4):
-            quadrature(j, j)
-        first_banks = (5, 6, 7, 4)
-        for j, bank in enumerate(first_banks):
-            group(bank, j, w4_q)
-        term_b[0] = times(5, factor_b[0], piece("term_b0", 21))
-        group(5, 5, w1_q)
-        for j in range(1, 4):
-            term_b[j] = times(first_banks[j], factor_b[j], factor_b[j])
-        term_a[5] = times(5, factor_a[5], piece("term_a5", TILES))
-        quarters = ((0, CROSS), (1, place_of(19)), (2, place_of(17) + 1536))
-        values = [turned(k % 2, QUARTER * (k // 2), QUARTER, bank, offset) for k, (bank, offset) in enumerate(quarters)]
-        for k, value in enumerate(values):
-            scatter(k % 2, QUARTER * (k // 2), QUARTER, value)
-        second_banks = {4: 6, 5: 7, 6: 4, 7: 0}
-        for j in range(4, TILES):
-            quadrature(j, second_banks[j])
-        group(4, 6, w4_q)
-        both = take_out(4, "both", place_of(16), 1.0)
-        for j in (4, 5, 7):
-            group(second_banks[j], j, w4_q)
-        term_b[6] = piece("term_b6", 19)
-        nc.gpsimd.tensor_tensor(term_b[6][:], both[:], factor_b[6][:], ALU.mult)
-        for j, place in ((4, 17), (5, 18)):
-            term_b[j] = times(second_banks[j], factor_b[j], piece(f"term_b{j}", place))
-        term_b[7] = times(second_banks[7], factor_b[7], piece("term_b7", 12))
-        later = (
-            (1, QUARTER, QUARTER, 3, place_of(13)), (0, N, QUARTER, 5, CROSS + 2048), (1, N, QUARTER, 1, CROSS + 3072),
-            (0, N + QUARTER, QUARTER, 2, CROSS + 1024), (1, N + QUARTER, QUARTER, 5, CROSS + 4096),
-        )
-        values = [turned(t, first, count, bank, offset) for t, first, count, bank, offset in later]
-        cross = [placed([P, S], F32, f"cross{t}", CROSS + 5120 + 4096 * (t - 2)) for t in range(2, PACK)]
-        for t, h, bank in ((2, 0, 0), (2, 1, 4), (3, 0, 1), (3, 1, 7)):
-            turn(bank, t, N * h, N, cross[t - 2][:, N * h : N * (h + 1)])
+        def now(j, bank):
+            group(bank, j, w2_q, True)
+            factor_a[j] = take_out(bank, f"factor_a{j}", place_of(TILES + j), 1.0)
+
+        def set_aside(bank, name, slot):
+            return take_out(bank, name, TAB + 2048 * slot, 1.0)
+
+        def side_product(other, factor, result=None):
+            result = factor if result is None else result
+            nc.gpsimd.tensor_tensor(result[:], other[:], factor[:], ALU.mult)
+            return result
+
+        for h in range(HALVES):
+            pick_tracks(0, h, 0, N)
+        for first in (0, QUARTER):
+            pick_tracks(1, 0, first, QUARTER)
+        pick_tracks(1, 1, 0, N)
+
+        def take_b(j, bank):
+            factor_b[j] = take_out(bank, f"factor_b{j}", place_of(j), -1.0)
+
+        for a in range(PASSES):
+            for j in range(TILES):
+                one_pass(j, j, a, w3_q)
+        for j in range(TILES):
+            take_b(j, j)
+        w4_q = [quantize(weave_weight(w4_raw[a], a, f"w4_woven{a}", nc.vector.tensor_copy), f"w4_{a}") for a in range(PASSES)]
+        for j in range(TILES):
+            one_pass(j, j, 0, w4_q)
+        for j in (0, 5, 6, 1, 2, 3, 4, 7):
+            one_pass(j, j, 1, w4_q)
+
+        def term_at(name, offset):
+            return placed([P, H], F32, name, offset)
+
+        first_raw, last_raw = RAW + 2 * 8192, RAW + 3 * 8192
+        w1_woven = [weave_weight(w1_raw[0], 2, "w1_woven0", shared_copy(88))]
+        term_b[0] = times(0, factor_b[0], term_at("term_b0", first_raw))
+        w1_q = [quantize(w1_woven[0], "w1_0")]
+        term_b[1] = times(1, factor_b[1], term_at("term_b1", first_raw + 2048))
+        aside = {j: take_out(j, f"aside_b{j}", first_raw + 2048 * (j - 3), 1.0) for j in (5, 6)}
+        w1_woven.append(weave_weight(w1_raw[1], 3, "w1_woven1", shared_copy(64)))
+        w1_q.append(quantize(w1_woven[1], "w1_1"))
+        for j in (2, 3):
+            term_b[j] = times(j, factor_b[j], term_at(f"term_b{j}", last_raw + 2048 * (j - 2)))
+        for j in (5, 6):
+            term_b[j] = side_product(aside[j], factor_b[j], term_at(f"term_b{j}", WOVEN + 3 * 4096 + 2048 * (j - 5)))
+        for j, bank in enumerate((0, 5)):
+            one_pass(bank, j, 0, w1_q)
+        now(0, 6)
+        now(1, 1)
+        for j, bank in enumerate((0, 5)):
+            one_pass(bank, j, 1, w1_q)
+        term_b[7] = side_product(take_out(7, "aside_b7", place_of(3), 1.0), factor_b[7])
+        term_a[0] = times(0, factor_a[0], factor_a[0])
+        term_a[1] = times(5, factor_a[1], term_at("term_a1", place_of(2)))
+        now(2, 2)
+        group(6, 2, w1_q)
+        now(3, 3)
+        term_b[4] = times(4, factor_b[4], term_at("term_b4", place_of(TILES + 1)))
+        term_a[2] = times(6, factor_a[2], factor_a[2])
+        value = {}
+        turned = {}
+
+        def value_tile(t, k):
+            value[t, k] = placed([P, QUARTER], F32, f"value{t}_{k}", CROSS + 1024 * (10 + 3 * k + t))
+            return value[t, k]
+
+        for t, bank in ((0, 1), (1, 0)):
+            nc.vector.tensor_tensor(value_tile(t, 0)[:], turn(bank, t, 0, QUARTER), weight_of(t, 0, QUARTER), ALU.mult)
+
+        def side_turn(t, k, bank, slot):
+            turned[t, k] = copied(turn(bank, t, QUARTER * k, QUARTER), f"turned{t}_{k}", CROSS + 2048 * slot)
+
+        def side_weigh(t, k):
+            nc.gpsimd.tensor_tensor(value_tile(t, k)[:], turned[t, k][:], weight_of(t, QUARTER * k, QUARTER), ALU.mult)
+
+        def side_factors(j, first_bank, second_bank):
+            now(j, first_bank)
+            group(second_bank, j, w1_q)
+            aside[j] = set_aside(second_bank, f"aside_a{j}", j)
+
+        def side_term(j):
+            term_a[j] = side_product(aside[j], factor_a[j], term_at(f"term_a{j}", CROSS + 2048 * (j - 4)))
+
+        put(0, 0, QUARTER, value[0, 0][:])
+        group(5, 3, w1_q)
+        term_a[3] = times(5, factor_a[3], factor_a[3])
+        side_turn(2, 0, 7, 0)
+        side_weigh(2, 0)
+        side_factors(4, 2, 4)
+        side_term(4)
+        side_factors(5, 0, 1)
+        for t, bank, slot in ((0, 3, 1), (1, 6, 2), (2, 7, 4)):
+            side_turn(t, 1, bank, slot)
+        side_weigh(0, 1)
+        side_weigh(1, 1)
+        side_term(5)
+        side_weigh(2, 1)
+        side_factors(6, 5, 2)
+        side_term(6)
+        side_factors(7, 4, 0)
+        for t, bank, slot in ((0, 1, 3), (1, 3, 4)):
+            side_turn(t, 2, bank, slot)
+            side_weigh(t, 2)
+        side_term(7)
+        whole_three = placed([P, S], F32, "value3", CROSS + 1024 * 22)
+        nc.scalar.copy(whole_three[:, :N], turn(1, 3, 0, N))
+        for t, bank in ((0, 7), (1, 5)):
+            value[t, 3] = copied(turn(bank, t, N + QUARTER, QUARTER), f"value{t}_3", CROSS + 1024 * (18 + t))
+        rest_two = copied(turn(2, 2, N, N), "value2_2", CROSS + 1024 * 20)
+        nc.scalar.copy(whole_three[:, N:], turn(4, 3, N, N))
+        for k in range(3):
+            for t in range(1 if k == 0 else 0, 3 if k < 2 else 2):
+                put(t, QUARTER * k, QUARTER, value[t, k][:])
 
         def pick_modes(codes, plane, first, count):
             nc.vector.tensor_copy(codes[:], tab2[:].bitcast(U32).indirect(entries(list2, first, count)))
@@ -320,10 +383,10 @@ def tile_list_track_phase_board_kernel(
             return codes, plane
 
         modes_first = pick_modes(
-            placed([P, P], U32, "modes_first_codes", place_of(13) + 1024), placed([P, P], U8, "modes_first_plane", place_of(13) + 1536), 0, P
+            placed([P, P], U32, "modes_first_codes", CROSS + 2048 * 4), placed([P, P], U8, "modes_first_plane", CROSS + 2048 * 4 + 512), 0, P
         )
-        for (t, first, count, bank, offset), value in zip(later, values):
-            scatter(t, first, count, value)
+        for t in range(2):
+            scatter(t, N + QUARTER, QUARTER, value[t, 3][:])
 
         board = [placed([P, PACK * N], BF16, f"board{c}", WOVEN + 4096 * c) for c in range(CHUNKS)]
 
@@ -345,8 +408,9 @@ def tile_list_track_phase_board_kernel(
                 pair[:].rearrange("p i c -> p c i"),
             )
 
-        low = [placed([P, 2, N], BF16, f"low{c}", place_of(number)) for c, number in ((0, 12), (1, 8))]
-        low = low + [placed([P, 2, N, 2], BF16, f"low{c}", place_of(number)) for c, number in ((2, 17), (3, 19))]
+        planes = placed([P, 2, 2, N], BF16, "low_planes", place_of(9) - 3072)
+        pairs = placed([P, 2, 2, N, 2], BF16, "low_pairs", place_of(9) + 1024)
+        low = [planes[:, 0], planes[:, 1], pairs[:, 0], pairs[:, 1]]
         high = [placed([P, 2, N], BF16, f"high{c}", place_of(c)) for c in range(2)]
         for t in range(2):
             for c in range(2):
@@ -355,16 +419,17 @@ def tile_list_track_phase_board_kernel(
                 round_into_pair(t, c)
         for c in range(2):
             weave_pair(nc.scalar.copy, low[c], 0, c)
-        scatter(2, 0, S, cross[0][:])
+        scatter(2, N, N, rest_two[:])
         for c in range(2):
             round_plane(nc.scalar.copy, high[c], 0, 2, c)
         for c in range(2, CHUNKS):
             round_into_pair(2, c)
-        scatter(3, 0, S, cross[1][:])
+        scatter(3, 0, S, whole_three[:])
         for c in range(2):
             round_plane(nc.vector.tensor_copy, high[c], 1, 3, c)
         for c in range(2, CHUNKS):
             round_into_pair(3, c)
+        for c in range(2, CHUNKS):
             weave_words(c)
         for c in range(2):
             weave_pair(nc.vector.tensor_copy, high[c], 1, c)
@@ -434,6 +499,7 @@ def tile_list_track_phase_board_kernel(
             whole = [placed([P, N], U32, f"whole{n}_{k}", offset) for k, offset in enumerate(offsets)]
             for k, cols in enumerate(halves):
                 nc.scalar.activation(picked[:, cols], picked[:, cols], ACT.Abs, bias=centre[:, n : n + 1])
+            for k, cols in enumerate(halves):
                 nc.scalar.activation(whole[k][:], picked[:, cols], ACT.Copy, bias=0.25)
             return whole
 

@@ -147,10 +147,12 @@ def tile_list_track_phase_board_kernel(
         nc.sync.dma_start(w2_codes[:].bitcast(I32), w2_words.rearrange("a p n -> p a n").bitcast(I32))
         load_page(0)
         weights = {}
-        load_weights((0, 1, 2), 0, QUARTER, 0)
+        load_weights((0, 1), 0, QUARTER, 0)
         load_page(1)
+        load_weights((2,), 0, QUARTER, 2048)
         load_page(2)
-        load_weights((0, 1, 2), QUARTER, QUARTER, 3072)
+        load_weights((0,), QUARTER, QUARTER, 3072)
+        load_weights((1, 2), QUARTER, QUARTER, 4096)
         load_weights((0, 1), N, QUARTER, 6144)
         tab2 = load_words(tab2_words[0], kept([P, T3], I32, "tab2"))
         for q in QUADRANTS:
@@ -300,9 +302,9 @@ def tile_list_track_phase_board_kernel(
         w1_woven = [weave_weight(w1_raw[0], 2, "w1_woven0", shared_copy(88))]
         term_b[0] = times(0, factor_b[0], term_at("term_b0", first_raw))
         w1_q = [quantize(w1_woven[0], "w1_0")]
-        term_b[1] = times(1, factor_b[1], term_at("term_b1", first_raw + 2048))
         aside = {j: take_out(j, f"aside_b{j}", first_raw + 2048 * (j - 3), 1.0) for j in (5, 6)}
-        w1_woven.append(weave_weight(w1_raw[1], 3, "w1_woven1", shared_copy(64)))
+        w1_woven.append(weave_weight(w1_raw[1], 3, "w1_woven1", shared_copy(84)))
+        term_b[1] = times(1, factor_b[1], term_at("term_b1", last_raw + 2 * 2048))
         w1_q.append(quantize(w1_woven[1], "w1_1"))
         for j in (2, 3):
             term_b[j] = times(j, factor_b[j], term_at(f"term_b{j}", last_raw + 2048 * (j - 2)))
@@ -348,7 +350,7 @@ def tile_list_track_phase_board_kernel(
 
         put(0, 0, QUARTER, value[0, 0][:])
         group(5, 3, w1_q)
-        term_a[3] = times(5, factor_a[3], factor_a[3])
+        term_a[3] = times(5, factor_a[3], term_at("term_a3", WGS))
         side_turn(2, 0, 7, 0)
         side_weigh(2, 0)
         side_factors(4, 2, 4)
@@ -433,7 +435,7 @@ def tile_list_track_phase_board_kernel(
             weave_words(c)
         for c in range(2):
             weave_pair(nc.vector.tensor_copy, high[c], 1, c)
-        board_q = [quantize(board[c], f"board{c}") for c in range(CHUNKS)]
+        board_q = [quantize(board[c], f"board{c}", CROSS if c == 2 else None) for c in range(CHUNKS)]
         last_board = WOVEN + 4096 * (CHUNKS - 1)
         modes_second = pick_modes(
             placed([P, P], U32, "modes_second_codes", last_board),
@@ -458,62 +460,38 @@ def tile_list_track_phase_board_kernel(
 
         shift = kept([P, S2 // P], F32, "shift")
         nc.gpsimd.tensor_scalar(shift[:], phase[:], 1.0 / TWO_PI, None, ALU.mult)
+        rows = range(S2 // P)
+        last = rows[-1]
+        picked = [[placed([P, N], F32, f"picked{n}_{h}", TAB + 4096 * n + 2048 * h) for h in range(2)] for n in rows]
+        turns = [placed([P, PICK], I32, f"turns{n}", CROSS) for n in range(last)]
+        turns.append(placed([P, PICK], I32, f"turns{last}", TAB + 4096 * (last - 1) - 2048))
+        parts = [placed([P, PICK], F32, f"part{n}", WGS + 4096 * n) for n in rows]
 
-        def pick(n, cols, picked):
-            window = match[n][:].indirect(entries(list4, cols.start, cols.stop - cols.start))
-            nc.vector.tensor_scalar(picked[:, cols], window, 1.0 / TWO_PI, 0.25, ALU.mult, ALU.add)
+        def pick_row(n):
+            for h in range(2):
+                chosen = match[n][:].indirect(entries(list4, N * h, N))
+                nc.vector.tensor_scalar(picked[n][h][:], chosen, 1.0 / TWO_PI, 0.25, ALU.mult, ALU.add)
 
-        def count(n, cols, picked, turns):
-            nc.vector.tensor_scalar(turns[:, cols], picked[:, cols], shift[:, n : n + 1], None, ALU.add)
-
-        def reduce(n, cols, picked, turns, part):
-            nc.vector.scalar_tensor_tensor(
-                part[:, cols], picked[:, cols], shift[:, n : n + 1], turns[:, cols], ALU.add, ALU.subtract
-            )
-
-        def cosine(n, cols, part, value):
-            nc.scalar.activation(value[:, cols], part[:, cols], ACT.Sin, scale=TWO_PI)
-            nc.sync.dma_start(out[P * n : P * (n + 1), cols], value[:, cols])
-
-        centre = kept([P, S2 // P], F32, "centre")
-        nc.gpsimd.tensor_scalar(centre[:], phase[:], 1.0 / TWO_PI, -0.25, ALU.mult, ALU.add)
-        halves = [slice(0, N), slice(N, PICK)]
-        parts = [placed([P, PICK], F32, f"part{n}", WGS + 4096 * n) for n in range(S2 // P)]
-
-        def pick_row(n, offset):
-            picked = placed([P, PICK], F32, f"picked{n}", offset)
-            for cols in halves:
-                pick(n, cols, picked)
-            return picked
-
-        def finish_row(n, picked, offset, width):
-            turns = placed([P, PICK], I32, f"turns{n}", offset)
-            for cols in halves:
-                count(n, cols, picked, turns)
+        def finish_row(n, width):
             for first in range(0, PICK, width):
                 cols = slice(first, first + width)
-                reduce(n, cols, picked, turns, parts[n])
-                cosine(n, cols, parts[n], parts[n])
-
-        def fold_row(n, picked, offsets):
-            whole = [placed([P, N], U32, f"whole{n}_{k}", offset) for k, offset in enumerate(offsets)]
-            for k, cols in enumerate(halves):
-                nc.scalar.activation(picked[:, cols], picked[:, cols], ACT.Abs, bias=centre[:, n : n + 1])
-            for k, cols in enumerate(halves):
-                nc.scalar.activation(whole[k][:], picked[:, cols], ACT.Copy, bias=0.25)
-            return whole
-
-        def finish_folded(n, folded, whole):
-            for k, cols in enumerate(halves):
+                values = picked[n][first // N][:, first % N : first % N + width]
                 nc.vector.scalar_tensor_tensor(
-                    parts[n][:, cols], folded[:, cols], 0.25, whole[k][:].bitcast(I32), ALU.add, ALU.subtract
+                    parts[n][:, cols], values, shift[:, n : n + 1], turns[n][:, cols], ALU.add, ALU.subtract
                 )
-                cosine(n, cols, parts[n], parts[n])
+                nc.scalar.activation(parts[n][:, cols], parts[n][:, cols], ACT.Sin, scale=TWO_PI)
+                nc.sync.dma_start(out[P * n : P * (n + 1), cols], parts[n][:, cols])
 
-        finish_row(0, pick_row(0, TAB), TAB + 8192, N)
-        folded = [pick_row(1, CROSS), pick_row(2, TAB + 4096)]
-        whole = [fold_row(1, folded[0], (CROSS + 4096, CROSS + 6144)), fold_row(2, folded[1], (TAB + 12288, CROSS + 8192))]
-        last = pick_row(3, TAB)
-        for n in (1, 2):
-            finish_folded(n, folded[n - 1], whole[n - 1])
-        finish_row(3, last, TAB + 12288 - 2048, QUARTER)
+        pick_row(0)
+        for n in range(last):
+            for h in range(2):
+                nc.gpsimd.tensor_scalar(
+                    turns[n][:, N * h : N * (h + 1)], picked[n][h][:], 1.0, shift[:, n : n + 1], ALU.mult, ALU.add
+                )
+            pick_row(n + 1)
+            finish_row(n, N)
+        for h in range(2):
+            nc.vector.tensor_scalar(
+                turns[last][:, N * h : N * (h + 1)], picked[last][h][:], shift[:, last : last + 1], None, ALU.add
+            )
+        finish_row(last, QUARTER)

@@ -36,8 +36,9 @@ TAB = RAW + 4 * 8192
 WOVEN = TAB + 2 * 8192
 TERM = WOVEN + 4 * 4096
 CROSS = TERM + 16 * 2048
-WGS = CROSS + 26 * 1024
+WGS = CROSS + 28 * 1024
 PLANE = WGS + 4 * 4096
+COUNT = TERM + 12 * 2048
 
 
 def tile_list_track_phase_board_kernel(
@@ -80,8 +81,8 @@ def tile_list_track_phase_board_kernel(
 
         tab_plane = placed([P, T], U8, "tab_plane", PLANE)
         nc.gpsimd.memset(tab_plane[:].bitcast(I32), 0)
-        w3_plane = zeroed_plane([P, PASSES, H], "w3_plane", nc.vector)
         w2_plane = zeroed_plane([P, PASSES, H], "w2_plane", nc.vector)
+        w3_plane = zeroed_plane([P, PASSES, H], "w3_plane", nc.vector)
         tab2_plane = zeroed_plane([P, T3], "tab2_plane", nc.vector)
         v_plane1 = zeroed_plane([P, S], "v_plane1", nc.vector)
         ident = kept([P, P], F32, "ident")
@@ -117,19 +118,15 @@ def tile_list_track_phase_board_kernel(
 
         list1 = load_list(offs, "list1")
         list3 = load_list(offs3, "list3")
-        for q in QUADRANTS:
-            nc.sync.dma_start(
-                tab_plane[32 * q : 32 * q + 4 * PASSES, :].bitcast(I32),
-                tab_scales[:, 4 * q : 4 * q + 4, :].bitcast(I32),
-            )
+        scale_rows = tab_scales.rearrange("a (q r) c -> r q a c", r=4)
+        for r in range(4):
+            nc.sync.dma_start(tab_plane[r:P:16, :].bitcast(I32), scale_rows[r].bitcast(I32))
         tab = [load_words(tab_words[0], placed([P, T], I32, "tab0", TAB))]
-        w3_codes = [load_words(w3_words[0], kept([P, H], I32, "w3_codes0"))]
-        load_weight_scales(nc.sync, w3_plane, w3_scales)
-        load_weight_scales(nc.gpsimd, w2_plane, w2_scales)
+        w2_codes = kept([P, PASSES, 2 * H], U8, "w2_codes")
+        nc.sync.dma_start(w2_codes[:].bitcast(I32), w2_words.rearrange("a p n -> p a n").bitcast(I32))
+        load_weight_scales(nc.sync, w2_plane, w2_scales)
         tab.append(load_words(tab_words[1], placed([P, T], I32, "tab1", TAB + 8192)))
-        w3_codes.append(load_words(w3_words[1], kept([P, H], I32, "w3_codes1")))
-        w4_raw = [load_raw(w4, a, f"w4_raw{a}", a) for a in range(PASSES)]
-        w1_raw = [load_raw(w1, 0, "w1_raw0", 2)]
+        list2 = load_list(offs2, "list2")
 
         v_codes = [[kept([P, N], U32, f"v_codes{a}_{h}") for h in range(HALVES)] for a in range(PASSES)]
         v_plane = kept([P, S], U8, "v_plane")
@@ -141,25 +138,25 @@ def tile_list_track_phase_board_kernel(
 
         nc.vector.tensor_copy(v_plane[:], tab_plane[:].indirect(list1[:]))
         for q in QUADRANTS:
-            nc.sync.dma_start(v_plane1[32 * q : 32 * q + 4, :].bitcast(I32), v_plane[32 * q + 4 : 32 * q + 8, :].bitcast(I32))
-        w1_raw.append(load_raw(w1, 1, "w1_raw1", 3))
-        w2_codes = kept([P, PASSES, 2 * H], U8, "w2_codes")
-        nc.sync.dma_start(w2_codes[:].bitcast(I32), w2_words.rearrange("a p n -> p a n").bitcast(I32))
+            nc.sync.dma_start(v_plane1[32 * q : 32 * q + 4, :].bitcast(I32), v_plane[32 * q + 16 : 32 * q + 20, :].bitcast(I32))
+        w1_raw = [load_raw(w1, a, f"w1_raw{a}", a) for a in range(PASSES)]
+        w4_raw = [load_raw(w4, 0, "w4_raw0", 2)]
+        load_weight_scales(nc.sync, w3_plane, w3_scales)
+        w4_raw.append(load_raw(w4, 1, "w4_raw1", 3))
+        w3_codes = [load_words(w3_words[a], kept([P, H], I32, f"w3_codes{a}")) for a in range(PASSES)]
         load_page(0)
         weights = {}
         load_weights((0, 1), 0, QUARTER, 0)
         load_page(1)
         load_weights((2,), 0, QUARTER, 2048)
         load_page(2)
-        load_weights((0,), QUARTER, QUARTER, 3072)
-        load_weights((1, 2), QUARTER, QUARTER, 4096)
+        load_weights((0, 1, 2), QUARTER, QUARTER, 3072)
         load_weights((0, 1), N, QUARTER, 6144)
         tab2 = load_words(tab2_words[0], kept([P, T3], I32, "tab2"))
         for q in QUADRANTS:
             nc.sync.dma_start(
                 tab2_plane[32 * q : 32 * q + 4, :].bitcast(I32), tab2_scales[0, 4 * q : 4 * q + 4, :].bitcast(I32)
             )
-        list2 = load_list(offs2, "list2")
         load_weights((0, 1), N + QUARTER, QUARTER, 10240)
         load_weights((2,), N, N, 8192)
         load_page(3)
@@ -172,7 +169,7 @@ def tile_list_track_phase_board_kernel(
         def one_pass(bank, j, a, weight, fp4=False):
             h, jj = divmod(j, TILES_PER_HALF)
             cols = slice(P * j, P * (j + 1))
-            v_scale = v_plane1[:, cols] if fp4 and a == 1 else v_plane[4 * a : P, cols]
+            v_scale = (v_plane, v_plane1)[a][:, cols]
             nc.tensor.matmul_mx(
                 out=banks[bank][:], lhsT=v_codes[a][h][:, P * jj : P * (jj + 1)].bitcast(FP8X4), lhsT_scale=v_scale,
                 rhs=weight[a][0], rhs_scale=weight[a][1], start=(a == 0), stop=(a == PASSES - 1),
@@ -220,10 +217,10 @@ def tile_list_track_phase_board_kernel(
         term_a = [None] * TILES
         term_b = [None] * TILES
 
-        def turn(bank, t, first, count, column=0):
-            for k in reversed(range(count // P)):
+        def turn(bank, t, first, count, column=0, early=False):
+            for k in range(count // P) if early else reversed(range(count // P)):
                 j = first // P + k
-                for n, term in enumerate((term_a, term_b)):
+                for n, term in enumerate((term_b, term_a) if early else (term_a, term_b)):
                     nc.tensor.matmul(
                         banks[bank][:, column + P * k : column + P * (k + 1)], term[j][:, P * t : P * (t + 1)], ident[:],
                         start=(n == 0), stop=(n == 1), is_transpose=True,
@@ -259,13 +256,9 @@ def tile_list_track_phase_board_kernel(
         factor_a = [None] * TILES
         factor_b = [None] * TILES
 
-        def before(j, bank):
-            group(bank, j, w3_q)
-            factor_b[j] = take_out(bank, f"factor_b{j}", place_of(j), -1.0)
-
         def now(j, bank):
-            group(bank, j, w2_q, True)
-            factor_a[j] = take_out(bank, f"factor_a{j}", place_of(TILES + j), 1.0)
+            group(bank, j, w3_q)
+            factor_a[j] = take_out(bank, f"factor_a{j}", place_of(TILES + j), -1.0)
 
         def set_aside(bank, name, slot):
             return take_out(bank, name, TAB + 2048 * slot, 1.0)
@@ -275,55 +268,52 @@ def tile_list_track_phase_board_kernel(
             nc.gpsimd.tensor_tensor(result[:], other[:], factor[:], ALU.mult)
             return result
 
-        for h in range(HALVES):
-            pick_tracks(0, h, 0, N)
-        for first in (0, QUARTER):
-            pick_tracks(1, 0, first, QUARTER)
-        pick_tracks(1, 1, 0, N)
-
-        def take_b(j, bank):
-            factor_b[j] = take_out(bank, f"factor_b{j}", place_of(j), -1.0)
+        for a in range(PASSES):
+            for first in (0, QUARTER):
+                pick_tracks(a, 0, first, QUARTER)
+            pick_tracks(a, 1, 0, N)
 
         for a in range(PASSES):
             for j in range(TILES):
-                one_pass(j, j, a, w3_q)
+                one_pass(j, j, a, w2_q, True)
         for j in range(TILES):
-            take_b(j, j)
-        w4_q = [quantize(weave_weight(w4_raw[a], a, f"w4_woven{a}", nc.vector.tensor_copy), f"w4_{a}") for a in range(PASSES)]
+            factor_b[j] = take_out(j, f"factor_b{j}", place_of(j), 1.0)
+        early_q = [quantize(weave_weight(w1_raw[a], a, f"w1_woven{a}", nc.vector.tensor_copy), f"w1_{a}") for a in range(PASSES)]
         for j in range(TILES):
-            one_pass(j, j, 0, w4_q)
-        for j in (0, 5, 6, 1, 2, 3, 4, 7):
-            one_pass(j, j, 1, w4_q)
+            one_pass(j, j, 0, early_q)
+        for j in (0, 4, 5, 1, 6, 2, 3, 7):
+            one_pass(j, j, 1, early_q)
 
         def term_at(name, offset):
             return placed([P, H], F32, name, offset)
 
         first_raw, last_raw = RAW + 2 * 8192, RAW + 3 * 8192
-        w1_woven = [weave_weight(w1_raw[0], 2, "w1_woven0", shared_copy(88))]
+        woven = weave_weight(w4_raw[0], 2, "w4_woven0", shared_copy(88))
         term_b[0] = times(0, factor_b[0], term_at("term_b0", first_raw))
-        w1_q = [quantize(w1_woven[0], "w1_0")]
-        aside = {j: take_out(j, f"aside_b{j}", first_raw + 2048 * (j - 3), 1.0) for j in (5, 6)}
-        w1_woven.append(weave_weight(w1_raw[1], 3, "w1_woven1", shared_copy(84)))
-        term_b[1] = times(1, factor_b[1], term_at("term_b1", last_raw + 2 * 2048))
-        w1_q.append(quantize(w1_woven[1], "w1_1"))
-        for j in (2, 3):
-            term_b[j] = times(j, factor_b[j], term_at(f"term_b{j}", last_raw + 2048 * (j - 2)))
+        late_q = [quantize(woven, "w4_0")]
+        aside = {4: take_out(4, "aside_b4", first_raw + 2048, 1.0)}
+        woven = weave_weight(w4_raw[1], 3, "w4_woven1", shared_copy(84))
+        term_b[1] = times(1, factor_b[1], term_at("term_b1", last_raw))
+        late_q.append(quantize(woven, "w4_1"))
         for j in (5, 6):
-            term_b[j] = side_product(aside[j], factor_b[j], term_at(f"term_b{j}", WOVEN + 3 * 4096 + 2048 * (j - 5)))
-        for j, bank in enumerate((0, 5)):
-            one_pass(bank, j, 0, w1_q)
-        now(0, 6)
-        now(1, 1)
-        for j, bank in enumerate((0, 5)):
-            one_pass(bank, j, 1, w1_q)
+            aside[j] = take_out(j, f"aside_b{j}", last_raw + 2048 * (j - 4), 1.0)
+        term_b[2] = times(2, factor_b[2], term_at("term_b2", last_raw + 3 * 2048))
+        term_b[3] = times(3, factor_b[3], term_at("term_b3", place_of(1)))
+        for j in (4, 5):
+            term_b[j] = side_product(aside[j], factor_b[j], term_at(f"term_b{j}", WOVEN + 3 * 4096 + 2048 * (j - 4)))
+        term_b[6] = side_product(aside[6], factor_b[6], term_at("term_b6", first_raw + 2048))
+        one_pass(0, 0, 0, late_q)
+        now(0, 4)
+        now(1, 5)
+        one_pass(1, 1, 0, late_q)
+        for j in range(2):
+            one_pass(j, j, 1, late_q)
         term_b[7] = side_product(take_out(7, "aside_b7", place_of(3), 1.0), factor_b[7])
-        term_a[0] = times(0, factor_a[0], factor_a[0])
-        term_a[1] = times(5, factor_a[1], term_at("term_a1", place_of(2)))
-        now(2, 2)
-        group(6, 2, w1_q)
-        now(3, 3)
-        term_b[4] = times(4, factor_b[4], term_at("term_b4", place_of(TILES + 1)))
-        term_a[2] = times(6, factor_a[2], factor_a[2])
+        now(2, 6)
+        group(2, 2, late_q)
+        now(3, 4)
+        for j in range(3):
+            term_a[j] = times(j, factor_a[j], factor_a[j])
         value = {}
         turned = {}
 
@@ -331,7 +321,7 @@ def tile_list_track_phase_board_kernel(
             value[t, k] = placed([P, QUARTER], F32, f"value{t}_{k}", CROSS + 1024 * (10 + 3 * k + t))
             return value[t, k]
 
-        for t, bank in ((0, 1), (1, 0)):
+        for t, bank in ((0, 5), (1, 7)):
             nc.vector.tensor_tensor(value_tile(t, 0)[:], turn(bank, t, 0, QUARTER), weight_of(t, 0, QUARTER), ALU.mult)
 
         def side_turn(t, k, bank, slot):
@@ -342,39 +332,39 @@ def tile_list_track_phase_board_kernel(
 
         def side_factors(j, first_bank, second_bank):
             now(j, first_bank)
-            group(second_bank, j, w1_q)
+            group(second_bank, j, late_q)
             aside[j] = set_aside(second_bank, f"aside_a{j}", j)
 
         def side_term(j):
             term_a[j] = side_product(aside[j], factor_a[j], term_at(f"term_a{j}", CROSS + 2048 * (j - 4)))
 
         put(0, 0, QUARTER, value[0, 0][:])
-        group(5, 3, w1_q)
-        term_a[3] = times(5, factor_a[3], term_at("term_a3", WGS))
-        side_turn(2, 0, 7, 0)
+        group(3, 3, late_q)
+        term_a[3] = times(3, factor_a[3], term_at("term_a3", WGS))
+        side_turn(2, 0, 0, 0)
         side_weigh(2, 0)
-        side_factors(4, 2, 4)
+        side_factors(4, 1, 6)
         side_term(4)
-        side_factors(5, 0, 1)
-        for t, bank, slot in ((0, 3, 1), (1, 6, 2), (2, 7, 4)):
+        side_factors(5, 2, 4)
+        for t, bank, slot in ((0, 5, 1), (1, 7, 2), (2, 0, 13)):
             side_turn(t, 1, bank, slot)
         side_weigh(0, 1)
         side_weigh(1, 1)
         side_term(5)
         side_weigh(2, 1)
-        side_factors(6, 5, 2)
+        side_factors(6, 3, 1)
         side_term(6)
-        side_factors(7, 4, 0)
-        for t, bank, slot in ((0, 1, 3), (1, 3, 4)):
+        side_factors(7, 6, 2)
+        for t, bank, slot in ((0, 4, 3), (1, 5, 13)):
             side_turn(t, 2, bank, slot)
             side_weigh(t, 2)
         side_term(7)
         whole_three = placed([P, S], F32, "value3", CROSS + 1024 * 22)
-        nc.scalar.copy(whole_three[:, :N], turn(1, 3, 0, N))
-        for t, bank in ((0, 7), (1, 5)):
+        nc.scalar.copy(whole_three[:, :N], turn(4, 3, 0, N))
+        for t, bank in ((0, 7), (1, 0)):
             value[t, 3] = copied(turn(bank, t, N + QUARTER, QUARTER), f"value{t}_3", CROSS + 1024 * (18 + t))
-        rest_two = copied(turn(2, 2, N, N), "value2_2", CROSS + 1024 * 20)
-        nc.scalar.copy(whole_three[:, N:], turn(4, 3, N, N))
+        rest_two = copied(turn(3, 2, N, N), "value2_2", CROSS + 1024 * 20)
+        nc.scalar.copy(whole_three[:, N:], turn(1, 3, N, N, early=True))
         for k in range(3):
             for t in range(1 if k == 0 else 0, 3 if k < 2 else 2):
                 put(t, QUARTER * k, QUARTER, value[t, k][:])
@@ -385,7 +375,7 @@ def tile_list_track_phase_board_kernel(
             return codes, plane
 
         modes_first = pick_modes(
-            placed([P, P], U32, "modes_first_codes", CROSS + 2048 * 4), placed([P, P], U8, "modes_first_plane", CROSS + 2048 * 4 + 512), 0, P
+            placed([P, P], U32, "modes_first_codes", CROSS + 2048 * 13), placed([P, P], U8, "modes_first_plane", CROSS + 2048 * 13 + 512), 0, P
         )
         for t in range(2):
             scatter(t, N + QUARTER, QUARTER, value[t, 3][:])
@@ -410,10 +400,10 @@ def tile_list_track_phase_board_kernel(
                 pair[:].rearrange("p i c -> p c i"),
             )
 
-        planes = placed([P, 2, 2, N], BF16, "low_planes", place_of(9) - 3072)
-        pairs = placed([P, 2, 2, N, 2], BF16, "low_pairs", place_of(9) + 1024)
+        planes = placed([P, 2, 2, N], BF16, "low_planes", CROSS + 7 * 1024)
+        pairs = placed([P, 2, 2, N, 2], BF16, "low_pairs", CROSS - 1024)
         low = [planes[:, 0], planes[:, 1], pairs[:, 0], pairs[:, 1]]
-        high = [placed([P, 2, N], BF16, f"high{c}", place_of(c)) for c in range(2)]
+        high = [placed([P, 2, N], BF16, f"high{c}", place_of(4 + c)) for c in range(2)]
         for t in range(2):
             for c in range(2):
                 round_plane(nc.scalar.copy, low[c], t, t, c)
@@ -435,7 +425,7 @@ def tile_list_track_phase_board_kernel(
             weave_words(c)
         for c in range(2):
             weave_pair(nc.vector.tensor_copy, high[c], 1, c)
-        board_q = [quantize(board[c], f"board{c}", CROSS if c == 2 else None) for c in range(CHUNKS)]
+        board_q = [quantize(board[c], f"board{c}", COUNT if c == 2 else None) for c in range(CHUNKS)]
         last_board = WOVEN + 4096 * (CHUNKS - 1)
         modes_second = pick_modes(
             placed([P, P], U32, "modes_second_codes", last_board),
@@ -463,7 +453,7 @@ def tile_list_track_phase_board_kernel(
         rows = range(S2 // P)
         last = rows[-1]
         picked = [[placed([P, N], F32, f"picked{n}_{h}", TAB + 4096 * n + 2048 * h) for h in range(2)] for n in rows]
-        turns = [placed([P, PICK], I32, f"turns{n}", CROSS) for n in range(last)]
+        turns = [placed([P, PICK], I32, f"turns{n}", COUNT) for n in range(last)]
         turns.append(placed([P, PICK], I32, f"turns{last}", TAB + 4096 * (last - 1) - 2048))
         parts = [placed([P, PICK], F32, f"part{n}", WGS + 4096 * n) for n in rows]
 

@@ -70,11 +70,9 @@ def tile_list_track_phase_board_kernel(
             return tile
 
         def load_weight_scales(queue, tile, source):
-            for q in QUADRANTS:
-                queue.dma_start(
-                    tile[32 * q : 32 * q + 4, :, :].bitcast(I32),
-                    source[:, 4 * q : 4 * q + 4, :].rearrange("a r c -> r a c").bitcast(I32),
-                )
+            rows = source.rearrange("a (q r) c -> r q a c", r=4)
+            for r in range(4):
+                queue.dma_start(tile[r:P:32, :, :].bitcast(I32), rows[r].bitcast(I32))
 
         def entries(tile, first, count):
             return tile[:, first // PER_COL : (first + count) // PER_COL]
@@ -137,8 +135,8 @@ def tile_list_track_phase_board_kernel(
             )
 
         nc.vector.tensor_copy(v_plane[:], tab_plane[:].indirect(list1[:]))
-        for q in QUADRANTS:
-            nc.sync.dma_start(v_plane1[32 * q : 32 * q + 4, :].bitcast(I32), v_plane[32 * q + 16 : 32 * q + 20, :].bitcast(I32))
+        for r in range(4):
+            nc.sync.dma_start(v_plane1[r:P:32, :].bitcast(I32), v_plane[16 + r : P : 32, :].bitcast(I32))
         w1_raw = [load_raw(w1, a, f"w1_raw{a}", a) for a in range(PASSES)]
         w4_raw = [load_raw(w4, 0, "w4_raw0", 2)]
         load_weight_scales(nc.sync, w3_plane, w3_scales)
@@ -308,12 +306,13 @@ def tile_list_track_phase_board_kernel(
         one_pass(1, 1, 0, late_q)
         for j in range(2):
             one_pass(j, j, 1, late_q)
-        term_b[7] = side_product(take_out(7, "aside_b7", place_of(3), 1.0), factor_b[7])
         now(2, 6)
         group(2, 2, late_q)
         now(3, 4)
-        for j in range(3):
-            term_a[j] = times(j, factor_a[j], factor_a[j])
+        term_a[0] = times(0, factor_a[0], term_at("term_a0", place_of(2)))
+        term_a[1] = times(1, factor_a[1], factor_a[1])
+        term_b[7] = times(7, factor_b[7], term_at("term_b7", place_of(TILES)))
+        term_a[2] = times(2, factor_a[2], factor_a[2])
         value = {}
         turned = {}
 
@@ -321,7 +320,7 @@ def tile_list_track_phase_board_kernel(
             value[t, k] = placed([P, QUARTER], F32, f"value{t}_{k}", CROSS + 1024 * (10 + 3 * k + t))
             return value[t, k]
 
-        for t, bank in ((0, 5), (1, 7)):
+        for t, bank in ((0, 5), (1, 0)):
             nc.vector.tensor_tensor(value_tile(t, 0)[:], turn(bank, t, 0, QUARTER), weight_of(t, 0, QUARTER), ALU.mult)
 
         def side_turn(t, k, bank, slot):
@@ -341,12 +340,12 @@ def tile_list_track_phase_board_kernel(
         put(0, 0, QUARTER, value[0, 0][:])
         group(3, 3, late_q)
         term_a[3] = times(3, factor_a[3], term_at("term_a3", WGS))
-        side_turn(2, 0, 0, 0)
+        side_turn(2, 0, 7, 0)
         side_weigh(2, 0)
         side_factors(4, 1, 6)
         side_term(4)
         side_factors(5, 2, 4)
-        for t, bank, slot in ((0, 5, 1), (1, 7, 2), (2, 0, 13)):
+        for t, bank, slot in ((0, 5, 1), (1, 0, 2), (2, 7, 3)):
             side_turn(t, 1, bank, slot)
         side_weigh(0, 1)
         side_weigh(1, 1)
@@ -355,18 +354,17 @@ def tile_list_track_phase_board_kernel(
         side_factors(6, 3, 1)
         side_term(6)
         side_factors(7, 6, 2)
-        for t, bank, slot in ((0, 4, 3), (1, 5, 13)):
-            side_turn(t, 2, bank, slot)
-            side_weigh(t, 2)
         side_term(7)
+        for t, bank in ((0, 4), (1, 5)):
+            value[t, 2] = copied(turn(bank, t, N, QUARTER), f"value{t}_2", TAB + 2048 * 6 + 1024 * (t + 1))
         whole_three = placed([P, S], F32, "value3", CROSS + 1024 * 22)
         nc.scalar.copy(whole_three[:, :N], turn(4, 3, 0, N))
-        for t, bank in ((0, 7), (1, 0)):
-            value[t, 3] = copied(turn(bank, t, N + QUARTER, QUARTER), f"value{t}_3", CROSS + 1024 * (18 + t))
+        for t, bank in ((0, 0), (1, 7)):
+            value[t, 3] = copied(turn(bank, t, N + QUARTER, QUARTER, early=(t == 0)), f"value{t}_3", CROSS + 1024 * (18 + t))
         rest_two = copied(turn(3, 2, N, N), "value2_2", CROSS + 1024 * 20)
         nc.scalar.copy(whole_three[:, N:], turn(1, 3, N, N, early=True))
-        for k in range(3):
-            for t in range(1 if k == 0 else 0, 3 if k < 2 else 2):
+        for k in range(2):
+            for t in range(1 - k, 3):
                 put(t, QUARTER * k, QUARTER, value[t, k][:])
 
         def pick_modes(codes, plane, first, count):
@@ -375,10 +373,11 @@ def tile_list_track_phase_board_kernel(
             return codes, plane
 
         modes_first = pick_modes(
-            placed([P, P], U32, "modes_first_codes", CROSS + 2048 * 13), placed([P, P], U8, "modes_first_plane", CROSS + 2048 * 13 + 512), 0, P
+            placed([P, P], U32, "modes_first_codes", TAB + 2048 * 6), placed([P, P], U8, "modes_first_plane", TAB + 2048 * 6 + 512), 0, P
         )
-        for t in range(2):
-            scatter(t, N + QUARTER, QUARTER, value[t, 3][:])
+        for k in (2, 3):
+            for t in range(2):
+                scatter(t, QUARTER * k, QUARTER, value[t, k][:])
 
         board = [placed([P, PACK * N], BF16, f"board{c}", WOVEN + 4096 * c) for c in range(CHUNKS)]
 
@@ -449,7 +448,7 @@ def tile_list_track_phase_board_kernel(
                 nc.scalar.copy(match[n][:, N * c : N * (c + 1)], bank[:])
 
         shift = kept([P, S2 // P], F32, "shift")
-        nc.gpsimd.tensor_scalar(shift[:], phase[:], 1.0 / TWO_PI, None, ALU.mult)
+        nc.vector.tensor_scalar(shift[:], phase[:], 1.0 / TWO_PI, None, ALU.mult)
         rows = range(S2 // P)
         last = rows[-1]
         picked = [[placed([P, N], F32, f"picked{n}_{h}", TAB + 4096 * n + 2048 * h) for h in range(2)] for n in rows]

import math
from contextlib import ExitStack

import concourse.mybir as mybir
from concourse.masks import make_identity

K, H, T, S, T2, PICK, S2, T3 = 1024, 512, 2048, 1024, 2048, 1024, 512, 1024
FLOPS = 2 * (4 * K * H * S + H * S2 * T2)

F32 = mybir.dt.float32
BF16 = mybir.dt.bfloat16
I32 = mybir.dt.int32
U32 = mybir.dt.uint32
U16 = mybir.dt.uint16
U8 = mybir.dt.uint8
FP8X4 = mybir.dt.float8_e4m3fn_x4
FP4X4 = mybir.dt.float4_e2m1fn_x4
ALU = mybir.AluOpType
ACT = mybir.ActivationFunctionType

P = 128
PACK = 4
N = 512
PASSES = K // (P * PACK)
HALVES = S // N
TILES_PER_HALF = N // P
CHUNKS = T2 // N
PER_COL = 16
BANKS = 8
TWO_PI = 2.0 * math.pi
TILES = S // P
QUARTER = S // 4
QUADRANTS = (0, 2, 1, 3)
RAW = 0
TAB = RAW + 4 * 8192
WOVEN = TAB + 2 * 8192
TERM = WOVEN + 4 * 4096
CROSS = TERM + 16 * 2048
WGS = CROSS + 28 * 1024
PLANE = WGS + 4 * 4096
COUNT = TERM + 12 * 2048


def tile_list_track_phase_board_kernel(
    tc, tab_words, tab_scales, offs, w1, w2_words, w2_scales, w3_words, w3_scales, w4,
    page0, wgs, offs3, tab2_words, tab2_scales, offs2, offs4, mode, out,
):
    nc = tc.nc
    with ExitStack() as ctx:
        keep = ctx.enter_context(tc.tile_pool(name="keep", bufs=1))
        arena = ctx.enter_context(tc.tile_pool(name="arena", bufs=1))
        psum = ctx.enter_context(tc.psum_pool(name="psum", bufs=1))

        def kept(shape, dtype, name):
            return keep.tile(shape, dtype, name=name, align_bytes=64)

        def placed(shape, dtype, name, offset):
            return arena.tile(shape, dtype, name=name, offset=offset, align_bytes=64)

        banks = [psum.tile([P, N], F32, name=f"bank{b}") for b in range(BANKS)]

        def load_list(source, name):
            tile = keep.tile(list(source.shape), U16, name=name)
            nc.sync.dma_start(tile[:], source)
            return tile

        def zeroed_plane(shape, name, engine):
            tile = kept(shape, U8, name)
            engine.memset(tile[:].bitcast(I32), 0)
            return tile

        def load_weight_scales(queue, tile, source):
            rows = source.rearrange("a (q r) c -> r q a c", r=4)
            for r in range(4):
                queue.dma_start(tile[r:P:32, :, :].bitcast(I32), rows[r].bitcast(I32))

        def entries(tile, first, count):
            return tile[:, first // PER_COL : (first + count) // PER_COL]

        tab_plane = placed([P, T], U8, "tab_plane", PLANE)
        nc.gpsimd.memset(tab_plane[:].bitcast(I32), 0)
        w2_plane = zeroed_plane([P, PASSES, H], "w2_plane", nc.vector)
        w3_plane = zeroed_plane([P, PASSES, H], "w3_plane", nc.vector)
        tab2_plane = zeroed_plane([P, T3], "tab2_plane", nc.vector)
        v_plane1 = zeroed_plane([P, S], "v_plane1", nc.vector)
        ident = kept([P, P], F32, "ident")
        make_identity(nc, ident[:])
        ready = kept([P, 1], F32, "ready")
        nc.scalar.activation(ready[:], ident[:, 0:1], ACT.Sin)

        def load_raw(w, a, name, place):
            raw = placed([P, PACK, H], F32, name, RAW + 8192 * place)
            nc.sync.dma_start(raw[:], w[N * a : N * (a + 1), :].rearrange("(p i) c -> p i c", i=PACK))
            return raw

        def load_words(source, tile):
            nc.sync.dma_start(tile[:], source.rearrange("p n i -> p (n i)").bitcast(I32))
            return tile

        page_rows = page0.rearrange("(p t) c -> t p c", t=PACK)
        wgs_rows = wgs.rearrange("(m t) j -> m t j", t=PACK)
        page = [kept([P, T2], F32, f"page{t}") for t in range(PACK)]

        def load_page(t):
            nc.sync.dma_start(page[t][:], page_rows[t])

        def load_weights(tiles, first, count, offset):
            tile = placed([P, len(tiles), count], F32, f"weight{tiles[0]}_{first}", WGS + offset)
            for q in QUADRANTS:
                nc.sync.dma_start(
                    tile[32 * q : 32 * (q + 1), :, :], wgs_rows[:, tiles[0] : tiles[-1] + 1, first : first + count]
                )
            for k, t in enumerate(tiles):
                for column in range(0, count, QUARTER):
                    weights[t, first + column] = (tile, k, column)

        list1 = load_list(offs, "list1")
        list3 = load_list(offs3, "list3")
        scale_rows = tab_scales.rearrange("a (q r) c -> r q a c", r=4)
        for r in range(4):
            nc.sync.dma_start(tab_plane[r:P:16, :].bitcast(I32), scale_rows[r].bitcast(I32))
        tab = [load_words(tab_words[0], placed([P, T], I32, "tab0", TAB))]
        w2_codes = kept([P, PASSES, 2 * H], U8, "w2_codes")
        nc.sync.dma_start(w2_codes[:].bitcast(I32), w2_words.rearrange("a p n -> p a n").bitcast(I32))
        load_weight_scales(nc.sync, w2_plane, w2_scales)
        tab.append(load_words(tab_words[1], placed([P, T], I32, "tab1", TAB + 8192)))
        list2 = load_list(offs2, "list2")

        v_codes = [[kept([P, N], U32, f"v_codes{a}_{h}") for h in range(HALVES)] for a in range(PASSES)]
        v_plane = kept([P, S], U8, "v_plane")

        def pick_tracks(a, h, first, count):
            nc.vector.tensor_copy(
                v_codes[a][h][:, first : first + count], tab[a][:].bitcast(U32).indirect(entries(list1, N * h + first, count))
            )

        nc.vector.tensor_copy(v_plane[:], tab_plane[:].indirect(list1[:]))
        for r in range(4):
            nc.sync.dma_start(v_plane1[r:P:32, :].bitcast(I32), v_plane[16 + r : P : 32, :].bitcast(I32))
        w1_raw = [load_raw(w1, a, f"w1_raw{a}", a) for a in range(PASSES)]
        w4_raw = [load_raw(w4, 0, "w4_raw0", 2)]
        load_weight_scales(nc.sync, w3_plane, w3_scales)
        w4_raw.append(load_raw(w4, 1, "w4_raw1", 3))
        w3_codes = [load_words(w3_words[a], kept([P, H], I32, f"w3_codes{a}")) for a in range(PASSES)]
        load_page(0)
        weights = {}
        load_weights((0, 1), 0, QUARTER, 0)
        load_page(1)
        load_weights((2,), 0, QUARTER, 2048)
        load_page(2)
        load_weights((0, 1, 2), QUARTER, QUARTER, 3072)
        load_weights((0, 1), N, QUARTER, 6144)
        tab2 = load_words(tab2_words[0], kept([P, T3], I32, "tab2"))
        for q in QUADRANTS:
            nc.sync.dma_start(
                tab2_plane[32 * q : 32 * q + 4, :].bitcast(I32), tab2_scales[0, 4 * q : 4 * q + 4, :].bitcast(I32)
            )
        load_weights((0, 1), N + QUARTER, QUARTER, 10240)
        load_weights((2,), N, N, 8192)
        load_page(3)
        load_weights((3,), 0, S, 12288)
        list4 = load_list(offs4, "list4")
        phase = kept([P, S2 // P], F32, "phase")
        with nc.allow_non_contiguous_dma(reason="one phase offset a partition"):
            nc.sync.dma_start(phase[:], mode.rearrange("(n p) -> p n", p=P))

        def one_pass(bank, j, a, weight, fp4=False):
            h, jj = divmod(j, TILES_PER_HALF)
            cols = slice(P * j, P * (j + 1))
            v_scale = (v_plane, v_plane1)[a][:, cols]
            nc.tensor.matmul_mx(
                out=banks[bank][:], lhsT=v_codes[a][h][:, P * jj : P * (jj + 1)].bitcast(FP8X4), lhsT_scale=v_scale,
                rhs=weight[a][0], rhs_scale=weight[a][1], start=(a == 0), stop=(a == PASSES - 1),
            )

        def take_out(bank, name, offset, sign):
            tile = placed([P, H], F32, name, offset)
            nc.scalar.activation(
                tile[:].rearrange("p (t g e) -> p g t e", t=PACK, e=PACK),
                banks[bank][:].rearrange("p (g e t) -> p g t e", t=PACK, e=PACK), ACT.Copy, scale=sign,
            )
            return tile

        def times(bank, tile, result):
            nc.vector.tensor_tensor(
                result[:].rearrange("p (t m) -> p t m", t=PACK), banks[bank][:].rearrange("p (m t) -> p t m", t=PACK),
                tile[:].rearrange("p (t m) -> p t m", t=PACK), ALU.mult,
            )
            return result

        def shared_copy(cut):
            def both(dst, src):
                nc.vector.tensor_copy(dst[:, :cut], src[:, :cut])
                nc.scalar.copy(dst[:, cut:], src[:, cut:])

            return both

        def weave_weight(raw, place, name, engine_copy):
            tile = placed([P, PACK * N], BF16, name, WOVEN + 4096 * place)
            engine_copy(
                tile[:].rearrange("p (g e i) -> p g i e", e=PACK, i=PACK),
                raw[:].rearrange("p i (g e) -> p g i e", e=PACK),
            )
            return tile

        def quantize(tile, name, offset=None):
            codes = kept([P, N], U32, f"{name}_codes") if offset is None else placed([P, N], U32, f"{name}_codes", offset)
            plane = kept([P, N], U8, f"{name}_plane")
            nc.vector.quantize_mx(out=codes[:].bitcast(FP8X4), scales=plane[:], in_=tile[:])
            return codes[:].bitcast(FP8X4), plane[:]

        w2_q = [(w2_codes[:, a, :].bitcast(FP4X4), w2_plane[:, a, :]) for a in range(PASSES)]
        w3_q = [(w3_codes[a][:].bitcast(FP8X4), w3_plane[:, a, :]) for a in range(PASSES)]

        term_a = [None] * TILES
        term_b = [None] * TILES

        def turn(bank, t, first, count, column=0, early=False):
            for k in range(count // P) if early else reversed(range(count // P)):
                j = first // P + k
                for n, term in enumerate((term_b, term_a) if early else (term_a, term_b)):
                    nc.tensor.matmul(
                        banks[bank][:, column + P * k : column + P * (k + 1)], term[j][:, P * t : P * (t + 1)], ident[:],
                        start=(n == 0), stop=(n == 1), is_transpose=True,
                    )
            return banks[bank][:, column : column + count]

        def weight_of(t, first, count):
            tile, k, column = weights[t, first]
            return tile[:, k, column : column + count]

        def window(t, first, count):
            return page[t][:].indirect(entries(list3, first, count))

        def scatter(t, first, count, values):
            nc.vector.tensor_tensor(window(t, first, count), values, weight_of(t, first, count), ALU.mult)

        def put(t, first, count, values):
            nc.vector.tensor_copy(window(t, first, count), values)

        def place_of(number):
            return TERM + 2048 * number

        def group(bank, j, weight, fp4=False):
            for a in range(PASSES):
                one_pass(bank, j, a, weight, fp4)

        def copied(source, name, offset):
            tile = placed([P, source.shape[1]], F32, name, offset)
            nc.scalar.copy(tile[:], source)
            return tile


        factor_a = [None] * TILES
        factor_b = [None] * TILES

        def now(j, bank):
            group(bank, j, w3_q)
            factor_a[j] = take_out(bank, f"factor_a{j}", place_of(TILES + j), -1.0)

        def set_aside(bank, name, slot):
            return take_out(bank, name, TAB + 2048 * slot, 1.0)

        def side_product(other, factor, result=None):
            result = factor if result is None else result
            nc.gpsimd.tensor_tensor(result[:], other[:], factor[:], ALU.mult)
            return result

        for a in range(PASSES):
            for first in (0, QUARTER):
                pick_tracks(a, 0, first, QUARTER)
            pick_tracks(a, 1, 0, N)

        for a in range(PASSES):
            for j in range(TILES):
                one_pass(j, j, a, w2_q, True)
        for j in range(TILES):
            factor_b[j] = take_out(j, f"factor_b{j}", place_of(j), 1.0)
        early_q = [quantize(weave_weight(w1_raw[a], a, f"w1_woven{a}", nc.vector.tensor_copy), f"w1_{a}") for a in range(PASSES)]
        for j in range(TILES):
            one_pass(j, j, 0, early_q)
        for j in (0, 4, 5, 1, 6, 2, 3, 7):
            one_pass(j, j, 1, early_q)

        def term_at(name, offset):
            return placed([P, H], F32, name, offset)

        first_raw, last_raw = RAW + 2 * 8192, RAW + 3 * 8192
        woven = weave_weight(w4_raw[0], 2, "w4_woven0", shared_copy(88))
        term_b[0] = times(0, factor_b[0], term_at("term_b0", first_raw))
        late_q = [quantize(woven, "w4_0")]
        aside = {4: take_out(4, "aside_b4", first_raw + 2048, 1.0)}
        woven = weave_weight(w4_raw[1], 3, "w4_woven1", shared_copy(84))
        term_b[1] = times(1, factor_b[1], term_at("term_b1", last_raw))
        late_q.append(quantize(woven, "w4_1"))
        for j in (5, 6):
            aside[j] = take_out(j, f"aside_b{j}", last_raw + 2048 * (j - 4), 1.0)
        term_b[2] = times(2, factor_b[2], term_at("term_b2", last_raw + 3 * 2048))
        term_b[3] = times(3, factor_b[3], term_at("term_b3", place_of(1)))
        for j in (4, 5):
            term_b[j] = side_product(aside[j], factor_b[j], term_at(f"term_b{j}", WOVEN + 3 * 4096 + 2048 * (j - 4)))
        term_b[6] = side_product(aside[6], factor_b[6], term_at("term_b6", first_raw + 2048))
        one_pass(0, 0, 0, late_q)
        now(0, 4)
        now(1, 5)
        one_pass(1, 1, 0, late_q)
        for j in range(2):
            one_pass(j, j, 1, late_q)
        now(2, 6)
        group(2, 2, late_q)
        now(3, 4)
        term_a[0] = times(0, factor_a[0], term_at("term_a0", place_of(2)))
        term_a[1] = times(1, factor_a[1], factor_a[1])
        term_b[7] = times(7, factor_b[7], term_at("term_b7", place_of(TILES)))
        term_a[2] = times(2, factor_a[2], factor_a[2])
        value = {}
        turned = {}

        def value_tile(t, k):
            value[t, k] = placed([P, QUARTER], F32, f"value{t}_{k}", CROSS + 1024 * (10 + 3 * k + t))
            return value[t, k]

        for t, bank in ((0, 5), (1, 0)):
            nc.vector.tensor_tensor(value_tile(t, 0)[:], turn(bank, t, 0, QUARTER), weight_of(t, 0, QUARTER), ALU.mult)

        def side_turn(t, k, bank, slot):
            turned[t, k] = copied(turn(bank, t, QUARTER * k, QUARTER), f"turned{t}_{k}", CROSS + 2048 * slot)

        def side_weigh(t, k):
            nc.gpsimd.tensor_tensor(value_tile(t, k)[:], turned[t, k][:], weight_of(t, QUARTER * k, QUARTER), ALU.mult)

        def side_factors(j, first_bank, second_bank):
            now(j, first_bank)
            group(second_bank, j, late_q)
            aside[j] = set_aside(second_bank, f"aside_a{j}", j)

        def side_term(j):
            term_a[j] = side_product(aside[j], factor_a[j], term_at(f"term_a{j}", CROSS + 2048 * (j - 4)))

        put(0, 0, QUARTER, value[0, 0][:])
        group(3, 3, late_q)
        term_a[3] = times(3, factor_a[3], term_at("term_a3", WGS))
        side_turn(2, 0, 7, 0)
        side_weigh(2, 0)
        side_factors(4, 1, 6)
        side_term(4)
        side_factors(5, 2, 4)
        for t, bank, slot in ((0, 5, 1), (1, 0, 2), (2, 7, 3)):
            side_turn(t, 1, bank, slot)
        side_weigh(0, 1)
        side_weigh(1, 1)
        side_term(5)
        side_weigh(2, 1)
        side_factors(6, 3, 1)
        side_term(6)
        side_factors(7, 6, 2)
        side_term(7)
        for t, bank in ((0, 4), (1, 5)):
            value[t, 2] = copied(turn(bank, t, N, QUARTER), f"value{t}_2", TAB + 2048 * 6 + 1024 * (t + 1))
        whole_three = placed([P, S], F32, "value3", CROSS + 1024 * 22)
        nc.scalar.copy(whole_three[:, :N], turn(4, 3, 0, N))
        for t, bank in ((0, 0), (1, 7)):
            value[t, 3] = copied(turn(bank, t, N + QUARTER, QUARTER, early=(t == 0)), f"value{t}_3", CROSS + 1024 * (18 + t))
        rest_two = copied(turn(3, 2, N, N), "value2_2", CROSS + 1024 * 20)
        nc.scalar.copy(whole_three[:, N:], turn(1, 3, N, N, early=True))
        for k in range(2):
            for t in range(1 - k, 3):
                put(t, QUARTER * k, QUARTER, value[t, k][:])

        def pick_modes(codes, plane, first, count):
            nc.vector.tensor_copy(codes[:], tab2[:].bitcast(U32).indirect(entries(list2, first, count)))
            nc.vector.tensor_copy(plane[:], tab2_plane[:].indirect(entries(list2, first, count)))
            return codes, plane

        modes_first = pick_modes(
            placed([P, P], U32, "modes_first_codes", TAB + 2048 * 6), placed([P, P], U8, "modes_first_plane", TAB + 2048 * 6 + 512), 0, P
        )
        for k in (2, 3):
            for t in range(2):
                scatter(t, QUARTER * k, QUARTER, value[t, k][:])

        board = [placed([P, PACK * N], BF16, f"board{c}", WOVEN + 4096 * c) for c in range(CHUNKS)]

        def round_into_pair(t, c):
            nc.scalar.copy(low[c][:, t // 2, :, t % 2], page[t][:, N * c : N * (c + 1)])

        def weave_words(c):
            nc.scalar.copy(
                board[c][:].bitcast(F32).rearrange("p (c u) -> p c u", u=2),
                low[c][:].rearrange("p u c i -> p u (c i)").bitcast(F32).rearrange("p u c -> p c u"),
            )

        def round_plane(engine_copy, planes, row, t, c):
            engine_copy(planes[:, row, :], page[t][:, N * c : N * (c + 1)])

        def weave_pair(engine_copy, pair, u, c):
            engine_copy(
                board[c][:].rearrange("p (c i) -> p c i", i=PACK)[:, :, 2 * u : 2 * u + 2],
                pair[:].rearrange("p i c -> p c i"),
            )

        planes = placed([P, 2, 2, N], BF16, "low_planes", CROSS + 7 * 1024)
        pairs = placed([P, 2, 2, N, 2], BF16, "low_pairs", CROSS - 1024)
        low = [planes[:, 0], planes[:, 1], pairs[:, 0], pairs[:, 1]]
        high = [placed([P, 2, N], BF16, f"high{c}", place_of(4 + c)) for c in range(2)]
        for t in range(2):
            for c in range(2):
                round_plane(nc.scalar.copy, low[c], t, t, c)
            for c in range(2, CHUNKS):
                round_into_pair(t, c)
        for c in range(2):
            weave_pair(nc.scalar.copy, low[c], 0, c)
        scatter(2, N, N, rest_two[:])
        for c in range(2):
            round_plane(nc.scalar.copy, high[c], 0, 2, c)
        for c in range(2, CHUNKS):
            round_into_pair(2, c)
        scatter(3, 0, S, whole_three[:])
        for c in range(2):
            round_plane(nc.vector.tensor_copy, high[c], 1, 3, c)
        for c in range(2, CHUNKS):
            round_into_pair(3, c)
        for c in range(2, CHUNKS):
            weave_words(c)
        for c in range(2):
            weave_pair(nc.vector.tensor_copy, high[c], 1, c)
        board_q = [quantize(board[c], f"board{c}", COUNT if c == 2 else None) for c in range(CHUNKS)]
        last_board = WOVEN + 4096 * (CHUNKS - 1)
        modes_second = pick_modes(
            placed([P, P], U32, "modes_second_codes", last_board),
            placed([P, P], U8, "modes_second_plane", last_board + 512), P, P,
        )
        modes_rest = pick_modes(
            placed([P, 2 * P], U32, "modes_rest_codes", last_board + 1024),
            placed([P, 2 * P], U8, "modes_rest_plane", last_board + 2048), 2 * P, 2 * P,
        )
        match = []
        for n in range(S2 // P):
            codes, plane = (modes_first, modes_second, modes_rest, modes_rest)[n]
            cols = slice(P * max(n - 2, 0), P * max(n - 1, 1))
            match.append(placed([P, T2], F32, f"match{n}", RAW + 8192 * n))
            for c in range(CHUNKS):
                bank = banks[(CHUNKS * n + c) % BANKS]
                nc.tensor.matmul_mx(
                    out=bank[:], lhsT=codes[:, cols].bitcast(FP8X4), lhsT_scale=plane[:, cols],
                    rhs=board_q[c][0], rhs_scale=board_q[c][1], start=True, stop=True,
                )
                nc.scalar.copy(match[n][:, N * c : N * (c + 1)], bank[:])

        shift = kept([P, S2 // P], F32, "shift")
        nc.vector.tensor_scalar(shift[:], phase[:], 1.0 / TWO_PI, None, ALU.mult)
        rows = range(S2 // P)
        last = rows[-1]
        picked = [[placed([P, N], F32, f"picked{n}_{h}", TAB + 4096 * n + 2048 * h) for h in range(2)] for n in rows]
        turns = [placed([P, PICK], I32, f"turns{n}", COUNT) for n in range(last)]
        turns.append(placed([P, PICK], I32, f"turns{last}", TAB + 4096 * (last - 1) - 2048))
        parts = [placed([P, PICK], F32, f"part{n}", WGS + 4096 * n) for n in rows]

        def pick_row(n):
            for h in range(2):
                chosen = match[n][:].indirect(entries(list4, N * h, N))
                nc.vector.tensor_scalar(picked[n][h][:], chosen, 1.0 / TWO_PI, 0.25, ALU.mult, ALU.add)

        def finish_row(n, width):
            for first in range(0, PICK, width):
                cols = slice(first, first + width)
                values = picked[n][first // N][:, first % N : first % N + width]
                nc.vector.scalar_tensor_tensor(
                    parts[n][:, cols], values, shift[:, n : n + 1], turns[n][:, cols], ALU.add, ALU.subtract
                )
                nc.scalar.activation(parts[n][:, cols], parts[n][:, cols], ACT.Sin, scale=TWO_PI)
                nc.sync.dma_start(out[P * n : P * (n + 1), cols], parts[n][:, cols])

        pick_row(0)
        for n in range(last):
            for h in range(2):
                nc.gpsimd.tensor_scalar(
                    turns[n][:, N * h : N * (h + 1)], picked[n][h][:], 1.0, shift[:, n : n + 1], ALU.mult, ALU.add
                )
            pick_row(n + 1)
            finish_row(n, N)
        for h in range(2):
            nc.vector.tensor_scalar(
                turns[last][:, N * h : N * (h + 1)], picked[last][h][:], shift[:, last : last + 1], None, ALU.add
            )
        finish_row(last, QUARTER)
